import numpy as np
import ml_dtypes


def mxq(x, axis, fmt="e4m3"):
    dtype, down = {"e4m3": (ml_dtypes.float8_e4m3fn, 7), "e5m2": (ml_dtypes.float8_e5m2, 14)}[fmt]
    v = np.moveaxis(np.asarray(x, np.float32).astype(ml_dtypes.bfloat16).astype(np.float64), axis, -1)
    blocks = v.reshape(v.shape[:-1] + (-1, 32))
    amax = np.abs(blocks).max(-1, keepdims=True)
    byte = np.maximum(np.where(amax > 0, np.frexp(amax)[1] - 1 + 127, 0) - down, 1)
    scale = np.exp2(byte - 127.0)
    codes = (blocks / scale).astype(np.float32).astype(dtype).astype(np.float64)
    return np.moveaxis((codes * scale).reshape(v.shape), -1, axis)


WIDE = False


def mx_kscale(k):
    if not WIDE:
        return np.ones(k)
    levels = np.array([10, -10, 5, -5, 0])
    if k % 512:
        return np.exp2(np.random.permutation(np.resize(levels, k // 32))).repeat(32)
    a = np.empty((k // 512, 16))
    for p in range(k // 512):
        a[p, :8] = np.random.permutation(np.resize(levels, 8))
        for g in range(8):
            far = levels[np.abs(levels - a[p, g]) >= 10]
            a[p, g + 8] = far[np.random.randint(len(far))]
    return np.exp2(a.ravel()).repeat(32)


BF16 = ml_dtypes.bfloat16


def bf(x):
    return np.asarray(x, np.float32).astype(BF16)


def f64(x):
    return np.asarray(x).astype(np.float64)

def planes(Y):
    n, m = Y.shape
    b = f64(bf(Y)).reshape(n // 32, 32, m)
    amax = np.abs(b).max(1)
    byte = np.clip(np.where(amax > 0, np.frexp(amax)[1] - 1 + 127 - 7, 1), 1, 254)
    codes = (b * np.exp2(127.0 - byte)[:, None, :]).reshape(n, m).astype(np.float32).astype(ml_dtypes.float8_e4m3fn).view(np.uint8)
    words = codes.reshape(n // 512, 128, 4, m).transpose(0, 1, 3, 2)
    return np.ascontiguousarray(words), np.ascontiguousarray(byte.astype(np.uint8).reshape(n // 512, 16, m))


N, P = 1024, 1024


def setup_inputs():
    s, t = mx_kscale(P), mx_kscale(N)
    x = np.random.standard_normal((N, P)) / s[None, :]
    g = np.random.standard_normal((N, P)) / np.sqrt(P) * s[None, :]
    c = (1.0 + 0.2 * np.random.standard_normal(N)) * t
    d = (1.0 + 0.2 * np.random.standard_normal(N)) / t
    eta = np.random.uniform(0.5, 0.8, N)
    return {"x": bf(x), "g": bf(g), "c": bf(c), "d": bf(d), "eta": bf(eta)}


def skew_gradient(x, g):
    s = mxq(g, 1, "e4m3") @ mxq(x.T, 0, "e4m3")
    return (s - s.T) / np.sqrt(2.0)


def core(x, g, c, d, eta):
    x, g, c, d, eta = f64(x), f64(g), f64(c), f64(d), f64(eta)
    n = x.shape[0]
    a = skew_gradient(x, g)
    l = a * c[None, :]
    r = d[:, None] * a
    q = (mxq(l, 1, "e4m3") @ mxq(r, 0, "e4m3")) / np.sqrt(n)
    step = eta[None, :]
    delta = -step * a + 0.5 * step * step * q
    return delta


def reference(x, g, c, d, eta):
    R_out = core(x, g, c, d, eta)
    words, scales = planes(R_out.T)
    return R_out, words, scales

@@ -1,0 +1,360 @@
+from contextlib import ExitStack
+import math
+
+import concourse.mybir as mybir
+from concourse.masks import make_identity
+
+F32 = mybir.dt.float32
+BF16 = mybir.dt.bfloat16
+I32 = mybir.dt.int32
+U32 = mybir.dt.uint32
+U8 = mybir.dt.uint8
+FP8X4 = mybir.dt.float8_e4m3fn_x4
+ALU = mybir.AluOpType
+COPY = mybir.ActivationFunctionType.Copy
+
+N = 1024
+P = 128
+FLOPS = 2 * 2 * N * N * N
+RSQRT2 = 1.0 / math.sqrt(2.0)
+
+
+def tile_skewgradientquadraticstep_kernel(tc, x, g, c, d, eta, out_0, out_1, out_2):
+    nc = tc.nc
+    with ExitStack() as ctx:
+        keep = ctx.enter_context(tc.tile_pool(name="keep", bufs=1))
+        xts = ctx.enter_context(tc.tile_pool(name="xts", bufs=4))
+        work = ctx.enter_context(tc.tile_pool(name="work", bufs=2))
+        psum = ctx.enter_context(tc.psum_pool(name="psum", bufs=8))
+        ctx.enter_context(tc.manual_schedule())
+
+        def new_bank():
+            return psum.tile([P, 512], F32, name="bank")
+
+        src = {"x": x.rearrange("(h m t) k -> h t m k", h=2, t=4), "g": g.rearrange("(h m t) k -> h t m k", h=2, t=4)}
+        raw = {}
+        groups = [(0,), (1,), (2, 3), (4, 5), (6, 7)]
+        for op, i in [(op, i) for grp in groups for op in ("x", "g") for i in grp]:
+            if True:
+                raw[op, i] = keep.tile([P, N], BF16, name="raw_%s%d" % (op, i))
+                nc.sync.dma_start(out=raw[op, i][:], in_=src[op][i // 4, i % 4])
+
+        ident = keep.tile([P, P], F32, name="ident")
+        make_identity(nc, ident[:])
+
+        vecs = keep.tile([P, 512], BF16, name="vecs")
+        nc.vector.memset(vecs[:], 0.0)
+        for v, vec in enumerate((c, d, eta)):
+            nc.scalar.dma_start(out=vecs[2 * v : 2 * v + 2, :], in_=vec.rearrange("(h w) -> h w", h=2))
+
+        fac = {}
+
+        def make_factors():
+            words = vecs[:].bitcast(F32)
+            bank = new_bank()
+            for u in range(2):
+                nc.tensor.transpose(bank[:, 128 * u : 128 * u + 128], words[:, u : 256 : 2], ident[:])
+            fv = keep.tile([P, 6, 4], BF16, name="fv")
+            nc.scalar.copy(
+                out=fv[:].rearrange("p r e -> p (r e)").bitcast(F32).rearrange("p (r u) -> p r u", u=2),
+                in_=bank[:, 0:256].rearrange("p (u r) -> p r u", u=2)[:, 0:6, :],
+            )
+            flat = fv[:].rearrange("p r e -> p (r e)")
+            fac["rl"] = keep.tile([P, 2, 8], F32, name="fac_rl")
+            fac["e"] = keep.tile([P, 8], F32, name="fac_e")
+            for dst, row, scale in ((fac["rl"][:, 0, :], 8, RSQRT2), (fac["rl"][:, 1, :], 0, -RSQRT2), (fac["e"][:], 16, RSQRT2)):
+                nc.scalar.activation(out=dst, in_=flat[:, row : row + 8], func=COPY, scale=scale)
+            fac["h"] = keep.tile([P, 8], F32, name="fac_h")
+            nc.vector.scalar_tensor_tensor(
+                out=fac["h"][:], in0=flat[:, 16:24], scalar=1.0 / 64.0, in1=flat[:, 16:24], op0=ALU.mult, op1=ALU.mult
+            )
+
+        codes, scales, xt = {}, {}, {}
+
+        def transpose_in(op, grp, i):
+            words = raw[op, i][:].bitcast(F32)
+            bank = new_bank()
+            for gi in range(2):
+                for u in range(2):
+                    lo = 128 * (2 * gi + u)
+                    nc.tensor.transpose(bank[:, lo : lo + 128], words[:, 256 * gi + u : 256 * gi + 256 : 2], ident[:])
+            if i == grp[0]:
+                xt[op, grp] = xts.tile([P, len(grp) * 1024], BF16, name="xt_" + op, align_bytes=64)
+            pos = i - grp[0]
+            nc.scalar.copy(
+                out=xt[op, grp][:, 1024 * pos : 1024 * pos + 1024].bitcast(F32).rearrange("p (g m u) -> p g m u", g=2, u=2),
+                in_=bank[:].rearrange("p (g u m) -> p g m u", g=2, u=2),
+            )
+
+        def quantize_in(op, grp):
+            width = 256 * len(grp)
+            c = keep.tile([P, width], U32, name="codes_%s%d" % (op, grp[0]), align_bytes=64)
+            s = keep.tile([P, width], U8, name="scales_%s%d" % (op, grp[0]), align_bytes=64)
+            nc.vector.quantize_mx(out=c[:].bitcast(FP8X4), scales=s[:], in_=xt[op, grp][:])
+            for i in grp:
+                for gi in range(2):
+                    lo = 256 * (i - grp[0]) + 128 * gi
+                    codes[op, i, gi] = c[:, lo : lo + 128].bitcast(FP8X4)
+                    scales[op, i, gi] = s[:, lo : lo + 128]
+
+        def negate(grp):
+            xt["n", grp] = xts.tile([P, len(grp) * 1024], BF16, name="xt_n", align_bytes=64)
+            nc.vector.tensor_scalar(out=xt["n", grp][:], in0=xt["x", grp][:], scalar1=-1.0, scalar2=None, op0=ALU.mult)
+
+        ea = keep.tile([P, 8, N], F32, name="ea")
+        abank, bf, qcodes, qscales = {}, {}, {}, {}
+
+        def mm1(h, s):
+            bank = new_bank()
+            abank[h, s] = bank
+            for t in range(4):
+                k = 4 * h + t
+                step = 0
+                for a, b in (("g", "x"), ("n", "g")):
+                    for gi in range(2):
+                        nc.tensor.matmul_mx(
+                            out=bank[:, 128 * t : 128 * t + 128],
+                            lhsT=codes[a, k, gi],
+                            lhsT_scale=scales[a, k, gi],
+                            rhs=codes[b, s, gi],
+                            rhs_scale=scales[b, s, gi],
+                            start=(step == 0),
+                            stop=(step == 3),
+                        )
+                        step += 1
+
+        scalar_l = {(0, 1), (1, 2), (0, 5), (0, 6), (0, 7), (1, 4), (1, 5), (1, 6)}
+
+        def start_quadrant(h, hp):
+            bf[h, hp] = work.tile([P, 2, 512, 4], BF16, name="bf_rl", align_bytes=64)
+            for o in ("r", "l"):
+                qcodes[o, h, hp] = keep.tile([P, 512], U32, name="qc_%s%d%d" % (o, h, hp), align_bytes=64)
+                qscales[o, h, hp] = keep.tile([P, 512], U8, name="qs_%s%d%d" % (o, h, hp), align_bytes=64)
+
+        def rl_out(h, s):
+            col = 128 * (s % 4)
+            both = 1 if (h, s) in scalar_l else 2
+            nc.vector.tensor_tensor(
+                out=bf[h, s // 4][:, 0:both, col : col + 128, :],
+                in0=abank[h, s][:].rearrange("p (t n) -> p n t", t=4).unsqueeze(1).to_broadcast([P, both, 128, 4]),
+                in1=fac["rl"][:, 0:both, 4 * h : 4 * h + 4].unsqueeze(2).to_broadcast([P, both, 128, 4]),
+                op=ALU.mult,
+            )
+
+        def l_out(h, s):
+            col = 128 * (s % 4)
+            st = work.tile([P, 4, 128], BF16, name="stage_l", align_bytes=64)
+            for t in range(4):
+                nc.scalar.activation(
+                    out=st[:, t, :],
+                    in_=abank[h, s][:, 128 * t : 128 * t + 128],
+                    func=COPY,
+                    scale=fac["rl"][:, 1, 4 * h + t : 4 * h + t + 1],
+                )
+            nc.gpsimd.tensor_scalar(
+                out=bf[h, s // 4][:, 1, col : col + 128, :],
+                in0=st[:].rearrange("p t n -> p n t"),
+                scalar1=1.0,
+                scalar2=0.0,
+                op0=ALU.mult,
+                op1=ALU.add,
+            )
+
+        def e_out(h, s):
+            for t in range(4):
+                nc.scalar.activation(
+                    out=ea[:, 4 * h + t, 128 * s : 128 * s + 128],
+                    in_=abank[h, s][:, 128 * t : 128 * t + 128],
+                    func=COPY,
+                    scale=fac["e"][:, 4 * h + t : 4 * h + t + 1],
+                )
+
+        def quantize_pair(o, h, pair):
+            hp = pair // 2
+            col = 256 * (pair % 2)
+            nc.vector.quantize_mx(
+                out=qcodes[o, h, hp][:, col : col + 256].bitcast(FP8X4),
+                scales=qscales[o, h, hp][:, col : col + 256],
+                in_=bf[h, hp][:, 0 if o == "r" else 1, col : col + 256, :].rearrange("p n t -> p (n t)"),
+            )
+
+        def quantize_quadrant(o, h, hp):
+            nc.vector.quantize_mx(
+                out=qcodes[o, h, hp][:].bitcast(FP8X4),
+                scales=qscales[o, h, hp][:],
+                in_=bf[h, hp][:, 0 if o == "r" else 1, :, :].rearrange("p n t -> p (n t)"),
+            )
+
+        qbank, out_t, il, osb = {}, {}, {}, {}
+
+        def mm2(h, hp, t):
+            bank = new_bank()
+            qbank[h, hp, t] = bank
+            for k in range(2):
+                nc.tensor.matmul_mx(
+                    out=bank[:],
+                    lhsT=qcodes["r", k, h][:, 128 * t : 128 * t + 128].bitcast(FP8X4),
+                    lhsT_scale=qscales["r", k, h][:, 128 * t : 128 * t + 128],
+                    rhs=qcodes["l", k, hp][:].bitcast(FP8X4),
+                    rhs_scale=qscales["l", k, hp][:],
+                    start=(k == 0),
+                    stop=(k == 1),
+                )
+
+        def combine(h, hp, t):
+            if t == 0:
+                out_t[h, hp] = work.tile([P, 4, 512], F32, name="out_t", align_bytes=64)
+            nc.vector.scalar_tensor_tensor(
+                out=out_t[h, hp][:, t, :],
+                in0=qbank[h, hp, t][:],
+                scalar=fac["h"][:, 4 * h + t : 4 * h + t + 1],
+                in1=ea[:, 4 * h + t, 512 * hp : 512 * hp + 512],
+                op0=ALU.mult,
+                op1=ALU.add,
+            )
+
+        def interleave_out(h, hp, rows, engine):
+            if (h, hp) not in il:
+                il[h, hp] = work.tile([P, 2048], BF16, name="il", align_bytes=64)
+            out = il[h, hp][:].rearrange("p (m a t) -> p a m t", a=4, t=4)[:, :, rows, :]
+            in_ = out_t[h, hp][:].rearrange("p t (a m) -> p a m t", a=4)[:, :, rows, :]
+            if engine == "V":
+                nc.vector.tensor_copy(out=out, in_=in_)
+            else:
+                nc.scalar.copy(out=out, in_=in_)
+
+        def quantize_out(h, hp):
+            oc = keep.tile([P, 512], U32, name="oc_%d%d" % (h, hp), align_bytes=64)
+            osc = keep.tile([P, 512], U8, name="os_%d%d" % (h, hp), align_bytes=64)
+            nc.vector.quantize_mx(out=oc[:].bitcast(FP8X4), scales=osc[:], in_=il[h, hp][:])
+            cols = slice(512 * hp, 512 * hp + 512)
+            nc.sync.dma_start(
+                out=out_1[h, :, cols, :].rearrange("p m b -> p (m b)").bitcast(I32), in_=oc[:].bitcast(I32)
+            )
+            for quad in range(4):
+                nc.sync.dma_start(
+                    out=out_2[h, 4 * quad : 4 * quad + 4, cols].bitcast(I32),
+                    in_=osc[32 * quad : 32 * quad + 4, :].bitcast(I32),
+                )
+
+        out_rows = out_0.rearrange("(h m a) j -> h m a j", h=2, a=4)
+
+        obank = {}
+
+        def transpose_out(h, hp, a):
+            bank = new_bank()
+            obank[h, hp, a] = bank
+            for t in range(4):
+                nc.tensor.transpose(
+                    bank[:, 128 * t : 128 * t + 128], out_t[h, hp][:, t, 128 * a : 128 * a + 128], ident[:]
+                )
+
+        def copy_out(h, hp, a):
+            if a == 0:
+                osb[h, hp] = work.tile([P, 4, 512], F32, name="osb", align_bytes=64)
+            nc.scalar.copy(
+                out=osb[h, hp][:, a, :].rearrange("m (p t) -> m p t", t=4),
+                in_=obank[h, hp, a][:].rearrange("m (t p) -> m p t", t=4),
+            )
+            size = 1 if (h, hp) == (1, 1) else 2
+            if a % size == size - 1:
+                rows = slice(a + 1 - size, a + 1)
+                nc.sync.dma_start(out=out_rows[hp, :, rows, 512 * h : 512 * h + 512], in_=osb[h, hp][:, rows, :])
+
+        banks = [(h, 4 * hp + t) for hp in range(2) for h in range(2) for t in range(4)]
+
+        def drain(bi):
+            h, s = banks[bi]
+            if s % 4 == 0:
+                start_quadrant(h, s // 4)
+            if bi == 15:
+                rl_out(h, s)
+            if (h, s) in scalar_l:
+                l_out(h, s)
+            e_out(h, s)
+            if bi != 15:
+                rl_out(h, s)
+            if bi % 2 == 0 and bi >= 2:
+                quantize_both(bi - 2)
+
+        def quantize_both(bi):
+            h, s = banks[bi]
+            if s < 4:
+                if s == 2:
+                    quantize_quadrant("r", h, 0)
+                    quantize_quadrant("l", h, 0)
+                return
+            quantize_pair("r", h, s // 2)
+            quantize_pair("l", h, s // 2)
+
+        for j, grp in enumerate(groups):
+            for op in ("x", "g"):
+                for i in grp:
+                    transpose_in(op, grp, i)
+                if j == 4 and op == "x":
+                    mm1(*banks[0])
+            negate(grp)
+            quantize_in("x", grp)
+            quantize_in("n", grp)
+            quantize_in("g", grp)
+            if j == 3:
+                make_factors()
+
+        first = (0, 0)
+        mm2_at = (12, 12, 13, 14)
+        combine_at = (10, 10, 12, 13)
+        lag = 3
+        for n in range(16 + lag):
+            if 0 < n < 16:
+                mm1(*banks[n])
+            if n - lag == 15:
+                interleave_out(*first, slice(0, 128), "S")
+            if n >= lag:
+                drain(n - lag)
+            for t in range(4):
+                if mm2_at[t] == n:
+                    mm2(*first, t)
+            for t in range(4):
+                if combine_at[t] == n - lag:
+                    combine(*first, t)
+            if n == 16:
+                for a in range(4):
+                    transpose_out(*first, a)
+        copy_out(*first, 0)
+        quantize_both(14)
+        quantize_out(*first)
+        for a in range(1, 4):
+            copy_out(*first, a)
+
+        vector_rows = {(1, 0): 64, (0, 1): 96, (1, 1): 128}
+
+        def interleave_both(h, hp):
+            rows = vector_rows[h, hp]
+            interleave_out(h, hp, slice(0, rows), "V")
+            if rows < 128:
+                interleave_out(h, hp, slice(rows, 128), "S")
+
+        blocks = [(1, 0), (0, 1), (1, 1)]
+        for n, blk in enumerate(blocks):
+            prev = blocks[n - 1]
+            for t in range(4):
+                mm2(*blk, t)
+            if n > 0:
+                for a in range(4):
+                    transpose_out(*prev, a)
+            for t in range(4):
+                combine(*blk, t)
+                if n > 0:
+                    if t == 0:
+                        interleave_both(*prev)
+                    if t == 3:
+                        quantize_out(*prev)
+                    copy_out(*prev, t)
+        last = blocks[-1]
+        for a in range(4):
+            transpose_out(*last, a)
+        interleave_both(*last)
+        for a in range(3):
+            copy_out(*last, a)
+        quantize_out(*last)
+        copy_out(*last, 3)

@@ -11,7 +11,7 @@ U32 = mybir.dt.uint32
 U8 = mybir.dt.uint8
 FP8X4 = mybir.dt.float8_e4m3fn_x4
 ALU = mybir.AluOpType
-COPY = mybir.ActivationFunctionType.Copy
+ACT = mybir.ActivationFunctionType
 
 N = 1024
 P = 128
@@ -23,7 +23,6 @@ def tile_skewgradientquadraticstep_kernel(tc, x, g, c, d, eta, out_0, out_1, out
     nc = tc.nc
     with ExitStack() as ctx:
         keep = ctx.enter_context(tc.tile_pool(name="keep", bufs=1))
-        xts = ctx.enter_context(tc.tile_pool(name="xts", bufs=4))
         work = ctx.enter_context(tc.tile_pool(name="work", bufs=2))
         psum = ctx.enter_context(tc.psum_pool(name="psum", bufs=8))
         ctx.enter_context(tc.manual_schedule())
@@ -33,19 +32,23 @@ def tile_skewgradientquadraticstep_kernel(tc, x, g, c, d, eta, out_0, out_1, out
 
         src = {"x": x.rearrange("(h m t) k -> h t m k", h=2, t=4), "g": g.rearrange("(h m t) k -> h t m k", h=2, t=4)}
         raw = {}
-        groups = [(0,), (1,), (2, 3), (4, 5), (6, 7)]
-        for op, i in [(op, i) for grp in groups for op in ("x", "g") for i in grp]:
-            if True:
-                raw[op, i] = keep.tile([P, N], BF16, name="raw_%s%d" % (op, i))
-                nc.sync.dma_start(out=raw[op, i][:], in_=src[op][i // 4, i % 4])
 
-        ident = keep.tile([P, P], F32, name="ident")
-        make_identity(nc, ident[:])
+        def load(op, i):
+            raw[op, i] = keep.tile([P, N], BF16, name="raw_%s%d" % (op, i))
+            nc.sync.dma_start(out=raw[op, i][:], in_=src[op][i // 4, i % 4])
 
         vecs = keep.tile([P, 512], BF16, name="vecs")
         nc.vector.memset(vecs[:], 0.0)
+        load("x", 0)
         for v, vec in enumerate((c, d, eta)):
-            nc.scalar.dma_start(out=vecs[2 * v : 2 * v + 2, :], in_=vec.rearrange("(h w) -> h w", h=2))
+            nc.sync.dma_start(out=vecs[2 * v : 2 * v + 2, :], in_=vec.rearrange("(h w) -> h w", h=2))
+        load("g", 0)
+        for i in range(1, 8):
+            load("x", i)
+            load("g", i)
+
+        ident = keep.tile([P, P], F32, name="ident")
+        make_identity(nc, ident[:])
 
         fac = {}
 
@@ -54,20 +57,20 @@ def tile_skewgradientquadraticstep_kernel(tc, x, g, c, d, eta, out_0, out_1, out
             bank = new_bank()
             for u in range(2):
                 nc.tensor.transpose(bank[:, 128 * u : 128 * u + 128], words[:, u : 256 : 2], ident[:])
-            fv = keep.tile([P, 6, 4], BF16, name="fv")
-            nc.scalar.copy(
-                out=fv[:].rearrange("p r e -> p (r e)").bitcast(F32).rearrange("p (r u) -> p r u", u=2),
-                in_=bank[:, 0:256].rearrange("p (u r) -> p r u", u=2)[:, 0:6, :],
-            )
-            flat = fv[:].rearrange("p r e -> p (r e)")
-            fac["rl"] = keep.tile([P, 2, 8], F32, name="fac_rl")
-            fac["e"] = keep.tile([P, 8], F32, name="fac_e")
-            for dst, row, scale in ((fac["rl"][:, 0, :], 8, RSQRT2), (fac["rl"][:, 1, :], 0, -RSQRT2), (fac["e"][:], 16, RSQRT2)):
-                nc.scalar.activation(out=dst, in_=flat[:, row : row + 8], func=COPY, scale=scale)
+            rows = bank[:, 0:256].bitcast(BF16).rearrange("p (u r e) -> p r u e", u=2, e=2)
+            for sign in (1, -1):
+                fac[sign] = keep.tile([P, 6, 4], F32, name="fac_%d" % (1 - sign))
+                nc.scalar.activation(
+                    out=fac[sign][:].rearrange("p r (u e) -> p r u e", u=2), in_=rows[:, 0:6, :, :], func=ACT.Copy, scale=sign * RSQRT2
+                )
             fac["h"] = keep.tile([P, 8], F32, name="fac_h")
-            nc.vector.scalar_tensor_tensor(
-                out=fac["h"][:], in0=flat[:, 16:24], scalar=1.0 / 64.0, in1=flat[:, 16:24], op0=ALU.mult, op1=ALU.mult
+            nc.scalar.activation(
+                out=fac["h"][:].rearrange("p (h u e) -> p h u e", h=2, u=2), in_=rows[:, 4:6, :, :], func=ACT.Square, scale=0.125
             )
+
+        def factor(o, h, s):
+            sign = (-1 if h == 0 and s >= 4 else 1) * (-1 if o == "l" else 1)
+            return fac[sign][:, 2 * {"l": 0, "r": 1, "e": 2}[o] + h, :]
 
         codes, scales, xt = {}, {}, {}
 
@@ -79,30 +82,40 @@ def tile_skewgradientquadraticstep_kernel(tc, x, g, c, d, eta, out_0, out_1, out
                     lo = 128 * (2 * gi + u)
                     nc.tensor.transpose(bank[:, lo : lo + 128], words[:, 256 * gi + u : 256 * gi + 256 : 2], ident[:])
             if i == grp[0]:
-                xt[op, grp] = xts.tile([P, len(grp) * 1024], BF16, name="xt_" + op, align_bytes=64)
+                signs = 2 if op == "x" else 1
+                xt[op, grp] = work.tile([P, signs * len(grp) * 1024], BF16, name="xt_" + op, align_bytes=64, bufs=3)
             pos = i - grp[0]
             nc.scalar.copy(
                 out=xt[op, grp][:, 1024 * pos : 1024 * pos + 1024].bitcast(F32).rearrange("p (g m u) -> p g m u", g=2, u=2),
                 in_=bank[:].rearrange("p (g u m) -> p g m u", g=2, u=2),
             )
 
-        def quantize_in(op, grp):
-            width = 256 * len(grp)
-            c = keep.tile([P, width], U32, name="codes_%s%d" % (op, grp[0]), align_bytes=64)
-            s = keep.tile([P, width], U8, name="scales_%s%d" % (op, grp[0]), align_bytes=64)
-            nc.vector.quantize_mx(out=c[:].bitcast(FP8X4), scales=s[:], in_=xt[op, grp][:])
-            for i in grp:
-                for gi in range(2):
-                    lo = 256 * (i - grp[0]) + 128 * gi
-                    codes[op, i, gi] = c[:, lo : lo + 128].bitcast(FP8X4)
-                    scales[op, i, gi] = s[:, lo : lo + 128]
-
         def negate(grp):
-            xt["n", grp] = xts.tile([P, len(grp) * 1024], BF16, name="xt_n", align_bytes=64)
-            nc.vector.tensor_scalar(out=xt["n", grp][:], in0=xt["x", grp][:], scalar1=-1.0, scalar2=None, op0=ALU.mult)
+            width = 1024 * len(grp)
+            nc.vector.tensor_scalar(
+                out=xt["x", grp][:, width : 2 * width], in0=xt["x", grp][:, 0:width], scalar1=-1.0, scalar2=None, op0=ALU.mult
+            )
 
-        ea = keep.tile([P, 8, N], F32, name="ea")
-        abank, bf, qcodes, qscales = {}, {}, {}, {}
+        def quantize_in(op, grp):
+            names = ("x", "n") if op == "x" else ("g",)
+            width = 256 * len(grp)
+            cw = keep.tile([P, len(names) * width], U32, name="codes_%s%d" % (op, grp[0]), align_bytes=64)
+            sc = keep.tile([P, len(names) * width], U8, name="scales_%s%d" % (op, grp[0]), align_bytes=64)
+            nc.vector.quantize_mx(out=cw[:].bitcast(FP8X4), scales=sc[:], in_=xt[op, grp][:])
+            for sign, name in enumerate(names):
+                for i in grp:
+                    for gi in range(2):
+                        lo = width * sign + 256 * (i - grp[0]) + 128 * gi
+                        codes[name, i, gi] = cw[:, lo : lo + 128].bitcast(FP8X4)
+                        scales[name, i, gi] = sc[:, lo : lo + 128]
+
+        ea = {(h, sp): keep.tile([P, 4, 256], F32, name="ea_%d%d" % (h, sp)) for h in range(2) for sp in range(4)}
+        abank, bf, stage, qcodes, qscales = {}, {}, {}, {}, {}
+        for o in ("r", "l"):
+            for h in range(2):
+                for hp in range(2):
+                    qcodes[o, h, hp] = keep.tile([P, 512], U32, name="qc_%s%d%d" % (o, h, hp), align_bytes=64)
+                    qscales[o, h, hp] = keep.tile([P, 512], U8, name="qs_%s%d%d" % (o, h, hp), align_bytes=64)
 
         def mm1(h, s):
             bank = new_bank()
@@ -123,238 +136,306 @@ def tile_skewgradientquadraticstep_kernel(tc, x, g, c, d, eta, out_0, out_1, out
                         )
                         step += 1
 
-        scalar_l = {(0, 1), (1, 2), (0, 5), (0, 6), (0, 7), (1, 4), (1, 5), (1, 6)}
+        def bf_tile(o, h, sp):
+            if (o, h, sp) not in bf:
+                bf[o, h, sp] = work.tile([P, 256, 4], BF16, name="bf_" + o, align_bytes=64, bufs=4)
+            return bf[o, h, sp]
 
-        def start_quadrant(h, hp):
-            bf[h, hp] = work.tile([P, 2, 512, 4], BF16, name="bf_rl", align_bytes=64)
-            for o in ("r", "l"):
-                qcodes[o, h, hp] = keep.tile([P, 512], U32, name="qc_%s%d%d" % (o, h, hp), align_bytes=64)
-                qscales[o, h, hp] = keep.tile([P, 512], U8, name="qs_%s%d%d" % (o, h, hp), align_bytes=64)
-
-        def rl_out(h, s):
-            col = 128 * (s % 4)
-            both = 1 if (h, s) in scalar_l else 2
+        def vector_out(o, h, s):
+            col = 128 * (s % 2)
             nc.vector.tensor_tensor(
-                out=bf[h, s // 4][:, 0:both, col : col + 128, :],
-                in0=abank[h, s][:].rearrange("p (t n) -> p n t", t=4).unsqueeze(1).to_broadcast([P, both, 128, 4]),
-                in1=fac["rl"][:, 0:both, 4 * h : 4 * h + 4].unsqueeze(2).to_broadcast([P, both, 128, 4]),
+                out=bf_tile(o, h, s // 2)[:, col : col + 128, :],
+                in0=abank[h, s][:].rearrange("p (t n) -> p n t", t=4),
+                in1=factor(o, h, s).unsqueeze(1).to_broadcast([P, 128, 4]),
                 op=ALU.mult,
             )
 
-        def l_out(h, s):
-            col = 128 * (s % 4)
-            st = work.tile([P, 4, 128], BF16, name="stage_l", align_bytes=64)
+        def l_scale(h, s):
+            if s % 2 == 0:
+                stage[h, s // 2] = work.tile([P, 4, 256], BF16, name="stage_l", align_bytes=64, bufs=3)
+            col = 128 * (s % 2)
             for t in range(4):
                 nc.scalar.activation(
-                    out=st[:, t, :],
+                    out=stage[h, s // 2][:, t, col : col + 128],
                     in_=abank[h, s][:, 128 * t : 128 * t + 128],
-                    func=COPY,
-                    scale=fac["rl"][:, 1, 4 * h + t : 4 * h + t + 1],
+                    func=ACT.Copy,
+                    scale=factor("l", h, s)[:, t : t + 1],
                 )
-            nc.gpsimd.tensor_scalar(
-                out=bf[h, s // 4][:, 1, col : col + 128, :],
-                in0=st[:].rearrange("p t n -> p n t"),
-                scalar1=1.0,
-                scalar2=0.0,
-                op0=ALU.mult,
-                op1=ALU.add,
-            )
+
+        def l_interleave(h, sp, engine):
+            out = bf_tile("l", h, sp)[:]
+            in_ = stage[h, sp][:].rearrange("p t n -> p n t")
+            if engine == "S":
+                nc.scalar.copy(out=out, in_=in_)
+            else:
+                nc.gpsimd.tensor_scalar(out=out, in0=in_, scalar1=1.0, scalar2=0.0, op0=ALU.mult, op1=ALU.add)
 
         def e_out(h, s):
+            col = 128 * (s % 2)
             for t in range(4):
                 nc.scalar.activation(
-                    out=ea[:, 4 * h + t, 128 * s : 128 * s + 128],
+                    out=ea[h, s // 2][:, t, col : col + 128],
                     in_=abank[h, s][:, 128 * t : 128 * t + 128],
-                    func=COPY,
-                    scale=fac["e"][:, 4 * h + t : 4 * h + t + 1],
+                    func=ACT.Copy,
+                    scale=factor("e", h, s)[:, t : t + 1],
                 )
 
-        def quantize_pair(o, h, pair):
-            hp = pair // 2
-            col = 256 * (pair % 2)
-            nc.vector.quantize_mx(
-                out=qcodes[o, h, hp][:, col : col + 256].bitcast(FP8X4),
-                scales=qscales[o, h, hp][:, col : col + 256],
-                in_=bf[h, hp][:, 0 if o == "r" else 1, col : col + 256, :].rearrange("p n t -> p (n t)"),
-            )
+        plain = {}
 
-        def quantize_quadrant(o, h, hp):
-            nc.vector.quantize_mx(
-                out=qcodes[o, h, hp][:].bitcast(FP8X4),
-                scales=qscales[o, h, hp][:],
-                in_=bf[h, hp][:, 0 if o == "r" else 1, :, :].rearrange("p n t -> p (n t)"),
-            )
+        def a_out(h, s):
+            plain[s] = keep.tile([P, 512], F32, name="plain_%d" % s)
+            nc.scalar.copy(out=plain[s][:], in_=abank[h, s][:])
 
-        qbank, out_t, il, osb = {}, {}, {}, {}
-
-        def mm2(h, hp, t):
+        def mirror(s):
             bank = new_bank()
-            qbank[h, hp, t] = bank
-            for k in range(2):
-                nc.tensor.matmul_mx(
-                    out=bank[:],
-                    lhsT=qcodes["r", k, h][:, 128 * t : 128 * t + 128].bitcast(FP8X4),
-                    lhsT_scale=qscales["r", k, h][:, 128 * t : 128 * t + 128],
-                    rhs=qcodes["l", k, hp][:].bitcast(FP8X4),
-                    rhs_scale=qscales["l", k, hp][:],
-                    start=(k == 0),
-                    stop=(k == 1),
-                )
+            abank[0, s] = bank
+            for t in range(4):
+                col = 128 * (s - 4)
+                nc.tensor.transpose(bank[:, 128 * t : 128 * t + 128], plain[t][:, col : col + 128], ident[:])
 
-        def combine(h, hp, t):
-            if t == 0:
-                out_t[h, hp] = work.tile([P, 4, 512], F32, name="out_t", align_bytes=64)
-            nc.vector.scalar_tensor_tensor(
-                out=out_t[h, hp][:, t, :],
-                in0=qbank[h, hp, t][:],
-                scalar=fac["h"][:, 4 * h + t : 4 * h + t + 1],
-                in1=ea[:, 4 * h + t, 512 * hp : 512 * hp + 512],
-                op0=ALU.mult,
-                op1=ALU.add,
+        def quantize_pair(o, h, sp):
+            col = 256 * (sp % 2)
+            nc.vector.quantize_mx(
+                out=qcodes[o, h, sp // 2][:, col : col + 256].bitcast(FP8X4),
+                scales=qscales[o, h, sp // 2][:, col : col + 256],
+                in_=bf[o, h, sp][:].rearrange("p n t -> p (n t)"),
             )
 
-        def interleave_out(h, hp, rows, engine):
-            if (h, hp) not in il:
-                il[h, hp] = work.tile([P, 2048], BF16, name="il", align_bytes=64)
-            out = il[h, hp][:].rearrange("p (m a t) -> p a m t", a=4, t=4)[:, :, rows, :]
-            in_ = out_t[h, hp][:].rearrange("p t (a m) -> p a m t", a=4)[:, :, rows, :]
+        qbank, out_t, il, osb, obank = {}, {}, {}, {}, {}
+        oscale = keep.tile([P, N], U8, name="oscale", align_bytes=64)
+
+        def mm2(h, sp, tp):
+            bank = new_bank()
+            qbank[h, sp, tp] = bank
+            col = 256 * (sp % 2)
+            for u in range(2):
+                t = 2 * tp + u
+                for k in range(2):
+                    nc.tensor.matmul_mx(
+                        out=bank[:, 256 * u : 256 * u + 256],
+                        lhsT=qcodes["r", k, h][:, 128 * t : 128 * t + 128].bitcast(FP8X4),
+                        lhsT_scale=qscales["r", k, h][:, 128 * t : 128 * t + 128],
+                        rhs=qcodes["l", k, sp // 2][:, col : col + 256].bitcast(FP8X4),
+                        rhs_scale=qscales["l", k, sp // 2][:, col : col + 256],
+                        start=(k == 0),
+                        stop=(k == 1),
+                    )
+
+        def combine(h, sp, tp):
+            if tp == 0:
+                out_t[h, sp] = work.tile([P, 4, 256], F32, name="out_t", align_bytes=64, bufs=4)
+            for u in range(2):
+                t = 2 * tp + u
+                nc.vector.scalar_tensor_tensor(
+                    out=out_t[h, sp][:, t, :].rearrange("p (m a) -> p m a", a=2),
+                    in0=qbank[h, sp, tp][:, 256 * u : 256 * u + 256].rearrange("p (a m) -> p m a", a=2),
+                    scalar=fac["h"][:, 4 * h + t : 4 * h + t + 1],
+                    in1=ea[h, sp][:, t, :].rearrange("p (a m) -> p m a", a=2),
+                    op0=ALU.mult,
+                    op1=ALU.add,
+                )
+
+        def interleave_out(h, sp, engine, rows=slice(0, P)):
+            if (h, sp // 2) not in il:
+                il[h, sp // 2] = work.tile([P, 2048], BF16, name="il", align_bytes=64, bufs=3)
+            lo = 2 * (sp % 2)
+            out = il[h, sp // 2][:].rearrange("p (m a t) -> p m a t", a=4, t=4)[:, rows, lo : lo + 2, :]
+            in_ = out_t[h, sp][:].rearrange("p t (m a) -> p m a t", a=2)[:, rows, :, :]
             if engine == "V":
                 nc.vector.tensor_copy(out=out, in_=in_)
-            else:
+            elif engine == "S":
                 nc.scalar.copy(out=out, in_=in_)
+            else:
+                nc.gpsimd.tensor_scalar(out=out, in0=in_, scalar1=1.0, scalar2=0.0, op0=ALU.mult, op1=ALU.add)
 
         def quantize_out(h, hp):
             oc = keep.tile([P, 512], U32, name="oc_%d%d" % (h, hp), align_bytes=64)
-            osc = keep.tile([P, 512], U8, name="os_%d%d" % (h, hp), align_bytes=64)
-            nc.vector.quantize_mx(out=oc[:].bitcast(FP8X4), scales=osc[:], in_=il[h, hp][:])
             cols = slice(512 * hp, 512 * hp + 512)
+            nc.vector.quantize_mx(out=oc[:].bitcast(FP8X4), scales=oscale[4 * h : P, cols], in_=il[h, hp][:])
             nc.sync.dma_start(
                 out=out_1[h, :, cols, :].rearrange("p m b -> p (m b)").bitcast(I32), in_=oc[:].bitcast(I32)
             )
-            for quad in range(4):
-                nc.sync.dma_start(
-                    out=out_2[h, 4 * quad : 4 * quad + 4, cols].bitcast(I32),
-                    in_=osc[32 * quad : 32 * quad + 4, :].bitcast(I32),
-                )
+            if (h, hp) == (1, 1):
+                for quad in range(4):
+                    nc.sync.dma_start(
+                        out=out_2[:, 4 * quad : 4 * quad + 4, :].bitcast(I32),
+                        in_=oscale[32 * quad : 32 * quad + 8, :].bitcast(I32),
+                    )
 
-        out_rows = out_0.rearrange("(h m a) j -> h m a j", h=2, a=4)
+        out_rows = out_0.rearrange("(h u m a) j -> h u m a j", h=2, u=2, a=4)
 
-        obank = {}
+        def transpose_out(h, sp):
+            for a in range(2):
+                bank = new_bank()
+                obank[h, sp, a] = bank
+                for t in range(4):
+                    nc.tensor.transpose(bank[:, 128 * t : 128 * t + 128], out_t[h, sp][:, t, 128 * a : 128 * a + 128], ident[:])
 
-        def transpose_out(h, hp, a):
-            bank = new_bank()
-            obank[h, hp, a] = bank
-            for t in range(4):
-                nc.tensor.transpose(
-                    bank[:, 128 * t : 128 * t + 128], out_t[h, hp][:, t, 128 * a : 128 * a + 128], ident[:]
-                )
+        def copy_out(h, sp, engines="SS"):
+            osb[h, sp] = work.tile([P, 2, 512], F32, name="osb", align_bytes=64, bufs=4)
+            for a in range(2):
+                out = osb[h, sp][:, a, :].rearrange("m (p t) -> m p t", t=4)
+                in_ = obank[h, sp, a][:].rearrange("m (t p) -> m p t", t=4)
+                if engines[a] == "S":
+                    nc.scalar.copy(out=out, in_=in_)
+                else:
+                    nc.vector.tensor_copy(out=out, in_=in_)
+                lo = 2 * (sp % 2)
+                nc.sync.dma_start(out=out_rows[sp // 2, a, :, lo : lo + 2, 512 * h : 512 * h + 512], in_=osb[h, sp][:, a, :])
 
-        def copy_out(h, hp, a):
-            if a == 0:
-                osb[h, hp] = work.tile([P, 4, 512], F32, name="osb", align_bytes=64)
-            nc.scalar.copy(
-                out=osb[h, hp][:, a, :].rearrange("m (p t) -> m p t", t=4),
-                in_=obank[h, hp, a][:].rearrange("m (t p) -> m p t", t=4),
-            )
-            size = 1 if (h, hp) == (1, 1) else 2
-            if a % size == size - 1:
-                rows = slice(a + 1 - size, a + 1)
-                nc.sync.dma_start(out=out_rows[hp, :, rows, 512 * h : 512 * h + 512], in_=osb[h, hp][:, rows, :])
+        groups = [(i,) for i in range(8)]
 
-        banks = [(h, 4 * hp + t) for hp in range(2) for h in range(2) for t in range(4)]
+        def mm2_unit(h, sp):
+            for tp in range(2):
+                mm2(h, sp, tp)
 
-        def drain(bi):
-            h, s = banks[bi]
-            if s % 4 == 0:
-                start_quadrant(h, s // 4)
-            if bi == 15:
-                rl_out(h, s)
-            if (h, s) in scalar_l:
-                l_out(h, s)
-            e_out(h, s)
-            if bi != 15:
-                rl_out(h, s)
-            if bi % 2 == 0 and bi >= 2:
-                quantize_both(bi - 2)
+        def combine_unit(h, sp):
+            for tp in range(2):
+                combine(h, sp, tp)
 
-        def quantize_both(bi):
-            h, s = banks[bi]
-            if s < 4:
-                if s == 2:
-                    quantize_quadrant("r", h, 0)
-                    quantize_quadrant("l", h, 0)
-                return
-            quantize_pair("r", h, s // 2)
-            quantize_pair("l", h, s // 2)
-
+        make_factors()
         for j, grp in enumerate(groups):
             for op in ("x", "g"):
                 for i in grp:
                     transpose_in(op, grp, i)
-                if j == 4 and op == "x":
-                    mm1(*banks[0])
-            negate(grp)
-            quantize_in("x", grp)
-            quantize_in("n", grp)
-            quantize_in("g", grp)
-            if j == 3:
-                make_factors()
-
-        first = (0, 0)
-        mm2_at = (12, 12, 13, 14)
-        combine_at = (10, 10, 12, 13)
-        lag = 3
-        for n in range(16 + lag):
-            if 0 < n < 16:
-                mm1(*banks[n])
-            if n - lag == 15:
-                interleave_out(*first, slice(0, 128), "S")
-            if n >= lag:
-                drain(n - lag)
-            for t in range(4):
-                if mm2_at[t] == n:
-                    mm2(*first, t)
-            for t in range(4):
-                if combine_at[t] == n - lag:
-                    combine(*first, t)
-            if n == 16:
-                for a in range(4):
-                    transpose_out(*first, a)
-        copy_out(*first, 0)
-        quantize_both(14)
-        quantize_out(*first)
-        for a in range(1, 4):
-            copy_out(*first, a)
-
-        vector_rows = {(1, 0): 64, (0, 1): 96, (1, 1): 128}
-
-        def interleave_both(h, hp):
-            rows = vector_rows[h, hp]
-            interleave_out(h, hp, slice(0, rows), "V")
-            if rows < 128:
-                interleave_out(h, hp, slice(rows, 128), "S")
-
-        blocks = [(1, 0), (0, 1), (1, 1)]
-        for n, blk in enumerate(blocks):
-            prev = blocks[n - 1]
-            for t in range(4):
-                mm2(*blk, t)
-            if n > 0:
-                for a in range(4):
-                    transpose_out(*prev, a)
-            for t in range(4):
-                combine(*blk, t)
-                if n > 0:
-                    if t == 0:
-                        interleave_both(*prev)
-                    if t == 3:
-                        quantize_out(*prev)
-                    copy_out(*prev, t)
-        last = blocks[-1]
-        for a in range(4):
-            transpose_out(*last, a)
-        interleave_both(*last)
-        for a in range(3):
-            copy_out(*last, a)
-        quantize_out(*last)
-        copy_out(*last, 3)
+                if op == "x":
+                    negate(grp)
+                    if j > 0:
+                        quantize_in("g", groups[j - 1])
+                    quantize_in("x", grp)
+        mm1(0, 0)
+        quantize_in("g", groups[-1])
+        mm1(0, 1)
+        mm1(0, 2)
+        mm1(0, 3)
+        mm1(1, 0)
+        mm1(1, 1)
+        mm1(1, 2)
+        mm1(1, 3)
+        vector_out("r", 0, 0)
+        vector_out("l", 0, 0)
+        e_out(0, 0)
+        vector_out("r", 0, 1)
+        vector_out("l", 0, 1)
+        e_out(0, 1)
+        mm1(1, 4)
+        mm1(1, 5)
+        vector_out("r", 0, 2)
+        quantize_pair("r", 0, 0)
+        quantize_pair("l", 0, 0)
+        vector_out("l", 0, 2)
+        e_out(0, 2)
+        vector_out("r", 0, 3)
+        vector_out("l", 0, 3)
+        e_out(0, 3)
+        vector_out("r", 1, 0)
+        quantize_pair("r", 0, 1)
+        quantize_pair("l", 0, 1)
+        vector_out("l", 1, 0)
+        a_out(1, 1)
+        vector_out("r", 1, 1)
+        vector_out("l", 1, 1)
+        a_out(1, 2)
+        a_out(1, 0)
+        a_out(1, 3)
+        e_out(1, 0)
+        e_out(1, 1)
+        mirror(4)
+        mirror(5)
+        mirror(6)
+        mirror(7)
+        vector_out("r", 1, 2)
+        quantize_pair("r", 1, 0)
+        quantize_pair("l", 1, 0)
+        vector_out("l", 1, 2)
+        e_out(1, 2)
+        vector_out("r", 1, 3)
+        vector_out("l", 1, 3)
+        e_out(1, 3)
+        mm1(1, 6)
+        mm1(1, 7)
+        vector_out("r", 1, 4)
+        quantize_pair("r", 1, 1)
+        quantize_pair("l", 1, 1)
+        l_scale(1, 4)
+        e_out(1, 4)
+        vector_out("r", 1, 5)
+        l_scale(1, 5)
+        l_interleave(1, 2, "G")
+        e_out(1, 5)
+        vector_out("r", 0, 4)
+        vector_out("r", 0, 5)
+        quantize_pair("r", 1, 2)
+        mm2_unit(0, 0)
+        l_scale(0, 4)
+        e_out(0, 4)
+        vector_out("r", 0, 6)
+        vector_out("r", 0, 7)
+        l_scale(0, 5)
+        l_interleave(0, 2, "G")
+        e_out(0, 5)
+        mm2_unit(0, 1)
+        combine_unit(0, 0)
+        quantize_pair("r", 0, 2)
+        quantize_pair("r", 0, 3)
+        quantize_pair("l", 1, 2)
+        l_scale(0, 6)
+        e_out(0, 6)
+        vector_out("r", 1, 6)
+        vector_out("r", 1, 7)
+        l_scale(0, 7)
+        l_interleave(0, 3, "G")
+        e_out(0, 7)
+        transpose_out(0, 0)
+        vector_out("l", 1, 6)
+        quantize_pair("r", 1, 3)
+        quantize_pair("l", 0, 2)
+        mm2_unit(1, 0)
+        vector_out("l", 1, 7)
+        e_out(1, 6)
+        e_out(1, 7)
+        combine_unit(0, 1)
+        mm2_unit(1, 1)
+        transpose_out(0, 1)
+        copy_out(0, 0)
+        quantize_pair("l", 1, 3)
+        quantize_pair("l", 0, 3)
+        interleave_out(0, 0, "V")
+        interleave_out(0, 1, "S")
+        combine_unit(1, 0)
+        interleave_out(1, 0, "G", slice(0, 64))
+        interleave_out(1, 0, "S", slice(64, P))
+        copy_out(0, 1)
+        mm2_unit(0, 2)
+        transpose_out(1, 0)
+        combine_unit(1, 1)
+        quantize_out(0, 0)
+        interleave_out(1, 1, "G", slice(0, 64))
+        interleave_out(1, 1, "S", slice(64, P))
+        mm2_unit(0, 3)
+        transpose_out(1, 1)
+        copy_out(1, 0)
+        combine_unit(0, 2)
+        interleave_out(0, 2, "G", slice(0, 64))
+        interleave_out(0, 2, "S", slice(64, P))
+        copy_out(1, 1)
+        mm2_unit(1, 2)
+        transpose_out(0, 2)
+        combine_unit(0, 3)
+        quantize_out(1, 0)
+        interleave_out(0, 3, "G", slice(0, 64))
+        interleave_out(0, 3, "S", slice(64, P))
+        mm2_unit(1, 3)
+        transpose_out(0, 3)
+        copy_out(0, 2)
+        combine_unit(1, 2)
+        interleave_out(1, 2, "S")
+        copy_out(0, 3)
+        transpose_out(1, 2)
+        combine_unit(1, 3)
+        quantize_out(0, 1)
+        transpose_out(1, 3)
+        copy_out(1, 2)
+        interleave_out(1, 3, "V")
+        quantize_out(1, 1)
+        copy_out(1, 3, engines="SV")

@@ -37,15 +37,16 @@ def tile_skewgradientquadraticstep_kernel(tc, x, g, c, d, eta, out_0, out_1, out
             raw[op, i] = keep.tile([P, N], BF16, name="raw_%s%d" % (op, i))
             nc.sync.dma_start(out=raw[op, i][:], in_=src[op][i // 4, i % 4])
 
-        vecs = keep.tile([P, 512], BF16, name="vecs")
-        nc.vector.memset(vecs[:], 0.0)
-        load("x", 0)
-        for v, vec in enumerate((c, d, eta)):
-            nc.sync.dma_start(out=vecs[2 * v : 2 * v + 2, :], in_=vec.rearrange("(h w) -> h w", h=2))
         load("g", 0)
+        load("x", 0)
+        vecs = keep.tile([P, 3, 16], BF16, name="vecs")
+        for v, vec in enumerate((c, d, eta)):
+            nc.sync.dma_start(
+                out=vecs[:, v, 0:8].rearrange("p (h t) -> p h t", h=2), in_=vec.rearrange("(h p t) -> p h t", h=2, t=4)
+            )
         for i in range(1, 8):
-            load("x", i)
             load("g", i)
+            load("x", i)
 
         ident = keep.tile([P, P], F32, name="ident")
         make_identity(nc, ident[:])
@@ -53,30 +54,21 @@ def tile_skewgradientquadraticstep_kernel(tc, x, g, c, d, eta, out_0, out_1, out
         fac = {}
 
         def make_factors():
-            words = vecs[:].bitcast(F32)
-            bank = new_bank()
-            for u in range(2):
-                nc.tensor.transpose(bank[:, 128 * u : 128 * u + 128], words[:, u : 256 : 2], ident[:])
-            rows = bank[:, 0:256].bitcast(BF16).rearrange("p (u r e) -> p r u e", u=2, e=2)
-            for sign in (1, -1):
-                fac[sign] = keep.tile([P, 6, 4], F32, name="fac_%d" % (1 - sign))
-                nc.scalar.activation(
-                    out=fac[sign][:].rearrange("p r (u e) -> p r u e", u=2), in_=rows[:, 0:6, :, :], func=ACT.Copy, scale=sign * RSQRT2
-                )
+            fac["a"] = keep.tile([P, 6, 8], F32, name="fac_a")
+            for dst, first, last, scale in ((slice(1, 6, 2), 0, 3, -RSQRT2), (slice(0, 3, 2), 1, 3, RSQRT2), (slice(4, 5), 0, 1, RSQRT2)):
+                nc.scalar.activation(out=fac["a"][:, dst, :], in_=vecs[:, first:last, 0:8], func=ACT.Copy, scale=scale)
             fac["h"] = keep.tile([P, 8], F32, name="fac_h")
-            nc.scalar.activation(
-                out=fac["h"][:].rearrange("p (h u e) -> p h u e", h=2, u=2), in_=rows[:, 4:6, :, :], func=ACT.Square, scale=0.125
-            )
+            nc.scalar.activation(out=fac["h"][:], in_=vecs[:, 2, 0:8], func=ACT.Square, scale=0.125)
 
-        def factor(o, h, s):
-            sign = (-1 if h == 0 and s >= 4 else 1) * (-1 if o == "l" else 1)
-            return fac[sign][:, 2 * {"l": 0, "r": 1, "e": 2}[o] + h, :]
+        def factor(h, s):
+            return fac["a"][:, 3:6, 0:4] if h == 0 and s >= 4 else fac["a"][:, 0:3, 4 * h : 4 * h + 4]
 
-        codes, scales, xt = {}, {}, {}
+        codes, scales, xt, in_bank = {}, {}, {}, {}
 
         def transpose_in(op, grp, i):
             words = raw[op, i][:].bitcast(F32)
             bank = new_bank()
+            in_bank[op, i] = bank
             for gi in range(2):
                 for u in range(2):
                     lo = 128 * (2 * gi + u)
@@ -96,6 +88,16 @@ def tile_skewgradientquadraticstep_kernel(tc, x, g, c, d, eta, out_0, out_1, out
                 out=xt["x", grp][:, width : 2 * width], in0=xt["x", grp][:, 0:width], scalar1=-1.0, scalar2=None, op0=ALU.mult
             )
 
+        def negate_from_bank(i):
+            for gi in range(2):
+                lo = 1024 + 512 * gi
+                nc.scalar.activation(
+                    out=xt["x", (i,)][:, lo : lo + 512].rearrange("p (m u e) -> p m u e", u=2, e=2),
+                    in_=in_bank["x", i][:, 256 * gi : 256 * gi + 256].bitcast(BF16).rearrange("p (u m e) -> p m u e", u=2, e=2),
+                    func=ACT.Copy,
+                    scale=-1.0,
+                )
+
         def quantize_in(op, grp):
             names = ("x", "n") if op == "x" else ("g",)
             width = 256 * len(grp)
@@ -109,13 +111,20 @@ def tile_skewgradientquadraticstep_kernel(tc, x, g, c, d, eta, out_0, out_1, out
                         codes[name, i, gi] = cw[:, lo : lo + 128].bitcast(FP8X4)
                         scales[name, i, gi] = sc[:, lo : lo + 128]
 
-        ea = {(h, sp): keep.tile([P, 4, 256], F32, name="ea_%d%d" % (h, sp)) for h in range(2) for sp in range(4)}
+        ea = {
+            (h, sp): keep.tile([P, 4, 256], F32, name="ea_%d%d" % (h, sp))[:]
+            for h in range(2)
+            for sp in range(4)
+            if h == 0 or sp >= 2
+        }
+        ea_low = keep.tile([P, 4, 512], F32, name="ea_low")
+        for sp in range(2):
+            ea[1, sp] = ea_low[:, :, 256 * sp : 256 * sp + 256]
         abank, bf, stage, qcodes, qscales = {}, {}, {}, {}, {}
-        for o in ("r", "l"):
-            for h in range(2):
-                for hp in range(2):
-                    qcodes[o, h, hp] = keep.tile([P, 512], U32, name="qc_%s%d%d" % (o, h, hp), align_bytes=64)
-                    qscales[o, h, hp] = keep.tile([P, 512], U8, name="qs_%s%d%d" % (o, h, hp), align_bytes=64)
+        for h in range(2):
+            for hp in range(2):
+                qcodes[h, hp] = keep.tile([P, 1024], U32, name="qc_%d%d" % (h, hp), align_bytes=64)
+                qscales[h, hp] = keep.tile([P, 1024], U8, name="qs_%d%d" % (h, hp), align_bytes=64)
 
         def mm1(h, s):
             bank = new_bank()
@@ -136,17 +145,18 @@ def tile_skewgradientquadraticstep_kernel(tc, x, g, c, d, eta, out_0, out_1, out
                         )
                         step += 1
 
-        def bf_tile(o, h, sp):
-            if (o, h, sp) not in bf:
-                bf[o, h, sp] = work.tile([P, 256, 4], BF16, name="bf_" + o, align_bytes=64, bufs=4)
-            return bf[o, h, sp]
+        def bf_tile(h, hp):
+            if (h, hp) not in bf:
+                bf[h, hp] = work.tile([P, 2, 512, 4], BF16, name="bf_rl", align_bytes=64, bufs=3)
+            return bf[h, hp]
 
         def vector_out(o, h, s):
-            col = 128 * (s % 2)
+            col = 128 * (s % 4)
+            lo, n = {"r": 0, "l": 1, "rl": 0}[o], len(o)
             nc.vector.tensor_tensor(
-                out=bf_tile(o, h, s // 2)[:, col : col + 128, :],
-                in0=abank[h, s][:].rearrange("p (t n) -> p n t", t=4),
-                in1=factor(o, h, s).unsqueeze(1).to_broadcast([P, 128, 4]),
+                out=bf_tile(h, s // 4)[:, lo : lo + n, col : col + 128, :],
+                in0=abank[h, s][:].rearrange("p (t n) -> p n t", t=4).unsqueeze(1).to_broadcast([P, n, 128, 4]),
+                in1=factor(h, s)[:, lo : lo + n, :].unsqueeze(2).to_broadcast([P, n, 128, 4]),
                 op=ALU.mult,
             )
 
@@ -159,11 +169,11 @@ def tile_skewgradientquadraticstep_kernel(tc, x, g, c, d, eta, out_0, out_1, out
                     out=stage[h, s // 2][:, t, col : col + 128],
                     in_=abank[h, s][:, 128 * t : 128 * t + 128],
                     func=ACT.Copy,
-                    scale=factor("l", h, s)[:, t : t + 1],
+                    scale=factor(h, s)[:, 1, t : t + 1],
                 )
 
         def l_interleave(h, sp, engine):
-            out = bf_tile("l", h, sp)[:]
+            out = bf_tile(h, sp // 2)[:, 1, 256 * (sp % 2) : 256 * (sp % 2) + 256, :]
             in_ = stage[h, sp][:].rearrange("p t n -> p n t")
             if engine == "S":
                 nc.scalar.copy(out=out, in_=in_)
@@ -177,28 +187,36 @@ def tile_skewgradientquadraticstep_kernel(tc, x, g, c, d, eta, out_0, out_1, out
                     out=ea[h, s // 2][:, t, col : col + 128],
                     in_=abank[h, s][:, 128 * t : 128 * t + 128],
                     func=ACT.Copy,
-                    scale=factor("e", h, s)[:, t : t + 1],
+                    scale=factor(h, s)[:, 2, t : t + 1],
                 )
 
-        plain = {}
+        plain = keep.tile([P, 4, 512], F32, name="plain")
 
         def a_out(h, s):
-            plain[s] = keep.tile([P, 512], F32, name="plain_%d" % s)
-            nc.scalar.copy(out=plain[s][:], in_=abank[h, s][:])
+            nc.scalar.copy(out=plain[:, s, :], in_=abank[h, s][:])
 
         def mirror(s):
             bank = new_bank()
             abank[0, s] = bank
             for t in range(4):
                 col = 128 * (s - 4)
-                nc.tensor.transpose(bank[:, 128 * t : 128 * t + 128], plain[t][:, col : col + 128], ident[:])
+                nc.tensor.transpose(bank[:, 128 * t : 128 * t + 128], plain[:, t, col : col + 128], ident[:])
 
-        def quantize_pair(o, h, sp):
-            col = 256 * (sp % 2)
+        def e_scale(t):
+            nc.gpsimd.tensor_scalar(
+                out=ea_low[:, t, :].rearrange("p (s n) -> p s n", s=4),
+                in0=plain[:, :, 128 * t : 128 * t + 128],
+                scalar1=factor(1, 0)[:, 2, t : t + 1],
+                scalar2=0.0,
+                op0=ALU.mult,
+                op1=ALU.add,
+            )
+
+        def quantize_rl(h, hp, lo, hi):
             nc.vector.quantize_mx(
-                out=qcodes[o, h, sp // 2][:, col : col + 256].bitcast(FP8X4),
-                scales=qscales[o, h, sp // 2][:, col : col + 256],
-                in_=bf[o, h, sp][:].rearrange("p n t -> p (n t)"),
+                out=qcodes[h, hp][:, lo:hi].bitcast(FP8X4),
+                scales=qscales[h, hp][:, lo:hi],
+                in_=bf[h, hp][:].rearrange("p o n t -> p (o n t)")[:, 4 * lo : 4 * hi],
             )
 
         qbank, out_t, il, osb, obank = {}, {}, {}, {}, {}
@@ -207,23 +225,23 @@ def tile_skewgradientquadraticstep_kernel(tc, x, g, c, d, eta, out_0, out_1, out
         def mm2(h, sp, tp):
             bank = new_bank()
             qbank[h, sp, tp] = bank
-            col = 256 * (sp % 2)
             for u in range(2):
-                t = 2 * tp + u
+                cols = slice(256 * tp + 128 * u, 256 * tp + 128 * u + 128)
+                rows = slice(512 + 256 * (sp % 2), 768 + 256 * (sp % 2))
                 for k in range(2):
                     nc.tensor.matmul_mx(
                         out=bank[:, 256 * u : 256 * u + 256],
-                        lhsT=qcodes["r", k, h][:, 128 * t : 128 * t + 128].bitcast(FP8X4),
-                        lhsT_scale=qscales["r", k, h][:, 128 * t : 128 * t + 128],
-                        rhs=qcodes["l", k, sp // 2][:, col : col + 256].bitcast(FP8X4),
-                        rhs_scale=qscales["l", k, sp // 2][:, col : col + 256],
+                        lhsT=qcodes[k, h][:, cols].bitcast(FP8X4),
+                        lhsT_scale=qscales[k, h][:, cols],
+                        rhs=qcodes[k, sp // 2][:, rows].bitcast(FP8X4),
+                        rhs_scale=qscales[k, sp // 2][:, rows],
                         start=(k == 0),
                         stop=(k == 1),
                     )
 
         def combine(h, sp, tp):
             if tp == 0:
-                out_t[h, sp] = work.tile([P, 4, 256], F32, name="out_t", align_bytes=64, bufs=4)
+                out_t[h, sp] = work.tile([P, 4, 256], F32, name="out_t", align_bytes=64, bufs=5)
             for u in range(2):
                 t = 2 * tp + u
                 nc.vector.scalar_tensor_tensor(
@@ -295,16 +313,17 @@ def tile_skewgradientquadraticstep_kernel(tc, x, g, c, d, eta, out_0, out_1, out
 
         make_factors()
         for j, grp in enumerate(groups):
-            for op in ("x", "g"):
-                for i in grp:
-                    transpose_in(op, grp, i)
-                if op == "x":
-                    negate(grp)
-                    if j > 0:
-                        quantize_in("g", groups[j - 1])
-                    quantize_in("x", grp)
+            transpose_in("g", grp, j)
+            quantize_in("g", grp)
+            if j > 0:
+                quantize_in("x", groups[j - 1])
+            transpose_in("x", grp, j)
+            if j < 7:
+                negate(grp)
+            else:
+                negate_from_bank(j)
         mm1(0, 0)
-        quantize_in("g", groups[-1])
+        quantize_in("x", groups[-1])
         mm1(0, 1)
         mm1(0, 2)
         mm1(0, 3)
@@ -312,130 +331,123 @@ def tile_skewgradientquadraticstep_kernel(tc, x, g, c, d, eta, out_0, out_1, out
         mm1(1, 1)
         mm1(1, 2)
         mm1(1, 3)
-        vector_out("r", 0, 0)
-        vector_out("l", 0, 0)
+        l_scale(0, 0)
         e_out(0, 0)
         vector_out("r", 0, 1)
-        vector_out("l", 0, 1)
+        vector_out("r", 0, 0)
+        l_scale(0, 1)
+        l_interleave(0, 0, "G")
         e_out(0, 1)
+        vector_out("r", 0, 2)
+        quantize_rl(0, 0, 0, 256)
         mm1(1, 4)
         mm1(1, 5)
-        vector_out("r", 0, 2)
-        quantize_pair("r", 0, 0)
-        quantize_pair("l", 0, 0)
-        vector_out("l", 0, 2)
-        e_out(0, 2)
         vector_out("r", 0, 3)
-        vector_out("l", 0, 3)
+        l_scale(0, 2)
+        e_out(0, 2)
+        l_scale(0, 3)
+        l_interleave(0, 1, "G")
         e_out(0, 3)
         vector_out("r", 1, 0)
-        quantize_pair("r", 0, 1)
-        quantize_pair("l", 0, 1)
-        vector_out("l", 1, 0)
-        a_out(1, 1)
+        quantize_rl(0, 0, 256, 512)
+        quantize_rl(0, 0, 512, 768)
         vector_out("r", 1, 1)
-        vector_out("l", 1, 1)
-        a_out(1, 2)
         a_out(1, 0)
+        l_scale(1, 0)
+        a_out(1, 1)
+        l_scale(1, 1)
+        l_interleave(1, 0, "G")
+        vector_out("rl", 1, 2)
+        quantize_rl(0, 0, 768, 1024)
+        vector_out("rl", 1, 3)
+        a_out(1, 2)
         a_out(1, 3)
-        e_out(1, 0)
-        e_out(1, 1)
         mirror(4)
         mirror(5)
         mirror(6)
         mirror(7)
-        vector_out("r", 1, 2)
-        quantize_pair("r", 1, 0)
-        quantize_pair("l", 1, 0)
-        vector_out("l", 1, 2)
-        e_out(1, 2)
-        vector_out("r", 1, 3)
-        vector_out("l", 1, 3)
-        e_out(1, 3)
         mm1(1, 6)
         mm1(1, 7)
         vector_out("r", 1, 4)
-        quantize_pair("r", 1, 1)
-        quantize_pair("l", 1, 1)
+        vector_out("r", 1, 5)
+        quantize_rl(1, 0, 0, 1024)
         l_scale(1, 4)
         e_out(1, 4)
-        vector_out("r", 1, 5)
         l_scale(1, 5)
         l_interleave(1, 2, "G")
+        e_scale(0)
+        e_scale(1)
+        e_scale(2)
+        e_scale(3)
         e_out(1, 5)
-        vector_out("r", 0, 4)
-        vector_out("r", 0, 5)
-        quantize_pair("r", 1, 2)
         mm2_unit(0, 0)
-        l_scale(0, 4)
+        vector_out("rl", 0, 4)
+        vector_out("rl", 0, 5)
         e_out(0, 4)
-        vector_out("r", 0, 6)
-        vector_out("r", 0, 7)
-        l_scale(0, 5)
-        l_interleave(0, 2, "G")
         e_out(0, 5)
         mm2_unit(0, 1)
-        combine_unit(0, 0)
-        quantize_pair("r", 0, 2)
-        quantize_pair("r", 0, 3)
-        quantize_pair("l", 1, 2)
-        l_scale(0, 6)
-        e_out(0, 6)
+        vector_out("r", 0, 6)
+        vector_out("r", 0, 7)
         vector_out("r", 1, 6)
         vector_out("r", 1, 7)
+        quantize_rl(0, 1, 0, 512)
+        quantize_rl(1, 1, 0, 512)
+        quantize_rl(0, 1, 512, 768)
+        quantize_rl(1, 1, 512, 768)
+        l_scale(0, 6)
+        e_out(0, 6)
+        l_scale(1, 6)
+        e_out(1, 6)
         l_scale(0, 7)
         l_interleave(0, 3, "G")
         e_out(0, 7)
-        transpose_out(0, 0)
-        vector_out("l", 1, 6)
-        quantize_pair("r", 1, 3)
-        quantize_pair("l", 0, 2)
-        mm2_unit(1, 0)
-        vector_out("l", 1, 7)
-        e_out(1, 6)
+        l_scale(1, 7)
+        l_interleave(1, 3, "G")
         e_out(1, 7)
-        combine_unit(0, 1)
+        mm2_unit(1, 0)
+        combine_unit(0, 0)
+        transpose_out(0, 0)
         mm2_unit(1, 1)
+        combine_unit(0, 1)
         transpose_out(0, 1)
         copy_out(0, 0)
-        quantize_pair("l", 1, 3)
-        quantize_pair("l", 0, 3)
-        interleave_out(0, 0, "V")
-        interleave_out(0, 1, "S")
-        combine_unit(1, 0)
-        interleave_out(1, 0, "G", slice(0, 64))
-        interleave_out(1, 0, "S", slice(64, P))
         copy_out(0, 1)
+        combine_unit(1, 0)
         mm2_unit(0, 2)
         transpose_out(1, 0)
+        interleave_out(0, 0, "V")
         combine_unit(1, 1)
-        quantize_out(0, 0)
-        interleave_out(1, 1, "G", slice(0, 64))
-        interleave_out(1, 1, "S", slice(64, P))
-        mm2_unit(0, 3)
-        transpose_out(1, 1)
+        quantize_rl(0, 1, 768, 1024)
+        quantize_rl(1, 1, 768, 1024)
+        interleave_out(0, 1, "S")
         copy_out(1, 0)
-        combine_unit(0, 2)
-        interleave_out(0, 2, "G", slice(0, 64))
-        interleave_out(0, 2, "S", slice(64, P))
-        copy_out(1, 1)
         mm2_unit(1, 2)
+        transpose_out(1, 1)
+        combine_unit(0, 2)
+        interleave_out(1, 0, "G", slice(0, 80))
+        interleave_out(1, 0, "S", slice(80, P))
+        interleave_out(1, 1, "G", slice(0, 80))
+        interleave_out(1, 1, "S", slice(80, P))
+        quantize_out(0, 0)
+        copy_out(1, 1)
+        mm2_unit(0, 3)
         transpose_out(0, 2)
+        combine_unit(1, 2)
+        mm2_unit(1, 3)
+        transpose_out(1, 2)
+        interleave_out(0, 2, "G")
+        copy_out(0, 2)
         combine_unit(0, 3)
         quantize_out(1, 0)
-        interleave_out(0, 3, "G", slice(0, 64))
-        interleave_out(0, 3, "S", slice(64, P))
-        mm2_unit(1, 3)
+        copy_out(1, 2)
+        interleave_out(1, 2, "V")
+        interleave_out(0, 3, "G", slice(0, 80))
+        interleave_out(0, 3, "S", slice(80, P))
         transpose_out(0, 3)
-        copy_out(0, 2)
-        combine_unit(1, 2)
-        interleave_out(1, 2, "S")
-        copy_out(0, 3)
-        transpose_out(1, 2)
         combine_unit(1, 3)
         quantize_out(0, 1)
+        copy_out(0, 3)
         transpose_out(1, 3)
-        copy_out(1, 2)
         interleave_out(1, 3, "V")
+        copy_out(1, 3, engines="SS")
         quantize_out(1, 1)
-        copy_out(1, 3, engines="SV")

@@ -117,9 +117,7 @@ def tile_skewgradientquadraticstep_kernel(tc, x, g, c, d, eta, out_0, out_1, out
             for sp in range(4)
             if h == 0 or sp >= 2
         }
-        ea_low = keep.tile([P, 4, 512], F32, name="ea_low")
-        for sp in range(2):
-            ea[1, sp] = ea_low[:, :, 256 * sp : 256 * sp + 256]
+
         abank, bf, stage, qcodes, qscales = {}, {}, {}, {}, {}
         for h in range(2):
             for hp in range(2):
@@ -147,7 +145,7 @@ def tile_skewgradientquadraticstep_kernel(tc, x, g, c, d, eta, out_0, out_1, out
 
         def bf_tile(h, hp):
             if (h, hp) not in bf:
-                bf[h, hp] = work.tile([P, 2, 512, 4], BF16, name="bf_rl", align_bytes=64, bufs=3)
+                bf[h, hp] = keep.tile([P, 2, 512, 4], BF16, name="bf_rl", tag="slot_%d%d" % (h, hp), align_bytes=64)
             return bf[h, hp]
 
         def vector_out(o, h, s):
@@ -203,8 +201,12 @@ def tile_skewgradientquadraticstep_kernel(tc, x, g, c, d, eta, out_0, out_1, out
                 nc.tensor.transpose(bank[:, 128 * t : 128 * t + 128], plain[:, t, col : col + 128], ident[:])
 
         def e_scale(t):
+            if t == 0:
+                ea["low"] = keep.tile([P, 4, 512], F32, name="ea_low", tag="slot_00", align_bytes=64)
+                for sp in range(2):
+                    ea[1, sp] = ea["low"][:, :, 256 * sp : 256 * sp + 256]
             nc.gpsimd.tensor_scalar(
-                out=ea_low[:, t, :].rearrange("p (s n) -> p s n", s=4),
+                out=ea["low"][:, t, :].rearrange("p (s n) -> p s n", s=4),
                 in0=plain[:, :, 128 * t : 128 * t + 128],
                 scalar1=factor(1, 0)[:, 2, t : t + 1],
                 scalar2=0.0,
@@ -255,7 +257,7 @@ def tile_skewgradientquadraticstep_kernel(tc, x, g, c, d, eta, out_0, out_1, out
 
         def interleave_out(h, sp, engine, rows=slice(0, P)):
             if (h, sp // 2) not in il:
-                il[h, sp // 2] = work.tile([P, 2048], BF16, name="il", align_bytes=64, bufs=3)
+                il[h, sp // 2] = keep.tile([P, 2048], BF16, name="il", tag={(0, 0): "slot_01", (1, 0): "slot_10", (0, 1): "slot_11", (1, 1): "il_11"}[h, sp // 2], align_bytes=64)
             lo = 2 * (sp % 2)
             out = il[h, sp // 2][:].rearrange("p (m a t) -> p m a t", a=4, t=4)[:, rows, lo : lo + 2, :]
             in_ = out_t[h, sp][:].rearrange("p t (m a) -> p m a t", a=2)[:, rows, :, :]
@@ -326,11 +328,11 @@ def tile_skewgradientquadraticstep_kernel(tc, x, g, c, d, eta, out_0, out_1, out
         quantize_in("x", groups[-1])
         mm1(0, 1)
         mm1(0, 2)
-        mm1(0, 3)
         mm1(1, 0)
         mm1(1, 1)
         mm1(1, 2)
         mm1(1, 3)
+        mm1(0, 3)
         l_scale(0, 0)
         e_out(0, 0)
         vector_out("r", 0, 1)
@@ -338,98 +340,101 @@ def tile_skewgradientquadraticstep_kernel(tc, x, g, c, d, eta, out_0, out_1, out
         l_scale(0, 1)
         l_interleave(0, 0, "G")
         e_out(0, 1)
-        vector_out("r", 0, 2)
-        quantize_rl(0, 0, 0, 256)
         mm1(1, 4)
-        mm1(1, 5)
-        vector_out("r", 0, 3)
-        l_scale(0, 2)
+        vector_out("rl", 0, 2)
         e_out(0, 2)
-        l_scale(0, 3)
-        l_interleave(0, 1, "G")
-        e_out(0, 3)
-        vector_out("r", 1, 0)
-        quantize_rl(0, 0, 256, 512)
+        vector_out("rl", 1, 0)
+        quantize_rl(0, 0, 0, 256)
         quantize_rl(0, 0, 512, 768)
-        vector_out("r", 1, 1)
         a_out(1, 0)
-        l_scale(1, 0)
+        vector_out("rl", 1, 1)
         a_out(1, 1)
-        l_scale(1, 1)
-        l_interleave(1, 0, "G")
-        vector_out("rl", 1, 2)
-        quantize_rl(0, 0, 768, 1024)
-        vector_out("rl", 1, 3)
+        vector_out("r", 1, 2)
+        vector_out("r", 1, 3)
         a_out(1, 2)
         a_out(1, 3)
         mirror(4)
         mirror(5)
         mirror(6)
         mirror(7)
-        mm1(1, 6)
-        mm1(1, 7)
-        vector_out("r", 1, 4)
-        vector_out("r", 1, 5)
-        quantize_rl(1, 0, 0, 1024)
-        l_scale(1, 4)
-        e_out(1, 4)
-        l_scale(1, 5)
-        l_interleave(1, 2, "G")
+        quantize_rl(1, 0, 0, 256)
+        quantize_rl(1, 0, 512, 768)
+        l_scale(1, 2)
+        l_scale(1, 3)
+        l_interleave(1, 1, "G")
         e_scale(0)
         e_scale(1)
-        e_scale(2)
-        e_scale(3)
-        e_out(1, 5)
+        vector_out("rl", 0, 3)
+        e_out(0, 3)
+        quantize_rl(0, 0, 256, 512)
+        quantize_rl(0, 0, 768, 1024)
+        quantize_rl(1, 0, 256, 512)
         mm2_unit(0, 0)
-        vector_out("rl", 0, 4)
-        vector_out("rl", 0, 5)
-        e_out(0, 4)
-        e_out(0, 5)
-        mm2_unit(0, 1)
+        mm1(1, 5)
+        mm1(1, 6)
+        vector_out("r", 1, 4)
+        l_scale(1, 4)
+        e_out(1, 4)
+        vector_out("r", 0, 4)
+        vector_out("r", 0, 5)
         vector_out("r", 0, 6)
         vector_out("r", 0, 7)
-        vector_out("r", 1, 6)
-        vector_out("r", 1, 7)
+        l_scale(0, 4)
+        e_out(0, 4)
+        mm1(1, 7)
+        l_scale(0, 5)
+        l_interleave(0, 2, "G")
+        e_scale(2)
+        e_scale(3)
+        e_out(0, 5)
         quantize_rl(0, 1, 0, 512)
-        quantize_rl(1, 1, 0, 512)
-        quantize_rl(0, 1, 512, 768)
-        quantize_rl(1, 1, 512, 768)
+        quantize_rl(1, 0, 768, 1024)
+        mm2_unit(0, 1)
+        combine_unit(0, 0)
+        transpose_out(0, 0)
+        vector_out("r", 1, 5)
+        vector_out("r", 1, 6)
         l_scale(0, 6)
         e_out(0, 6)
-        l_scale(1, 6)
-        e_out(1, 6)
+        vector_out("r", 1, 7)
+        copy_out(0, 0)
         l_scale(0, 7)
         l_interleave(0, 3, "G")
         e_out(0, 7)
-        l_scale(1, 7)
-        l_interleave(1, 3, "G")
-        e_out(1, 7)
+        combine(0, 1, 0)
+        quantize_rl(1, 1, 0, 512)
+        quantize_rl(0, 1, 512, 768)
         mm2_unit(1, 0)
-        combine_unit(0, 0)
-        transpose_out(0, 0)
-        mm2_unit(1, 1)
-        combine_unit(0, 1)
+        combine(0, 1, 1)
         transpose_out(0, 1)
-        copy_out(0, 0)
+        vector_out("l", 1, 6)
+        vector_out("l", 1, 7)
+        l_scale(1, 5)
+        l_interleave(1, 2, "G")
+        e_out(1, 5)
+        mm2_unit(1, 1)
+        e_out(1, 6)
+        e_out(1, 7)
         copy_out(0, 1)
         combine_unit(1, 0)
-        mm2_unit(0, 2)
         transpose_out(1, 0)
-        interleave_out(0, 0, "V")
-        combine_unit(1, 1)
+        combine(1, 1, 0)
+        quantize_rl(1, 1, 512, 1024)
         quantize_rl(0, 1, 768, 1024)
-        quantize_rl(1, 1, 768, 1024)
-        interleave_out(0, 1, "S")
-        copy_out(1, 0)
+        interleave_out(0, 0, "G")
+        mm2_unit(0, 2)
+        combine(1, 1, 1)
         mm2_unit(1, 2)
         transpose_out(1, 1)
+        interleave_out(0, 1, "S")
+        copy_out(1, 0)
         combine_unit(0, 2)
         interleave_out(1, 0, "G", slice(0, 80))
         interleave_out(1, 0, "S", slice(80, P))
-        interleave_out(1, 1, "G", slice(0, 80))
-        interleave_out(1, 1, "S", slice(80, P))
         quantize_out(0, 0)
         copy_out(1, 1)
+        interleave_out(1, 1, "G", slice(0, 80))
+        interleave_out(1, 1, "S", slice(80, P))
         mm2_unit(0, 3)
         transpose_out(0, 2)
         combine_unit(1, 2)
@@ -439,14 +444,14 @@ def tile_skewgradientquadraticstep_kernel(tc, x, g, c, d, eta, out_0, out_1, out
         copy_out(0, 2)
         combine_unit(0, 3)
         quantize_out(1, 0)
+        interleave_out(0, 3, "G")
         copy_out(1, 2)
-        interleave_out(1, 2, "V")
-        interleave_out(0, 3, "G", slice(0, 80))
-        interleave_out(0, 3, "S", slice(80, P))
         transpose_out(0, 3)
         combine_unit(1, 3)
-        quantize_out(0, 1)
         copy_out(0, 3)
+        interleave_out(1, 2, "V", slice(0, 64))
+        interleave_out(1, 2, "S", slice(64, P))
+        quantize_out(0, 1)
         transpose_out(1, 3)
         interleave_out(1, 3, "V")
         copy_out(1, 3, engines="SS")

@@ -257,14 +257,14 @@ def tile_skewgradientquadraticstep_kernel(tc, x, g, c, d, eta, out_0, out_1, out
 
         def interleave_out(h, sp, engine, rows=slice(0, P)):
             if (h, sp // 2) not in il:
-                il[h, sp // 2] = keep.tile([P, 2048], BF16, name="il", tag={(0, 0): "slot_01", (1, 0): "slot_10", (0, 1): "slot_11", (1, 1): "il_11"}[h, sp // 2], align_bytes=64)
+                il[h, sp // 2] = keep.tile([P, 2048], BF16, name="il", tag={(0, 0): "slot_01", (1, 0): "slot_01", (0, 1): "slot_01", (1, 1): "il_11"}[h, sp // 2], align_bytes=64)
             lo = 2 * (sp % 2)
             out = il[h, sp // 2][:].rearrange("p (m a t) -> p m a t", a=4, t=4)[:, rows, lo : lo + 2, :]
             in_ = out_t[h, sp][:].rearrange("p t (m a) -> p m a t", a=2)[:, rows, :, :]
             if engine == "V":
-                nc.vector.tensor_copy(out=out, in_=in_)
+                nc.vector.tensor_copy(out=out.rearrange("p m a t -> p m t a"), in_=in_.rearrange("p m a t -> p m t a"))
             elif engine == "S":
-                nc.scalar.copy(out=out, in_=in_)
+                nc.scalar.copy(out=out.rearrange("p m a t -> p m t a"), in_=in_.rearrange("p m a t -> p m t a"))
             else:
                 nc.gpsimd.tensor_scalar(out=out, in0=in_, scalar1=1.0, scalar2=0.0, op0=ALU.mult, op1=ALU.add)
 
@@ -277,7 +277,7 @@ def tile_skewgradientquadraticstep_kernel(tc, x, g, c, d, eta, out_0, out_1, out
             )
             if (h, hp) == (1, 1):
                 for quad in range(4):
-                    nc.sync.dma_start(
+                    nc.scalar.dma_start(
                         out=out_2[:, 4 * quad : 4 * quad + 4, :].bitcast(I32),
                         in_=oscale[32 * quad : 32 * quad + 8, :].bitcast(I32),
                     )
@@ -424,35 +424,32 @@ def tile_skewgradientquadraticstep_kernel(tc, x, g, c, d, eta, out_0, out_1, out
         interleave_out(0, 0, "G")
         mm2_unit(0, 2)
         combine(1, 1, 1)
-        mm2_unit(1, 2)
+        mm2_unit(0, 3)
         transpose_out(1, 1)
         interleave_out(0, 1, "S")
         copy_out(1, 0)
         combine_unit(0, 2)
-        interleave_out(1, 0, "G", slice(0, 80))
-        interleave_out(1, 0, "S", slice(80, P))
         quantize_out(0, 0)
+        interleave_out(1, 0, "G")
         copy_out(1, 1)
-        interleave_out(1, 1, "G", slice(0, 80))
-        interleave_out(1, 1, "S", slice(80, P))
-        mm2_unit(0, 3)
+        interleave_out(1, 1, "S")
+        mm2_unit(1, 2)
         transpose_out(0, 2)
-        combine_unit(1, 2)
-        mm2_unit(1, 3)
-        transpose_out(1, 2)
-        interleave_out(0, 2, "G")
-        copy_out(0, 2)
         combine_unit(0, 3)
-        quantize_out(1, 0)
-        interleave_out(0, 3, "G")
-        copy_out(1, 2)
+        mm2_unit(1, 3)
         transpose_out(0, 3)
-        combine_unit(1, 3)
+        copy_out(0, 2)
+        combine_unit(1, 2)
+        quantize_out(1, 0)
+        interleave_out(0, 2, "G")
         copy_out(0, 3)
-        interleave_out(1, 2, "V", slice(0, 64))
-        interleave_out(1, 2, "S", slice(64, P))
-        quantize_out(0, 1)
+        transpose_out(1, 2)
+        combine_unit(1, 3)
+        interleave_out(0, 3, "S")
+        copy_out(1, 2, engines="VV")
         transpose_out(1, 3)
+        interleave_out(1, 2, "V")
+        quantize_out(0, 1)
         interleave_out(1, 3, "V")
         copy_out(1, 3, engines="SS")
         quantize_out(1, 1)

@@ -37,16 +37,14 @@ def tile_skewgradientquadraticstep_kernel(tc, x, g, c, d, eta, out_0, out_1, out
             raw[op, i] = keep.tile([P, N], BF16, name="raw_%s%d" % (op, i))
             nc.sync.dma_start(out=raw[op, i][:], in_=src[op][i // 4, i % 4])
 
-        load("g", 0)
-        load("x", 0)
+        for i in range(8):
+            load("g", i)
+            load("x", i)
         vecs = keep.tile([P, 3, 16], BF16, name="vecs")
         for v, vec in enumerate((c, d, eta)):
             nc.sync.dma_start(
                 out=vecs[:, v, 0:8].rearrange("p (h t) -> p h t", h=2), in_=vec.rearrange("(h p t) -> p h t", h=2, t=4)
             )
-        for i in range(1, 8):
-            load("g", i)
-            load("x", i)
 
         ident = keep.tile([P, P], F32, name="ident")
         make_identity(nc, ident[:])
@@ -56,19 +54,22 @@ def tile_skewgradientquadraticstep_kernel(tc, x, g, c, d, eta, out_0, out_1, out
         def make_factors():
             fac["a"] = keep.tile([P, 6, 8], F32, name="fac_a")
             for dst, first, last, scale in ((slice(1, 6, 2), 0, 3, -RSQRT2), (slice(0, 3, 2), 1, 3, RSQRT2), (slice(4, 5), 0, 1, RSQRT2)):
-                nc.scalar.activation(out=fac["a"][:, dst, :], in_=vecs[:, first:last, 0:8], func=ACT.Copy, scale=scale)
+                nc.vector.tensor_scalar(
+                    out=fac["a"][:, dst, :], in0=vecs[:, first:last, 0:8], scalar1=scale, scalar2=None, op0=ALU.mult
+                )
             fac["h"] = keep.tile([P, 8], F32, name="fac_h")
-            nc.scalar.activation(out=fac["h"][:], in_=vecs[:, 2, 0:8], func=ACT.Square, scale=0.125)
+            nc.vector.scalar_tensor_tensor(
+                out=fac["h"][:], in0=vecs[:, 2, 0:8], scalar=1.0 / 64.0, in1=vecs[:, 2, 0:8], op0=ALU.mult, op1=ALU.mult
+            )
 
         def factor(h, s):
             return fac["a"][:, 3:6, 0:4] if h == 0 and s >= 4 else fac["a"][:, 0:3, 4 * h : 4 * h + 4]
 
-        codes, scales, xt, in_bank = {}, {}, {}, {}
+        codes, scales, xt = {}, {}, {}
 
         def transpose_in(op, grp, i):
             words = raw[op, i][:].bitcast(F32)
             bank = new_bank()
-            in_bank[op, i] = bank
             for gi in range(2):
                 for u in range(2):
                     lo = 128 * (2 * gi + u)
@@ -87,16 +88,6 @@ def tile_skewgradientquadraticstep_kernel(tc, x, g, c, d, eta, out_0, out_1, out
             nc.vector.tensor_scalar(
                 out=xt["x", grp][:, width : 2 * width], in0=xt["x", grp][:, 0:width], scalar1=-1.0, scalar2=None, op0=ALU.mult
             )
-
-        def negate_from_bank(i):
-            for gi in range(2):
-                lo = 1024 + 512 * gi
-                nc.scalar.activation(
-                    out=xt["x", (i,)][:, lo : lo + 512].rearrange("p (m u e) -> p m u e", u=2, e=2),
-                    in_=in_bank["x", i][:, 256 * gi : 256 * gi + 256].bitcast(BF16).rearrange("p (u m e) -> p m u e", u=2, e=2),
-                    func=ACT.Copy,
-                    scale=-1.0,
-                )
 
         def quantize_in(op, grp):
             names = ("x", "n") if op == "x" else ("g",)
@@ -313,18 +304,15 @@ def tile_skewgradientquadraticstep_kernel(tc, x, g, c, d, eta, out_0, out_1, out
             for tp in range(2):
                 combine(h, sp, tp)
 
-        make_factors()
         for j, grp in enumerate(groups):
             transpose_in("g", grp, j)
             quantize_in("g", grp)
             if j > 0:
                 quantize_in("x", groups[j - 1])
             transpose_in("x", grp, j)
-            if j < 7:
-                negate(grp)
-            else:
-                negate_from_bank(j)
+            negate(grp)
         mm1(0, 0)
+        make_factors()
         quantize_in("x", groups[-1])
         mm1(0, 1)
         mm1(0, 2)

@@ -134,16 +134,36 @@ def tile_skewgradientquadraticstep_kernel(tc, x, g, c, d, eta, out_0, out_1, out
                         )
                         step += 1
 
-        def bf_tile(h, hp):
-            if (h, hp) not in bf:
-                bf[h, hp] = keep.tile([P, 2, 512, 4], BF16, name="bf_rl", tag="slot_%d%d" % (h, hp), align_bytes=64)
-            return bf[h, hp]
+        def bf_tile(o, h, hp):
+            if hp == 0:
+                if (h, 0) not in bf:
+                    bf[h, 0] = keep.tile([P, 2, 512, 4], BF16, name="bf_rl", tag="slot_%d0" % h, align_bytes=64)
+                lo = 1 if o == "l" else 0
+                return bf[h, 0][:, lo : lo + len(o), :, :]
+            if (o, h) not in bf:
+                bf[o, h] = keep.tile([P, 1, 512, 4], BF16, name="bf_" + o, tag={("r", 0): "r0", ("r", 1): "r1", ("l", 1): "l02"}[o, h], align_bytes=64)
+            return bf[o, h][:]
+
+        def l_pair(h, sp):
+            if h == 0 and sp >= 2:
+                if ("l", 0, sp) not in bf:
+                    bf["l", 0, sp] = keep.tile([P, 256, 4], BF16, name="bf_l0", tag=("l02", "l02")[sp - 2], align_bytes=64)
+                return bf["l", 0, sp][:]
+            return bf_tile("l", h, sp // 2)[:, 0, 256 * (sp % 2) : 256 * (sp % 2) + 256, :]
 
         def vector_out(o, h, s):
             col = 128 * (s % 4)
+            if (o, h) == ("l", 0) and s >= 4:
+                nc.vector.tensor_tensor(
+                    out=l_pair(0, s // 2)[:, col % 256 : col % 256 + 128, :],
+                    in0=abank[h, s][:].rearrange("p (t n) -> p n t", t=4),
+                    in1=factor(h, s)[:, 1, :].unsqueeze(1).to_broadcast([P, 128, 4]),
+                    op=ALU.mult,
+                )
+                return
             lo, n = {"r": 0, "l": 1, "rl": 0}[o], len(o)
             nc.vector.tensor_tensor(
-                out=bf_tile(h, s // 4)[:, lo : lo + n, col : col + 128, :],
+                out=bf_tile(o, h, s // 4)[:, :, col : col + 128, :],
                 in0=abank[h, s][:].rearrange("p (t n) -> p n t", t=4).unsqueeze(1).to_broadcast([P, n, 128, 4]),
                 in1=factor(h, s)[:, lo : lo + n, :].unsqueeze(2).to_broadcast([P, n, 128, 4]),
                 op=ALU.mult,
@@ -162,7 +182,7 @@ def tile_skewgradientquadraticstep_kernel(tc, x, g, c, d, eta, out_0, out_1, out
                 )
 
         def l_interleave(h, sp, engine):
-            out = bf_tile(h, sp // 2)[:, 1, 256 * (sp % 2) : 256 * (sp % 2) + 256, :]
+            out = l_pair(h, sp)
             in_ = stage[h, sp][:].rearrange("p t n -> p n t")
             if engine == "S":
                 nc.scalar.copy(out=out, in_=in_)
@@ -179,6 +199,7 @@ def tile_skewgradientquadraticstep_kernel(tc, x, g, c, d, eta, out_0, out_1, out
                     scale=factor(h, s)[:, 2, t : t + 1],
                 )
 
+        low = {}
         plain = keep.tile([P, 4, 512], F32, name="plain")
 
         def a_out(h, s):
@@ -192,12 +213,10 @@ def tile_skewgradientquadraticstep_kernel(tc, x, g, c, d, eta, out_0, out_1, out
                 nc.tensor.transpose(bank[:, 128 * t : 128 * t + 128], plain[:, t, col : col + 128], ident[:])
 
         def e_scale(t):
-            if t == 0:
-                ea["low"] = keep.tile([P, 4, 512], F32, name="ea_low", tag="slot_00", align_bytes=64)
-                for sp in range(2):
-                    ea[1, sp] = ea["low"][:, :, 256 * sp : 256 * sp + 256]
+            if t % 2 == 0:
+                low[t // 2] = keep.tile([P, 2, 512], F32, name="ea_low", tag=("low0", "slot_10")[t // 2], align_bytes=64)
             nc.gpsimd.tensor_scalar(
-                out=ea["low"][:, t, :].rearrange("p (s n) -> p s n", s=4),
+                out=low[t // 2][:, t % 2, :].rearrange("p (s n) -> p s n", s=4),
                 in0=plain[:, :, 128 * t : 128 * t + 128],
                 scalar1=factor(1, 0)[:, 2, t : t + 1],
                 scalar2=0.0,
@@ -205,11 +224,25 @@ def tile_skewgradientquadraticstep_kernel(tc, x, g, c, d, eta, out_0, out_1, out
                 op1=ALU.add,
             )
 
+        def ea_row(h, sp, t):
+            if h == 1 and sp < 2:
+                return low[t // 2][:, t % 2, 256 * sp : 256 * sp + 256]
+            return ea[h, sp][:, t, :]
+
         def quantize_rl(h, hp, lo, hi):
+            o = "r" if lo < 512 else "l"
+            first = lo % 512
+            if hp == 0:
+                nc.vector.quantize_mx(
+                    out=qcodes[h, hp][:, lo:hi].bitcast(FP8X4),
+                    scales=qscales[h, hp][:, lo:hi],
+                    in_=bf_tile("rl", h, 0).rearrange("p o n t -> p (o n t)")[:, 4 * lo : 4 * hi],
+                )
+                return
             nc.vector.quantize_mx(
                 out=qcodes[h, hp][:, lo:hi].bitcast(FP8X4),
                 scales=qscales[h, hp][:, lo:hi],
-                in_=bf[h, hp][:].rearrange("p o n t -> p (o n t)")[:, 4 * lo : 4 * hi],
+                in_=(l_pair(0, 2 + first // 256) if (o, h, hp) == ("l", 0, 1) else bf_tile(o, h, hp)[:, 0, first : first + hi - lo, :]).rearrange("p n t -> p (n t)"),
             )
 
         qbank, out_t, il, osb, obank = {}, {}, {}, {}, {}
@@ -234,21 +267,21 @@ def tile_skewgradientquadraticstep_kernel(tc, x, g, c, d, eta, out_0, out_1, out
 
         def combine(h, sp, tp):
             if tp == 0:
-                out_t[h, sp] = work.tile([P, 4, 256], F32, name="out_t", align_bytes=64, bufs=5)
+                out_t[h, sp] = work.tile([P, 4, 256], F32, name="out_t", align_bytes=64, bufs=7)
             for u in range(2):
                 t = 2 * tp + u
                 nc.vector.scalar_tensor_tensor(
                     out=out_t[h, sp][:, t, :].rearrange("p (m a) -> p m a", a=2),
                     in0=qbank[h, sp, tp][:, 256 * u : 256 * u + 256].rearrange("p (a m) -> p m a", a=2),
                     scalar=fac["h"][:, 4 * h + t : 4 * h + t + 1],
-                    in1=ea[h, sp][:, t, :].rearrange("p (a m) -> p m a", a=2),
+                    in1=ea_row(h, sp, t).rearrange("p (a m) -> p m a", a=2),
                     op0=ALU.mult,
                     op1=ALU.add,
                 )
 
         def interleave_out(h, sp, engine, rows=slice(0, P)):
             if (h, sp // 2) not in il:
-                il[h, sp // 2] = keep.tile([P, 2048], BF16, name="il", tag={(0, 0): "slot_01", (1, 0): "slot_01", (0, 1): "slot_01", (1, 1): "il_11"}[h, sp // 2], align_bytes=64)
+                il[h, sp // 2] = keep.tile([P, 2048], BF16, name="il", tag={(0, 0): "r1", (1, 0): "r1", (0, 1): "slot_00", (1, 1): "r0"}[h, sp // 2], align_bytes=64)
             lo = 2 * (sp % 2)
             out = il[h, sp // 2][:].rearrange("p (m a t) -> p m a t", a=4, t=4)[:, rows, lo : lo + 2, :]
             in_ = out_t[h, sp][:].rearrange("p t (m a) -> p m a t", a=2)[:, rows, :, :]
@@ -331,113 +364,111 @@ def tile_skewgradientquadraticstep_kernel(tc, x, g, c, d, eta, out_0, out_1, out
         mm1(1, 4)
         vector_out("rl", 0, 2)
         e_out(0, 2)
-        vector_out("rl", 1, 0)
+        vector_out("r", 1, 0)
+        a_out(1, 0)
+        l_scale(1, 0)
+        vector_out("r", 1, 1)
         quantize_rl(0, 0, 0, 256)
         quantize_rl(0, 0, 512, 768)
-        a_out(1, 0)
-        vector_out("rl", 1, 1)
+        quantize_rl(1, 0, 0, 256)
         a_out(1, 1)
-        vector_out("r", 1, 2)
-        vector_out("r", 1, 3)
+        l_scale(1, 1)
+        l_interleave(1, 0, "G")
+        vector_out("rl", 1, 2)
         a_out(1, 2)
+        vector_out("rl", 1, 3)
         a_out(1, 3)
         mirror(4)
         mirror(5)
         mirror(6)
         mirror(7)
-        quantize_rl(1, 0, 0, 256)
-        quantize_rl(1, 0, 512, 768)
-        l_scale(1, 2)
-        l_scale(1, 3)
-        l_interleave(1, 1, "G")
         e_scale(0)
         e_scale(1)
         vector_out("rl", 0, 3)
         e_out(0, 3)
-        quantize_rl(0, 0, 256, 512)
-        quantize_rl(0, 0, 768, 1024)
-        quantize_rl(1, 0, 256, 512)
-        mm2_unit(0, 0)
         mm1(1, 5)
         mm1(1, 6)
         vector_out("r", 1, 4)
-        l_scale(1, 4)
-        e_out(1, 4)
         vector_out("r", 0, 4)
         vector_out("r", 0, 5)
-        vector_out("r", 0, 6)
-        vector_out("r", 0, 7)
-        l_scale(0, 4)
-        e_out(0, 4)
-        mm1(1, 7)
-        l_scale(0, 5)
-        l_interleave(0, 2, "G")
+        quantize_rl(0, 0, 256, 512)
+        quantize_rl(0, 0, 768, 1024)
+        quantize_rl(1, 0, 768, 1024)
+        quantize_rl(1, 0, 256, 768)
         e_scale(2)
         e_scale(3)
+        l_scale(1, 4)
+        e_out(1, 4)
+        mm1(1, 7)
+        l_scale(0, 4)
+        e_out(0, 4)
+        mm2_unit(0, 0)
+        l_scale(0, 5)
+        l_interleave(0, 2, "G")
         e_out(0, 5)
-        quantize_rl(0, 1, 0, 512)
-        quantize_rl(1, 0, 768, 1024)
-        mm2_unit(0, 1)
-        combine_unit(0, 0)
-        transpose_out(0, 0)
+        vector_out("r", 0, 6)
+        vector_out("r", 0, 7)
         vector_out("r", 1, 5)
         vector_out("r", 1, 6)
-        l_scale(0, 6)
-        e_out(0, 6)
         vector_out("r", 1, 7)
-        copy_out(0, 0)
-        l_scale(0, 7)
-        l_interleave(0, 3, "G")
-        e_out(0, 7)
-        combine(0, 1, 0)
+        l_scale(1, 5)
+        e_out(1, 5)
+        mm2_unit(0, 1)
+        combine(0, 0, 0)
+        quantize_rl(0, 1, 0, 512)
         quantize_rl(1, 1, 0, 512)
         quantize_rl(0, 1, 512, 768)
+        l_interleave(1, 2, "G")
         mm2_unit(1, 0)
-        combine(0, 1, 1)
+        l_scale(0, 6)
+        e_out(0, 6)
+        l_scale(0, 7)
+        e_out(0, 7)
+        combine(0, 0, 1)
+        interleave_out(0, 0, "S")
+        transpose_out(0, 0)
+        copy_out(0, 0)
+        combine_unit(0, 1)
+        mm2_unit(1, 1)
         transpose_out(0, 1)
         vector_out("l", 1, 6)
         vector_out("l", 1, 7)
-        l_scale(1, 5)
-        l_interleave(1, 2, "G")
-        e_out(1, 5)
-        mm2_unit(1, 1)
         e_out(1, 6)
         e_out(1, 7)
+        quantize_rl(1, 1, 512, 1024)
+        l_interleave(0, 3, "G")
+        mm2_unit(0, 2)
+        interleave_out(0, 1, "S")
         copy_out(0, 1)
         combine_unit(1, 0)
         transpose_out(1, 0)
-        combine(1, 1, 0)
-        quantize_rl(1, 1, 512, 1024)
-        quantize_rl(0, 1, 768, 1024)
-        interleave_out(0, 0, "G")
-        mm2_unit(0, 2)
-        combine(1, 1, 1)
-        mm2_unit(0, 3)
-        transpose_out(1, 1)
-        interleave_out(0, 1, "S")
+        mm2_unit(1, 2)
         copy_out(1, 0)
-        combine_unit(0, 2)
+        combine_unit(1, 1)
+        quantize_rl(0, 1, 768, 1024)
         quantize_out(0, 0)
         interleave_out(1, 0, "G")
+        interleave_out(1, 1, "G")
+        transpose_out(1, 1)
+        mm2_unit(0, 3)
         copy_out(1, 1)
-        interleave_out(1, 1, "S")
-        mm2_unit(1, 2)
+        combine_unit(0, 2)
         transpose_out(0, 2)
-        combine_unit(0, 3)
-        mm2_unit(1, 3)
-        transpose_out(0, 3)
+        interleave_out(0, 2, "S")
         copy_out(0, 2)
         combine_unit(1, 2)
-        quantize_out(1, 0)
-        interleave_out(0, 2, "G")
-        copy_out(0, 3)
         transpose_out(1, 2)
+        mm2_unit(1, 3)
+        combine_unit(0, 3)
+        copy_out(1, 2)
+        transpose_out(0, 3)
         combine_unit(1, 3)
-        interleave_out(0, 3, "S")
-        copy_out(1, 2, engines="VV")
+        quantize_out(1, 0)
         transpose_out(1, 3)
+        copy_out(0, 3)
+        copy_out(1, 3, engines="SS")
+        interleave_out(0, 3, "V")
         interleave_out(1, 2, "V")
         quantize_out(0, 1)
         interleave_out(1, 3, "V")
-        copy_out(1, 3, engines="SS")
         quantize_out(1, 1)

@@ -11,12 +11,27 @@ U32 = mybir.dt.uint32
 U8 = mybir.dt.uint8
 FP8X4 = mybir.dt.float8_e4m3fn_x4
 ALU = mybir.AluOpType
-ACT = mybir.ActivationFunctionType
+COPY = mybir.ActivationFunctionType.Copy
 
 N = 1024
 P = 128
 FLOPS = 2 * 2 * N * N * N
 RSQRT2 = 1.0 / math.sqrt(2.0)
+PSUM_BANKS = 8
+TURNED_BUFS = 3
+L_ROWS_BUFS = 3
+OUT_T_BUFS = 7
+ROWS_BUFS = 4
+Q_SCALE = 0.5 / 32.0
+
+SLOT = {
+    ("rl", 0): "a", ("planes", 0, 1): "a",
+    ("rl", 1): "b", ("eta_a", 1): "b",
+    ("r", 0): "c", ("planes", 1, 1): "c",
+    ("r", 1): "d", ("planes", 0, 0): "d", ("planes", 1, 0): "d",
+    ("l", 0, 2): "e", ("l", 1): "e", ("l", 0, 3): "e",
+    ("eta_a", 0): "f",
+}
 
 
 def tile_skewgradientquadraticstep_kernel(tc, x, g, c, d, eta, out_0, out_1, out_2):
@@ -24,451 +39,394 @@ def tile_skewgradientquadraticstep_kernel(tc, x, g, c, d, eta, out_0, out_1, out
     with ExitStack() as ctx:
         keep = ctx.enter_context(tc.tile_pool(name="keep", bufs=1))
         work = ctx.enter_context(tc.tile_pool(name="work", bufs=2))
-        psum = ctx.enter_context(tc.psum_pool(name="psum", bufs=8))
+        psum = ctx.enter_context(tc.psum_pool(name="psum", bufs=PSUM_BANKS))
         ctx.enter_context(tc.manual_schedule())
 
         def new_bank():
             return psum.tile([P, 512], F32, name="bank")
 
+        shared = {}
+
+        def slot_tile(key, shape, dtype):
+            if key not in shared:
+                shared[key] = keep.tile(shape, dtype, name=key[0], tag="slot_" + SLOT[key], align_bytes=64)
+            return shared[key]
+
         src = {"x": x.rearrange("(h m t) k -> h t m k", h=2, t=4), "g": g.rearrange("(h m t) k -> h t m k", h=2, t=4)}
         raw = {}
-
-        def load(op, i):
-            raw[op, i] = keep.tile([P, N], BF16, name="raw_%s%d" % (op, i))
-            nc.sync.dma_start(out=raw[op, i][:], in_=src[op][i // 4, i % 4])
-
-        for i in range(8):
-            load("g", i)
-            load("x", i)
+        for s in range(8):
+            for op in ("g", "x"):
+                raw[op, s] = keep.tile([P, N], BF16, name="raw_%s%d" % (op, s))
+                nc.sync.dma_start(out=raw[op, s][:], in_=src[op][s // 4, s % 4])
         vecs = keep.tile([P, 3, 16], BF16, name="vecs")
         for v, vec in enumerate((c, d, eta)):
             nc.sync.dma_start(
                 out=vecs[:, v, 0:8].rearrange("p (h t) -> p h t", h=2), in_=vec.rearrange("(h p t) -> p h t", h=2, t=4)
             )
-
         ident = keep.tile([P, P], F32, name="ident")
         make_identity(nc, ident[:])
 
-        fac = {}
+        row_factor = keep.tile([P, 6, 8], F32, name="row_factor")
+        q_factor = keep.tile([P, 8], F32, name="q_factor")
 
         def make_factors():
-            fac["a"] = keep.tile([P, 6, 8], F32, name="fac_a")
-            for dst, first, last, scale in ((slice(1, 6, 2), 0, 3, -RSQRT2), (slice(0, 3, 2), 1, 3, RSQRT2), (slice(4, 5), 0, 1, RSQRT2)):
+            for rows, first, last, sign in ((slice(1, 6, 2), 0, 3, -1.0), (slice(0, 3, 2), 1, 3, 1.0), (slice(4, 5), 0, 1, 1.0)):
                 nc.vector.tensor_scalar(
-                    out=fac["a"][:, dst, :], in0=vecs[:, first:last, 0:8], scalar1=scale, scalar2=None, op0=ALU.mult
+                    out=row_factor[:, rows, :], in0=vecs[:, first:last, 0:8], scalar1=sign * RSQRT2, scalar2=None, op0=ALU.mult
                 )
-            fac["h"] = keep.tile([P, 8], F32, name="fac_h")
             nc.vector.scalar_tensor_tensor(
-                out=fac["h"][:], in0=vecs[:, 2, 0:8], scalar=1.0 / 64.0, in1=vecs[:, 2, 0:8], op0=ALU.mult, op1=ALU.mult
+                out=q_factor[:], in0=vecs[:, 2, 0:8], scalar=Q_SCALE, in1=vecs[:, 2, 0:8], op0=ALU.mult, op1=ALU.mult
             )
 
         def factor(h, s):
-            return fac["a"][:, 3:6, 0:4] if h == 0 and s >= 4 else fac["a"][:, 0:3, 4 * h : 4 * h + 4]
+            return row_factor[:, 3:6, 0:4] if h == 0 and s >= 4 else row_factor[:, 0:3, 4 * h : 4 * h + 4]
 
-        codes, scales, xt = {}, {}, {}
+        codes, scales, turned = {}, {}, {}
 
-        def transpose_in(op, grp, i):
-            words = raw[op, i][:].bitcast(F32)
+        def transpose_in(op, s):
+            words = raw[op, s][:].bitcast(F32)
             bank = new_bank()
-            for gi in range(2):
+            for h in range(2):
                 for u in range(2):
-                    lo = 128 * (2 * gi + u)
-                    nc.tensor.transpose(bank[:, lo : lo + 128], words[:, 256 * gi + u : 256 * gi + 256 : 2], ident[:])
-            if i == grp[0]:
-                signs = 2 if op == "x" else 1
-                xt[op, grp] = work.tile([P, signs * len(grp) * 1024], BF16, name="xt_" + op, align_bytes=64, bufs=3)
-            pos = i - grp[0]
+                    lo = 128 * (2 * h + u)
+                    nc.tensor.transpose(bank[:, lo : lo + 128], words[:, 256 * h + u : 256 * h + 256 : 2], ident[:])
+            width = 2 * N if op == "x" else N
+            turned[op, s] = work.tile([P, width], BF16, name="turned_" + op, align_bytes=64, bufs=TURNED_BUFS)
             nc.scalar.copy(
-                out=xt[op, grp][:, 1024 * pos : 1024 * pos + 1024].bitcast(F32).rearrange("p (g m u) -> p g m u", g=2, u=2),
-                in_=bank[:].rearrange("p (g u m) -> p g m u", g=2, u=2),
+                out=turned[op, s][:, 0:N].bitcast(F32).rearrange("p (h m u) -> p h m u", h=2, u=2),
+                in_=bank[:].rearrange("p (h u m) -> p h m u", h=2, u=2),
             )
 
-        def negate(grp):
-            width = 1024 * len(grp)
+        def negate(s):
             nc.vector.tensor_scalar(
-                out=xt["x", grp][:, width : 2 * width], in0=xt["x", grp][:, 0:width], scalar1=-1.0, scalar2=None, op0=ALU.mult
+                out=turned["x", s][:, N : 2 * N], in0=turned["x", s][:, 0:N], scalar1=-1.0, scalar2=None, op0=ALU.mult
             )
 
-        def quantize_in(op, grp):
-            names = ("x", "n") if op == "x" else ("g",)
-            width = 256 * len(grp)
-            cw = keep.tile([P, len(names) * width], U32, name="codes_%s%d" % (op, grp[0]), align_bytes=64)
-            sc = keep.tile([P, len(names) * width], U8, name="scales_%s%d" % (op, grp[0]), align_bytes=64)
-            nc.vector.quantize_mx(out=cw[:].bitcast(FP8X4), scales=sc[:], in_=xt[op, grp][:])
-            for sign, name in enumerate(names):
-                for i in grp:
-                    for gi in range(2):
-                        lo = width * sign + 256 * (i - grp[0]) + 128 * gi
-                        codes[name, i, gi] = cw[:, lo : lo + 128].bitcast(FP8X4)
-                        scales[name, i, gi] = sc[:, lo : lo + 128]
+        def quantize_in(op, s):
+            names = ("x", "minus_x") if op == "x" else ("g",)
+            words = keep.tile([P, 256 * len(names)], U32, name="codes_%s%d" % (op, s), align_bytes=64)
+            plane = keep.tile([P, 256 * len(names)], U8, name="scales_%s%d" % (op, s), align_bytes=64)
+            nc.vector.quantize_mx(out=words[:].bitcast(FP8X4), scales=plane[:], in_=turned[op, s][:])
+            for pos, name in enumerate(names):
+                for h in range(2):
+                    lo = 256 * pos + 128 * h
+                    codes[name, s, h] = words[:, lo : lo + 128].bitcast(FP8X4)
+                    scales[name, s, h] = plane[:, lo : lo + 128]
 
-        ea = {
-            (h, sp): keep.tile([P, 4, 256], F32, name="ea_%d%d" % (h, sp))[:]
-            for h in range(2)
-            for sp in range(4)
-            if h == 0 or sp >= 2
-        }
-
-        abank, bf, stage, qcodes, qscales = {}, {}, {}, {}, {}
+        a_bank, l_rows, eta_a, rl_codes, rl_scales = {}, {}, {}, {}, {}
         for h in range(2):
+            for sp in range(4):
+                if h == 0 or sp >= 2:
+                    eta_a[h, sp] = keep.tile([P, 4, 256], F32, name="eta_a_%d%d" % (h, sp))
             for hp in range(2):
-                qcodes[h, hp] = keep.tile([P, 1024], U32, name="qc_%d%d" % (h, hp), align_bytes=64)
-                qscales[h, hp] = keep.tile([P, 1024], U8, name="qs_%d%d" % (h, hp), align_bytes=64)
+                rl_codes[h, hp] = keep.tile([P, 1024], U32, name="rl_codes_%d%d" % (h, hp), align_bytes=64)
+                rl_scales[h, hp] = keep.tile([P, 1024], U8, name="rl_scales_%d%d" % (h, hp), align_bytes=64)
+        plain = keep.tile([P, 4, 512], F32, name="plain")
 
-        def mm1(h, s):
-            bank = new_bank()
-            abank[h, s] = bank
+        def matmul_a(h, s):
+            a_bank[h, s] = new_bank()
+            passes = [(left, right, k) for left, right in (("g", "x"), ("minus_x", "g")) for k in range(2)]
             for t in range(4):
-                k = 4 * h + t
-                step = 0
-                for a, b in (("g", "x"), ("n", "g")):
-                    for gi in range(2):
-                        nc.tensor.matmul_mx(
-                            out=bank[:, 128 * t : 128 * t + 128],
-                            lhsT=codes[a, k, gi],
-                            lhsT_scale=scales[a, k, gi],
-                            rhs=codes[b, s, gi],
-                            rhs_scale=scales[b, s, gi],
-                            start=(step == 0),
-                            stop=(step == 3),
-                        )
-                        step += 1
+                for step, (left, right, k) in enumerate(passes):
+                    nc.tensor.matmul_mx(
+                        out=a_bank[h, s][:, 128 * t : 128 * t + 128],
+                        lhsT=codes[left, 4 * h + t, k],
+                        lhsT_scale=scales[left, 4 * h + t, k],
+                        rhs=codes[right, s, k],
+                        rhs_scale=scales[right, s, k],
+                        start=(step == 0),
+                        stop=(step == 3),
+                    )
 
-        def bf_tile(o, h, hp):
-            if hp == 0:
-                if (h, 0) not in bf:
-                    bf[h, 0] = keep.tile([P, 2, 512, 4], BF16, name="bf_rl", tag="slot_%d0" % h, align_bytes=64)
-                lo = 1 if o == "l" else 0
-                return bf[h, 0][:, lo : lo + len(o), :, :]
-            if (o, h) not in bf:
-                bf[o, h] = keep.tile([P, 1, 512, 4], BF16, name="bf_" + o, tag={("r", 0): "r0", ("r", 1): "r1", ("l", 1): "l02"}[o, h], align_bytes=64)
-            return bf[o, h][:]
+        def copy_plain(s):
+            nc.scalar.copy(out=plain[:, s, :], in_=a_bank[1, s][:])
 
-        def l_pair(h, sp):
-            if h == 0 and sp >= 2:
-                if ("l", 0, sp) not in bf:
-                    bf["l", 0, sp] = keep.tile([P, 256, 4], BF16, name="bf_l0", tag=("l02", "l02")[sp - 2], align_bytes=64)
-                return bf["l", 0, sp][:]
-            return bf_tile("l", h, sp // 2)[:, 0, 256 * (sp % 2) : 256 * (sp % 2) + 256, :]
+        def mirror_a(s):
+            a_bank[0, s] = new_bank()
+            for t in range(4):
+                col = 128 * (s - 4)
+                nc.tensor.transpose(a_bank[0, s][:, 128 * t : 128 * t + 128], plain[:, t, col : col + 128], ident[:])
 
-        def vector_out(o, h, s):
-            col = 128 * (s % 4)
-            if (o, h) == ("l", 0) and s >= 4:
-                nc.vector.tensor_tensor(
-                    out=l_pair(0, s // 2)[:, col % 256 : col % 256 + 128, :],
-                    in0=abank[h, s][:].rearrange("p (t n) -> p n t", t=4),
-                    in1=factor(h, s)[:, 1, :].unsqueeze(1).to_broadcast([P, 128, 4]),
-                    op=ALU.mult,
-                )
-                return
-            lo, n = {"r": 0, "l": 1, "rl": 0}[o], len(o)
+        def rl_tile(h):
+            return slot_tile(("rl", h), [P, 2, 512, 4], BF16)
+
+        def r_tile(h):
+            return slot_tile(("r", h), [P, 512, 4], BF16)
+
+        def l_tile(h, sp):
+            if sp < 2:
+                return rl_tile(h)[:, 1, 256 * sp : 256 * sp + 256, :]
+            if h == 1:
+                return slot_tile(("l", 1), [P, 512, 4], BF16)[:, 256 * (sp - 2) : 256 * (sp - 1), :]
+            return slot_tile(("l", 0, sp), [P, 256, 4], BF16)[:]
+
+        def scale_interleaved(out, h, s, first, count):
             nc.vector.tensor_tensor(
-                out=bf_tile(o, h, s // 4)[:, :, col : col + 128, :],
-                in0=abank[h, s][:].rearrange("p (t n) -> p n t", t=4).unsqueeze(1).to_broadcast([P, n, 128, 4]),
-                in1=factor(h, s)[:, lo : lo + n, :].unsqueeze(2).to_broadcast([P, n, 128, 4]),
+                out=out,
+                in0=a_bank[h, s][:].rearrange("p (t n) -> p n t", t=4).unsqueeze(1).to_broadcast([P, count, 128, 4]),
+                in1=factor(h, s)[:, first : first + count, :].unsqueeze(2).to_broadcast([P, count, 128, 4]),
                 op=ALU.mult,
             )
 
-        def l_scale(h, s):
+        def vector_r(h, s):
+            tile = rl_tile(h)[:, 0, :, :] if s < 4 else r_tile(h)[:]
+            scale_interleaved(tile[:, 128 * (s % 4) : 128 * (s % 4) + 128, :].unsqueeze(1), h, s, 0, 1)
+
+        def vector_l(h, s):
+            scale_interleaved(l_tile(h, s // 2)[:, 128 * (s % 2) : 128 * (s % 2) + 128, :].unsqueeze(1), h, s, 1, 1)
+
+        def vector_rl(h, s):
+            scale_interleaved(rl_tile(h)[:, :, 128 * s : 128 * s + 128, :], h, s, 0, 2)
+
+        def scale_rows(tile, h, s, row):
+            col = 128 * (s % 2)
+            for t in range(4):
+                nc.scalar.activation(
+                    out=tile[:, t, col : col + 128],
+                    in_=a_bank[h, s][:, 128 * t : 128 * t + 128],
+                    func=COPY,
+                    scale=factor(h, s)[:, row, t : t + 1],
+                )
+
+        def scalar_l(h, s):
             if s % 2 == 0:
-                stage[h, s // 2] = work.tile([P, 4, 256], BF16, name="stage_l", align_bytes=64, bufs=3)
-            col = 128 * (s % 2)
-            for t in range(4):
-                nc.scalar.activation(
-                    out=stage[h, s // 2][:, t, col : col + 128],
-                    in_=abank[h, s][:, 128 * t : 128 * t + 128],
-                    func=ACT.Copy,
-                    scale=factor(h, s)[:, 1, t : t + 1],
-                )
+                l_rows[h, s // 2] = work.tile([P, 4, 256], BF16, name="l_rows", align_bytes=64, bufs=L_ROWS_BUFS)
+            scale_rows(l_rows[h, s // 2], h, s, 1)
 
-        def l_interleave(h, sp, engine):
-            out = l_pair(h, sp)
-            in_ = stage[h, sp][:].rearrange("p t n -> p n t")
-            if engine == "S":
-                nc.scalar.copy(out=out, in_=in_)
-            else:
-                nc.gpsimd.tensor_scalar(out=out, in0=in_, scalar1=1.0, scalar2=0.0, op0=ALU.mult, op1=ALU.add)
+        def scalar_eta(h, s):
+            scale_rows(eta_a[h, s // 2], h, s, 2)
 
-        def e_out(h, s):
-            col = 128 * (s % 2)
-            for t in range(4):
-                nc.scalar.activation(
-                    out=ea[h, s // 2][:, t, col : col + 128],
-                    in_=abank[h, s][:, 128 * t : 128 * t + 128],
-                    func=ACT.Copy,
-                    scale=factor(h, s)[:, 2, t : t + 1],
-                )
+        def gpsimd_move(out, in_, scale=1.0):
+            nc.gpsimd.tensor_scalar(out=out, in0=in_, scalar1=scale, scalar2=0.0, op0=ALU.mult, op1=ALU.add)
 
-        low = {}
-        plain = keep.tile([P, 4, 512], F32, name="plain")
+        def gpsimd_l(h, sp):
+            gpsimd_move(l_tile(h, sp), l_rows[h, sp][:].rearrange("p t n -> p n t"))
 
-        def a_out(h, s):
-            nc.scalar.copy(out=plain[:, s, :], in_=abank[h, s][:])
+        def eta_plain(t):
+            return slot_tile(("eta_a", t // 2), [P, 2, 512], F32)[:, t % 2, :]
 
-        def mirror(s):
-            bank = new_bank()
-            abank[0, s] = bank
-            for t in range(4):
-                col = 128 * (s - 4)
-                nc.tensor.transpose(bank[:, 128 * t : 128 * t + 128], plain[:, t, col : col + 128], ident[:])
-
-        def e_scale(t):
-            if t % 2 == 0:
-                low[t // 2] = keep.tile([P, 2, 512], F32, name="ea_low", tag=("low0", "slot_10")[t // 2], align_bytes=64)
-            nc.gpsimd.tensor_scalar(
-                out=low[t // 2][:, t % 2, :].rearrange("p (s n) -> p s n", s=4),
-                in0=plain[:, :, 128 * t : 128 * t + 128],
-                scalar1=factor(1, 0)[:, 2, t : t + 1],
-                scalar2=0.0,
-                op0=ALU.mult,
-                op1=ALU.add,
+        def gpsimd_eta(t):
+            gpsimd_move(
+                eta_plain(t).rearrange("p (s n) -> p s n", s=4),
+                plain[:, :, 128 * t : 128 * t + 128],
+                factor(1, 0)[:, 2, t : t + 1],
             )
 
-        def ea_row(h, sp, t):
-            if h == 1 and sp < 2:
-                return low[t // 2][:, t % 2, 256 * sp : 256 * sp + 256]
-            return ea[h, sp][:, t, :]
+        def quantize_rl(in_, h, hp, lo, hi):
+            nc.vector.quantize_mx(out=rl_codes[h, hp][:, lo:hi].bitcast(FP8X4), scales=rl_scales[h, hp][:, lo:hi], in_=in_)
 
-        def quantize_rl(h, hp, lo, hi):
-            o = "r" if lo < 512 else "l"
-            first = lo % 512
-            if hp == 0:
-                nc.vector.quantize_mx(
-                    out=qcodes[h, hp][:, lo:hi].bitcast(FP8X4),
-                    scales=qscales[h, hp][:, lo:hi],
-                    in_=bf_tile("rl", h, 0).rearrange("p o n t -> p (o n t)")[:, 4 * lo : 4 * hi],
-                )
-                return
-            nc.vector.quantize_mx(
-                out=qcodes[h, hp][:, lo:hi].bitcast(FP8X4),
-                scales=qscales[h, hp][:, lo:hi],
-                in_=(l_pair(0, 2 + first // 256) if (o, h, hp) == ("l", 0, 1) else bf_tile(o, h, hp)[:, 0, first : first + hi - lo, :]).rearrange("p n t -> p (n t)"),
-            )
+        def quantize_low(h, lo, hi):
+            quantize_rl(rl_tile(h)[:].rearrange("p o n t -> p (o n t)")[:, 4 * lo : 4 * hi], h, 0, lo, hi)
 
-        qbank, out_t, il, osb, obank = {}, {}, {}, {}, {}
-        oscale = keep.tile([P, N], U8, name="oscale", align_bytes=64)
+        def quantize_r(h):
+            quantize_rl(r_tile(h)[:].rearrange("p n t -> p (n t)"), h, 1, 0, 512)
 
-        def mm2(h, sp, tp):
-            bank = new_bank()
-            qbank[h, sp, tp] = bank
-            for u in range(2):
-                cols = slice(256 * tp + 128 * u, 256 * tp + 128 * u + 128)
-                rows = slice(512 + 256 * (sp % 2), 768 + 256 * (sp % 2))
+        def quantize_l_pair(sp):
+            quantize_rl(l_tile(0, sp).rearrange("p n t -> p (n t)"), 0, 1, 256 * sp, 256 * sp + 256)
+
+        def quantize_l_half():
+            quantize_rl(shared["l", 1][:].rearrange("p n t -> p (n t)"), 1, 1, 512, 1024)
+
+        q_bank, out_t, out_bank = {}, {}, {}
+        out_scales = keep.tile([P, N], U8, name="out_scales", align_bytes=64)
+        out_rows = out_0.rearrange("(hp u m a) j -> hp u m a j", hp=2, u=2, a=4)
+
+        def matmul_q(h, sp):
+            rows = slice(512 + 256 * (sp % 2), 768 + 256 * (sp % 2))
+            for t in range(4):
+                if t % 2 == 0:
+                    q_bank[h, sp, t // 2] = new_bank()
+                cols = slice(128 * t, 128 * t + 128)
                 for k in range(2):
                     nc.tensor.matmul_mx(
-                        out=bank[:, 256 * u : 256 * u + 256],
-                        lhsT=qcodes[k, h][:, cols].bitcast(FP8X4),
-                        lhsT_scale=qscales[k, h][:, cols],
-                        rhs=qcodes[k, sp // 2][:, rows].bitcast(FP8X4),
-                        rhs_scale=qscales[k, sp // 2][:, rows],
+                        out=q_bank[h, sp, t // 2][:, 256 * (t % 2) : 256 * (t % 2) + 256],
+                        lhsT=rl_codes[k, h][:, cols].bitcast(FP8X4),
+                        lhsT_scale=rl_scales[k, h][:, cols],
+                        rhs=rl_codes[k, sp // 2][:, rows].bitcast(FP8X4),
+                        rhs_scale=rl_scales[k, sp // 2][:, rows],
                         start=(k == 0),
                         stop=(k == 1),
                     )
 
-        def combine(h, sp, tp):
-            if tp == 0:
-                out_t[h, sp] = work.tile([P, 4, 256], F32, name="out_t", align_bytes=64, bufs=7)
-            for u in range(2):
-                t = 2 * tp + u
+        def combine(h, sp, lanes=range(4)):
+            if (h, sp) not in out_t:
+                out_t[h, sp] = work.tile([P, 4, 256], F32, name="out_t", align_bytes=64, bufs=OUT_T_BUFS)
+            for t in lanes:
+                first = eta_plain(t)[:, 256 * sp : 256 * sp + 256] if h == 1 and sp < 2 else eta_a[h, sp][:, t, :]
                 nc.vector.scalar_tensor_tensor(
                     out=out_t[h, sp][:, t, :].rearrange("p (m a) -> p m a", a=2),
-                    in0=qbank[h, sp, tp][:, 256 * u : 256 * u + 256].rearrange("p (a m) -> p m a", a=2),
-                    scalar=fac["h"][:, 4 * h + t : 4 * h + t + 1],
-                    in1=ea_row(h, sp, t).rearrange("p (a m) -> p m a", a=2),
+                    in0=q_bank[h, sp, t // 2][:, 256 * (t % 2) : 256 * (t % 2) + 256].rearrange("p (a m) -> p m a", a=2),
+                    scalar=q_factor[:, 4 * h + t : 4 * h + t + 1],
+                    in1=first.rearrange("p (a m) -> p m a", a=2),
                     op0=ALU.mult,
                     op1=ALU.add,
                 )
 
-        def interleave_out(h, sp, engine, rows=slice(0, P)):
-            if (h, sp // 2) not in il:
-                il[h, sp // 2] = keep.tile([P, 2048], BF16, name="il", tag={(0, 0): "r1", (1, 0): "r1", (0, 1): "slot_00", (1, 1): "r0"}[h, sp // 2], align_bytes=64)
+        def planes_tile(h, hp):
+            return slot_tile(("planes", h, hp), [P, 2048], BF16)
+
+        def interleave_out(h, sp, engine):
             lo = 2 * (sp % 2)
-            out = il[h, sp // 2][:].rearrange("p (m a t) -> p m a t", a=4, t=4)[:, rows, lo : lo + 2, :]
-            in_ = out_t[h, sp][:].rearrange("p t (m a) -> p m a t", a=2)[:, rows, :, :]
-            if engine == "V":
-                nc.vector.tensor_copy(out=out.rearrange("p m a t -> p m t a"), in_=in_.rearrange("p m a t -> p m t a"))
-            elif engine == "S":
-                nc.scalar.copy(out=out.rearrange("p m a t -> p m t a"), in_=in_.rearrange("p m a t -> p m t a"))
+            out = planes_tile(h, sp // 2)[:].rearrange("p (m a t) -> p m t a", a=4, t=4)[:, :, :, lo : lo + 2]
+            in_ = out_t[h, sp][:].rearrange("p t (m a) -> p m t a", a=2)
+            if engine is nc.vector:
+                nc.vector.tensor_copy(out=out, in_=in_)
+            elif engine is nc.scalar:
+                nc.scalar.copy(out=out, in_=in_)
             else:
-                nc.gpsimd.tensor_scalar(out=out, in0=in_, scalar1=1.0, scalar2=0.0, op0=ALU.mult, op1=ALU.add)
+                gpsimd_move(out.rearrange("p m t a -> p m a t"), in_.rearrange("p m t a -> p m a t"))
 
         def quantize_out(h, hp):
-            oc = keep.tile([P, 512], U32, name="oc_%d%d" % (h, hp), align_bytes=64)
+            words = keep.tile([P, 512], U32, name="out_codes_%d%d" % (h, hp), align_bytes=64)
             cols = slice(512 * hp, 512 * hp + 512)
-            nc.vector.quantize_mx(out=oc[:].bitcast(FP8X4), scales=oscale[4 * h : P, cols], in_=il[h, hp][:])
-            nc.sync.dma_start(
-                out=out_1[h, :, cols, :].rearrange("p m b -> p (m b)").bitcast(I32), in_=oc[:].bitcast(I32)
-            )
-            if (h, hp) == (1, 1):
-                for quad in range(4):
-                    nc.scalar.dma_start(
-                        out=out_2[:, 4 * quad : 4 * quad + 4, :].bitcast(I32),
-                        in_=oscale[32 * quad : 32 * quad + 8, :].bitcast(I32),
-                    )
+            nc.vector.quantize_mx(out=words[:].bitcast(FP8X4), scales=out_scales[4 * h : P, cols], in_=planes_tile(h, hp)[:])
+            nc.sync.dma_start(out=out_1[h, :, cols, :].rearrange("p m b -> p (m b)").bitcast(I32), in_=words[:].bitcast(I32))
 
-        out_rows = out_0.rearrange("(h u m a) j -> h u m a j", h=2, u=2, a=4)
+        def store_scales():
+            for quad in range(4):
+                nc.scalar.dma_start(
+                    out=out_2[:, 4 * quad : 4 * quad + 4, :].bitcast(I32),
+                    in_=out_scales[32 * quad : 32 * quad + 8, :].bitcast(I32),
+                )
 
         def transpose_out(h, sp):
-            for a in range(2):
-                bank = new_bank()
-                obank[h, sp, a] = bank
+            for u in range(2):
+                out_bank[h, sp, u] = new_bank()
                 for t in range(4):
-                    nc.tensor.transpose(bank[:, 128 * t : 128 * t + 128], out_t[h, sp][:, t, 128 * a : 128 * a + 128], ident[:])
+                    nc.tensor.transpose(
+                        out_bank[h, sp, u][:, 128 * t : 128 * t + 128], out_t[h, sp][:, t, 128 * u : 128 * u + 128], ident[:]
+                    )
 
-        def copy_out(h, sp, engines="SS"):
-            osb[h, sp] = work.tile([P, 2, 512], F32, name="osb", align_bytes=64, bufs=4)
-            for a in range(2):
-                out = osb[h, sp][:, a, :].rearrange("m (p t) -> m p t", t=4)
-                in_ = obank[h, sp, a][:].rearrange("m (t p) -> m p t", t=4)
-                if engines[a] == "S":
-                    nc.scalar.copy(out=out, in_=in_)
-                else:
-                    nc.vector.tensor_copy(out=out, in_=in_)
-                lo = 2 * (sp % 2)
-                nc.sync.dma_start(out=out_rows[sp // 2, a, :, lo : lo + 2, 512 * h : 512 * h + 512], in_=osb[h, sp][:, a, :])
+        def store_out(h, sp):
+            rows = work.tile([P, 2, 512], F32, name="rows", align_bytes=64, bufs=ROWS_BUFS)
+            lo = 2 * (sp % 2)
+            for u in range(2):
+                nc.scalar.copy(
+                    out=rows[:, u, :].rearrange("m (p t) -> m p t", t=4),
+                    in_=out_bank[h, sp, u][:].rearrange("m (t p) -> m p t", t=4),
+                )
+                nc.sync.dma_start(out=out_rows[sp // 2, u, :, lo : lo + 2, 512 * h : 512 * h + 512], in_=rows[:, u, :])
 
-        groups = [(i,) for i in range(8)]
-
-        def mm2_unit(h, sp):
-            for tp in range(2):
-                mm2(h, sp, tp)
-
-        def combine_unit(h, sp):
-            for tp in range(2):
-                combine(h, sp, tp)
-
-        for j, grp in enumerate(groups):
-            transpose_in("g", grp, j)
-            quantize_in("g", grp)
-            if j > 0:
-                quantize_in("x", groups[j - 1])
-            transpose_in("x", grp, j)
-            negate(grp)
-        mm1(0, 0)
+        for s in range(8):
+            transpose_in("g", s)
+            quantize_in("g", s)
+            if s > 0:
+                quantize_in("x", s - 1)
+            transpose_in("x", s)
+            negate(s)
+        matmul_a(0, 0)
         make_factors()
-        quantize_in("x", groups[-1])
-        mm1(0, 1)
-        mm1(0, 2)
-        mm1(1, 0)
-        mm1(1, 1)
-        mm1(1, 2)
-        mm1(1, 3)
-        mm1(0, 3)
-        l_scale(0, 0)
-        e_out(0, 0)
-        vector_out("r", 0, 1)
-        vector_out("r", 0, 0)
-        l_scale(0, 1)
-        l_interleave(0, 0, "G")
-        e_out(0, 1)
-        mm1(1, 4)
-        vector_out("rl", 0, 2)
-        e_out(0, 2)
-        vector_out("r", 1, 0)
-        a_out(1, 0)
-        l_scale(1, 0)
-        vector_out("r", 1, 1)
-        quantize_rl(0, 0, 0, 256)
-        quantize_rl(0, 0, 512, 768)
-        quantize_rl(1, 0, 0, 256)
-        a_out(1, 1)
-        l_scale(1, 1)
-        l_interleave(1, 0, "G")
-        vector_out("rl", 1, 2)
-        a_out(1, 2)
-        vector_out("rl", 1, 3)
-        a_out(1, 3)
-        mirror(4)
-        mirror(5)
-        mirror(6)
-        mirror(7)
-        e_scale(0)
-        e_scale(1)
-        vector_out("rl", 0, 3)
-        e_out(0, 3)
-        mm1(1, 5)
-        mm1(1, 6)
-        vector_out("r", 1, 4)
-        vector_out("r", 0, 4)
-        vector_out("r", 0, 5)
-        quantize_rl(0, 0, 256, 512)
-        quantize_rl(0, 0, 768, 1024)
-        quantize_rl(1, 0, 768, 1024)
-        quantize_rl(1, 0, 256, 768)
-        e_scale(2)
-        e_scale(3)
-        l_scale(1, 4)
-        e_out(1, 4)
-        mm1(1, 7)
-        l_scale(0, 4)
-        e_out(0, 4)
-        mm2_unit(0, 0)
-        l_scale(0, 5)
-        l_interleave(0, 2, "G")
-        e_out(0, 5)
-        vector_out("r", 0, 6)
-        vector_out("r", 0, 7)
-        vector_out("r", 1, 5)
-        vector_out("r", 1, 6)
-        vector_out("r", 1, 7)
-        l_scale(1, 5)
-        e_out(1, 5)
-        mm2_unit(0, 1)
-        combine(0, 0, 0)
-        quantize_rl(0, 1, 0, 512)
-        quantize_rl(1, 1, 0, 512)
-        quantize_rl(0, 1, 512, 768)
-        l_interleave(1, 2, "G")
-        mm2_unit(1, 0)
-        l_scale(0, 6)
-        e_out(0, 6)
-        l_scale(0, 7)
-        e_out(0, 7)
-        combine(0, 0, 1)
-        interleave_out(0, 0, "S")
+        quantize_in("x", 7)
+
+        for h, s in ((0, 1), (0, 2), (1, 0), (1, 1), (1, 2), (1, 3), (0, 3)):
+            matmul_a(h, s)
+        scalar_l(0, 0)
+        scalar_eta(0, 0)
+        vector_r(0, 1)
+        vector_r(0, 0)
+        scalar_l(0, 1)
+        gpsimd_l(0, 0)
+        scalar_eta(0, 1)
+        matmul_a(1, 4)
+        vector_rl(0, 2)
+        scalar_eta(0, 2)
+        for s in range(2):
+            vector_r(1, s)
+            copy_plain(s)
+            scalar_l(1, s)
+        quantize_low(0, 0, 256)
+        quantize_low(0, 512, 768)
+        quantize_low(1, 0, 256)
+        gpsimd_l(1, 0)
+        for s in range(2, 4):
+            vector_rl(1, s)
+            copy_plain(s)
+        for s in range(4, 8):
+            mirror_a(s)
+        gpsimd_eta(0)
+        gpsimd_eta(1)
+        vector_rl(0, 3)
+        scalar_eta(0, 3)
+        matmul_a(1, 5)
+        matmul_a(1, 6)
+
+        for h, s in ((1, 4), (0, 4), (0, 5)):
+            vector_r(h, s)
+        quantize_low(0, 256, 512)
+        quantize_low(0, 768, 1024)
+        quantize_low(1, 768, 1024)
+        quantize_low(1, 256, 768)
+        gpsimd_eta(2)
+        gpsimd_eta(3)
+        for h in (1, 0):
+            scalar_l(h, 4)
+            scalar_eta(h, 4)
+        matmul_a(1, 7)
+        matmul_q(0, 0)
+        scalar_l(0, 5)
+        gpsimd_l(0, 2)
+        scalar_eta(0, 5)
+        for h, s in ((0, 6), (0, 7), (1, 5), (1, 6), (1, 7)):
+            vector_r(h, s)
+        scalar_l(1, 5)
+        scalar_eta(1, 5)
+        matmul_q(0, 1)
+        combine(0, 0, (0, 1))
+        quantize_r(0)
+        quantize_r(1)
+        quantize_l_pair(2)
+        gpsimd_l(1, 2)
+        matmul_q(1, 0)
+        for s in (6, 7):
+            scalar_l(0, s)
+            scalar_eta(0, s)
+        combine(0, 0, (2, 3))
+
+        interleave_out(0, 0, nc.scalar)
         transpose_out(0, 0)
-        copy_out(0, 0)
-        combine_unit(0, 1)
-        mm2_unit(1, 1)
+        store_out(0, 0)
+        combine(0, 1)
+        matmul_q(1, 1)
         transpose_out(0, 1)
-        vector_out("l", 1, 6)
-        vector_out("l", 1, 7)
-        e_out(1, 6)
-        e_out(1, 7)
-        quantize_rl(1, 1, 512, 1024)
-        l_interleave(0, 3, "G")
-        mm2_unit(0, 2)
-        interleave_out(0, 1, "S")
-        copy_out(0, 1)
-        combine_unit(1, 0)
+        for s in (6, 7):
+            vector_l(1, s)
+            scalar_eta(1, s)
+        quantize_l_half()
+        gpsimd_l(0, 3)
+        matmul_q(0, 2)
+        interleave_out(0, 1, nc.scalar)
+        store_out(0, 1)
+        combine(1, 0)
         transpose_out(1, 0)
-        mm2_unit(1, 2)
-        copy_out(1, 0)
-        combine_unit(1, 1)
-        quantize_rl(0, 1, 768, 1024)
+        matmul_q(1, 2)
+        store_out(1, 0)
+        combine(1, 1)
+        quantize_l_pair(3)
         quantize_out(0, 0)
-        interleave_out(1, 0, "G")
-        interleave_out(1, 1, "G")
+
+        for sp in range(2):
+            interleave_out(1, sp, nc.gpsimd)
         transpose_out(1, 1)
-        mm2_unit(0, 3)
-        copy_out(1, 1)
-        combine_unit(0, 2)
+        matmul_q(0, 3)
+        store_out(1, 1)
+        combine(0, 2)
         transpose_out(0, 2)
-        interleave_out(0, 2, "S")
-        copy_out(0, 2)
-        combine_unit(1, 2)
+        interleave_out(0, 2, nc.scalar)
+        store_out(0, 2)
+        combine(1, 2)
         transpose_out(1, 2)
-        mm2_unit(1, 3)
-        combine_unit(0, 3)
-        copy_out(1, 2)
+        matmul_q(1, 3)
+        combine(0, 3)
+        store_out(1, 2)
         transpose_out(0, 3)
-        combine_unit(1, 3)
+        combine(1, 3)
         quantize_out(1, 0)
         transpose_out(1, 3)
-        copy_out(0, 3)
-        copy_out(1, 3, engines="SS")
-        interleave_out(0, 3, "V")
-        interleave_out(1, 2, "V")
+        for h in range(2):
+            store_out(h, 3)
+        interleave_out(0, 3, nc.vector)
+        interleave_out(1, 2, nc.vector)
         quantize_out(0, 1)
-        interleave_out(1, 3, "V")
+        interleave_out(1, 3, nc.vector)
         quantize_out(1, 1)
+        store_scales()

@@ -424,9 +424,9 @@ def tile_skewgradientquadraticstep_kernel(tc, x, g, c, d, eta, out_0, out_1, out
         transpose_out(1, 3)
         for h in range(2):
             store_out(h, 3)
-        interleave_out(0, 3, nc.vector)
-        interleave_out(1, 2, nc.vector)
+        interleave_out(0, 3, nc.gpsimd)
+        interleave_out(1, 2, nc.gpsimd)
+        interleave_out(1, 3, nc.gpsimd)
         quantize_out(0, 1)
-        interleave_out(1, 3, nc.vector)
         quantize_out(1, 1)
         store_scales()

@@ -18,19 +18,26 @@ P = 128
 FLOPS = 2 * 2 * N * N * N
 RSQRT2 = 1.0 / math.sqrt(2.0)
 PSUM_BANKS = 8
-TURNED_BUFS = 3
-L_ROWS_BUFS = 3
-OUT_T_BUFS = 7
-ROWS_BUFS = 4
+L_ROWS_BUFS = 4
 Q_SCALE = 0.5 / 32.0
 
 SLOT = {
-    ("rl", 0): "a", ("planes", 0, 1): "a",
-    ("rl", 1): "b", ("eta_a", 1): "b",
-    ("r", 0): "c", ("planes", 1, 1): "c",
-    ("r", 1): "d", ("planes", 0, 0): "d", ("planes", 1, 0): "d",
-    ("l", 0, 2): "e", ("l", 1): "e", ("l", 0, 3): "e",
-    ("eta_a", 0): "f",
+    ("minus", 0): "m0",
+    ("minus", 1): "m1",
+    ("minus", 2): "m0",
+    ("minus", 3): "m1",
+    ("rl", 0, 0): "a",
+    ("rl", 1, 0): "b",
+    ("r", 0): "c",
+    ("l", 0): "f",
+    ("r", 1): "d",
+    ("l", 1): "d",
+    ("eta", 0): "h",
+    ("eta", 1): "i",
+    ("planes", 0, 0): "m0",
+    ("planes", 1, 0): "g",
+    ("planes", 0, 1): "a",
+    ("planes", 1, 1): "b",
 }
 
 
@@ -56,7 +63,7 @@ def tile_skewgradientquadraticstep_kernel(tc, x, g, c, d, eta, out_0, out_1, out
         raw = {}
         for s in range(8):
             for op in ("g", "x"):
-                raw[op, s] = keep.tile([P, N], BF16, name="raw_%s%d" % (op, s))
+                raw[op, s] = keep.tile([P, N], BF16, name="raw", tag="rows_%s%d" % (op, s), align_bytes=64)
                 nc.sync.dma_start(out=raw[op, s][:], in_=src[op][s // 4, s % 4])
         vecs = keep.tile([P, 3, 16], BF16, name="vecs")
         for v, vec in enumerate((c, d, eta)):
@@ -69,19 +76,19 @@ def tile_skewgradientquadraticstep_kernel(tc, x, g, c, d, eta, out_0, out_1, out
         row_factor = keep.tile([P, 6, 8], F32, name="row_factor")
         q_factor = keep.tile([P, 8], F32, name="q_factor")
 
-        def make_factors():
+        def make_row_factors():
             for rows, first, last, sign in ((slice(1, 6, 2), 0, 3, -1.0), (slice(0, 3, 2), 1, 3, 1.0), (slice(4, 5), 0, 1, 1.0)):
-                nc.vector.tensor_scalar(
-                    out=row_factor[:, rows, :], in0=vecs[:, first:last, 0:8], scalar1=sign * RSQRT2, scalar2=None, op0=ALU.mult
-                )
+                nc.scalar.activation(out=row_factor[:, rows, :], in_=vecs[:, first:last, 0:8], func=COPY, scale=sign * RSQRT2)
+
+        def make_q_factor():
             nc.vector.scalar_tensor_tensor(
                 out=q_factor[:], in0=vecs[:, 2, 0:8], scalar=Q_SCALE, in1=vecs[:, 2, 0:8], op0=ALU.mult, op1=ALU.mult
             )
 
         def factor(h, s):
-            return row_factor[:, 3:6, 0:4] if h == 0 and s >= 4 else row_factor[:, 0:3, 4 * h : 4 * h + 4]
+            return row_factor[:, 3:6, 4:8] if h == 1 and s < 4 else row_factor[:, 0:3, 4 * h : 4 * h + 4]
 
-        codes, scales, turned = {}, {}, {}
+        codes, scales, turned, minus, in_bank = {}, {}, {}, {}, {}
 
         def transpose_in(op, s):
             words = raw[op, s][:].bitcast(F32)
@@ -90,43 +97,71 @@ def tile_skewgradientquadraticstep_kernel(tc, x, g, c, d, eta, out_0, out_1, out
                 for u in range(2):
                     lo = 128 * (2 * h + u)
                     nc.tensor.transpose(bank[:, lo : lo + 128], words[:, 256 * h + u : 256 * h + 256 : 2], ident[:])
-            width = 2 * N if op == "x" else N
-            turned[op, s] = work.tile([P, width], BF16, name="turned_" + op, align_bytes=64, bufs=TURNED_BUFS)
+            in_bank[op, s] = bank
+
+        def copy_in(op, s):
+            bank = in_bank[op, s]
+            if s // 2 not in turned:
+                turned[s // 2] = keep.tile([P, 4 * N], BF16, name="turned", tag="wide_%d" % (s // 2), align_bytes=64)
+            lo = N * (2 * (s % 2) + (op == "x"))
             nc.scalar.copy(
-                out=turned[op, s][:, 0:N].bitcast(F32).rearrange("p (h m u) -> p h m u", h=2, u=2),
+                out=turned[s // 2][:, lo : lo + N].bitcast(F32).rearrange("p (h m u) -> p h m u", h=2, u=2),
                 in_=bank[:].rearrange("p (h u m) -> p h m u", h=2, u=2),
             )
 
-        def negate(s):
-            nc.vector.tensor_scalar(
-                out=turned["x", s][:, N : 2 * N], in0=turned["x", s][:, 0:N], scalar1=-1.0, scalar2=None, op0=ALU.mult
-            )
-
-        def quantize_in(op, s):
-            names = ("x", "minus_x") if op == "x" else ("g",)
-            words = keep.tile([P, 256 * len(names)], U32, name="codes_%s%d" % (op, s), align_bytes=64)
-            plane = keep.tile([P, 256 * len(names)], U8, name="scales_%s%d" % (op, s), align_bytes=64)
-            nc.vector.quantize_mx(out=words[:].bitcast(FP8X4), scales=plane[:], in_=turned[op, s][:])
-            for pos, name in enumerate(names):
+        def quantize_operands(in_, names):
+            label = "%s%d" % names[0]
+            words = keep.tile([P, 256 * len(names)], U32, name="codes_" + label, align_bytes=64)
+            plane = keep.tile([P, 256 * len(names)], U8, name="scales_" + label, align_bytes=64)
+            nc.vector.quantize_mx(out=words[:].bitcast(FP8X4), scales=plane[:], in_=in_)
+            for pos, (name, s) in enumerate(names):
                 for h in range(2):
                     lo = 256 * pos + 128 * h
                     codes[name, s, h] = words[:, lo : lo + 128].bitcast(FP8X4)
                     scales[name, s, h] = plane[:, lo : lo + 128]
 
+        def quantize_in(s):
+            lo = 2 * N * (s % 2)
+            quantize_operands(turned[s // 2][:, lo : lo + 2 * N], (("g", s), ("x", s)))
+
+        def quantize_one(op, s):
+            lo = N * (2 * (s % 2) + (op == "x"))
+            quantize_operands(turned[s // 2][:, lo : lo + N], ((op, s),))
+
+        def negate(sp):
+            minus[sp] = slot_tile(("minus", sp), [P, 2 * N], BF16)
+            nc.vector.tensor_scalar(
+                out=minus[sp][:].rearrange("p (j k) -> p j k", j=2),
+                in0=turned[sp][:].rearrange("p (j o k) -> p j o k", j=2, o=2)[:, :, 1, :],
+                scalar1=-1.0,
+                scalar2=None,
+                op0=ALU.mult,
+            )
+
+        def quantize_minus(sp):
+            quantize_operands(minus[sp][:], (("minus_x", 2 * sp), ("minus_x", 2 * sp + 1)))
+
+        eta_wide = {}
         a_bank, l_rows, eta_a, rl_codes, rl_scales = {}, {}, {}, {}, {}
         for h in range(2):
             for sp in range(4):
-                if h == 0 or sp >= 2:
+                if sp == 2:
+                    eta_wide[h] = slot_tile(("eta", h), [P, 4, 512], F32)
+                if sp < 2:
                     eta_a[h, sp] = keep.tile([P, 4, 256], F32, name="eta_a_%d%d" % (h, sp))
+                else:
+                    eta_a[h, sp] = eta_wide[h][:, :, 256 * sp - 512 : 256 * sp - 256]
             for hp in range(2):
                 rl_codes[h, hp] = keep.tile([P, 1024], U32, name="rl_codes_%d%d" % (h, hp), align_bytes=64)
                 rl_scales[h, hp] = keep.tile([P, 1024], U8, name="rl_scales_%d%d" % (h, hp), align_bytes=64)
-        plain = keep.tile([P, 4, 512], F32, name="plain")
+        plain_of = [keep.tile([P, 4, 512], F32, name="plain_%d" % h) for h in range(2)]
+        plain = plain_of[0]
 
-        def matmul_a(h, s):
-            a_bank[h, s] = new_bank()
+        def matmul_a(h, s, lanes=range(4)):
+            if (h, s) not in a_bank:
+                a_bank[h, s] = new_bank()
             passes = [(left, right, k) for left, right in (("g", "x"), ("minus_x", "g")) for k in range(2)]
-            for t in range(4):
+            for t in lanes:
                 for step, (left, right, k) in enumerate(passes):
                     nc.tensor.matmul_mx(
                         out=a_bank[h, s][:, 128 * t : 128 * t + 128],
@@ -139,44 +174,95 @@ def tile_skewgradientquadraticstep_kernel(tc, x, g, c, d, eta, out_0, out_1, out
                     )
 
         def copy_plain(s):
-            nc.scalar.copy(out=plain[:, s, :], in_=a_bank[1, s][:])
+            nc.scalar.copy(out=plain[:, s - 4, :], in_=a_bank[0, s][:])
 
-        def mirror_a(s):
-            a_bank[0, s] = new_bank()
+        def copy_plain1(s):
+            nc.scalar.copy(out=plain_of[1][:, s - 4, :], in_=a_bank[1, s][:])
+
+        def gpsimd_l_plain(h, sp):
+            nc.gpsimd.tensor_tensor(
+                out=l_flat(h, sp).rearrange("p (j n t) -> p j n t", j=2, t=4),
+                in0=plain_of[h][:, 2 * sp - 4 : 2 * sp - 2, :].rearrange("p j (t n) -> p j n t", t=4),
+                in1=factor(h, 4)[:, 1:2, :].unsqueeze(1).to_broadcast([P, 2, 128, 4]),
+                op=ALU.mult,
+            )
+
+        def gpsimd_eta_wide(h, t):
+            gpsimd_move(
+                eta_wide[h][:, t, :].rearrange("p (s n) -> p s n", s=4),
+                plain_of[h][:, :, 128 * t : 128 * t + 128],
+                factor(h, 4)[:, 2, t : t + 1],
+            )
+
+        def scalar_eta_wide(h, t):
+            nc.scalar.activation(
+                out=eta_wide[h][:, t, :].rearrange("p (s n) -> p s n", s=4),
+                in_=plain_of[h][:, :, 128 * t : 128 * t + 128],
+                func=COPY,
+                scale=factor(h, 4)[:, 2, t : t + 1],
+            )
+
+        def mirror_a(sp):
+            for s in (2 * sp, 2 * sp + 1):
+                a_bank[1, s] = new_bank()
             for t in range(4):
-                col = 128 * (s - 4)
-                nc.tensor.transpose(a_bank[0, s][:, 128 * t : 128 * t + 128], plain[:, t, col : col + 128], ident[:])
+                for s in (2 * sp, 2 * sp + 1):
+                    nc.tensor.transpose(
+                        a_bank[1, s][:, 128 * t : 128 * t + 128], plain[:, t, 128 * s : 128 * s + 128], ident[:]
+                    )
 
-        def rl_tile(h):
-            return slot_tile(("rl", h), [P, 2, 512, 4], BF16)
+        def rl_tile(h, hp):
+            return slot_tile(("rl", h, hp), [P, 4096], BF16)
 
-        def r_tile(h):
-            return slot_tile(("r", h), [P, 512, 4], BF16)
+        def rl_part(h, hp, first, last):
+            if hp == 0:
+                return rl_tile(h, hp)[:, 1024 * first : 1024 * last]
+            if first < 2:
+                return slot_tile(("r", h), [P, 2048], BF16)[:, 1024 * first : 1024 * last]
+            if ("l", h) in SLOT:
+                return slot_tile(("l", h), [P, 2048], BF16)[:, 1024 * (first - 2) : 1024 * (last - 2)]
+            return slot_tile(("l", h, first), [P, 1024], BF16)[:]
+
+        def r_part(h, s):
+            lo = 512 * (s % 2)
+            return rl_part(h, s // 4, s % 4 // 2, s % 4 // 2 + 1)[:, lo : lo + 512].rearrange("p (n t) -> p n t", t=4)
+
+        def l_flat(h, sp):
+            return rl_part(h, sp // 2, 2 + sp % 2, 3 + sp % 2)
 
         def l_tile(h, sp):
-            if sp < 2:
-                return rl_tile(h)[:, 1, 256 * sp : 256 * sp + 256, :]
-            if h == 1:
-                return slot_tile(("l", 1), [P, 512, 4], BF16)[:, 256 * (sp - 2) : 256 * (sp - 1), :]
-            return slot_tile(("l", 0, sp), [P, 256, 4], BF16)[:]
+            return l_flat(h, sp).rearrange("p (n t) -> p n t", t=4)
 
-        def scale_interleaved(out, h, s, first, count):
+        def scale_interleaved(out, h, s, row):
             nc.vector.tensor_tensor(
                 out=out,
-                in0=a_bank[h, s][:].rearrange("p (t n) -> p n t", t=4).unsqueeze(1).to_broadcast([P, count, 128, 4]),
-                in1=factor(h, s)[:, first : first + count, :].unsqueeze(2).to_broadcast([P, count, 128, 4]),
+                in0=a_bank[h, s][:].rearrange("p (t n) -> p n t", t=4),
+                in1=factor(h, s)[:, row : row + 1, :].to_broadcast([P, 128, 4]),
                 op=ALU.mult,
             )
 
         def vector_r(h, s):
-            tile = rl_tile(h)[:, 0, :, :] if s < 4 else r_tile(h)[:]
-            scale_interleaved(tile[:, 128 * (s % 4) : 128 * (s % 4) + 128, :].unsqueeze(1), h, s, 0, 1)
+            scale_interleaved(r_part(h, s), h, s, 0)
 
         def vector_l(h, s):
-            scale_interleaved(l_tile(h, s // 2)[:, 128 * (s % 2) : 128 * (s % 2) + 128, :].unsqueeze(1), h, s, 1, 1)
+            if s < 6:
+                scale_interleaved(l_tile(h, s // 2)[:, 128 * (s % 2) : 128 * (s % 2) + 128, :], h, s, 1)
+            else:
+                nc.vector.tensor_tensor(
+                    out=l_flat(h, 3).rearrange("p (u a m t) -> p a u m t", u=2, a=2, t=4)[:, s % 2],
+                    in0=a_bank[h, s][:].rearrange("p (t u m) -> p u m t", t=4, u=2),
+                    in1=factor(h, s)[:, 1:2, :].unsqueeze(1).to_broadcast([P, 2, 64, 4]),
+                    op=ALU.mult,
+                )
 
         def vector_rl(h, s):
-            scale_interleaved(rl_tile(h)[:, :, 128 * s : 128 * s + 128, :], h, s, 0, 2)
+            lo = 512 * (s % 4)
+            nc.vector.tensor_tensor(
+                out=rl_tile(h, s // 4)[:].rearrange("p (o n t) -> p o n t", o=2, t=4)[:, :, lo // 4 : lo // 4 + 128, :],
+                in0=a_bank[h, s][:].rearrange("p (t n) -> p n t", t=4).unsqueeze(1).to_broadcast([P, 2, 128, 4]),
+                in1=factor(h, s)[:, 0:2, :].unsqueeze(2).to_broadcast([P, 2, 128, 4]),
+                op=ALU.mult,
+            )
 
         def scale_rows(tile, h, s, row):
             col = 128 * (s % 2)
@@ -189,9 +275,62 @@ def tile_skewgradientquadraticstep_kernel(tc, x, g, c, d, eta, out_0, out_1, out
                 )
 
         def scalar_l(h, s):
-            if s % 2 == 0:
+            if (h, s // 2) not in l_rows:
                 l_rows[h, s // 2] = work.tile([P, 4, 256], BF16, name="l_rows", align_bytes=64, bufs=L_ROWS_BUFS)
-            scale_rows(l_rows[h, s // 2], h, s, 1)
+            if s < 6:
+                scale_rows(l_rows[h, s // 2], h, s, 1)
+            else:
+                for t in range(4):
+                    nc.scalar.activation(
+                        out=l_rows[h, 3][:, t, :].rearrange("p (u a m) -> p a u m", u=2, a=2)[:, s % 2],
+                        in_=a_bank[h, s][:, 128 * t : 128 * t + 128].rearrange("p (u m) -> p u m", u=2),
+                        func=COPY,
+                        scale=factor(h, s)[:, 1, t : t + 1],
+                    )
+
+        def scale_plain(tile, first, count, row):
+            lo = 128 * (first % 2)
+            for t in range(4):
+                nc.scalar.activation(
+                    out=tile[:, t, lo : lo + 128 * count].rearrange("p (j n) -> p j n", j=count),
+                    in_=plain[:, first - 4 : first - 4 + count, 128 * t : 128 * t + 128],
+                    func=COPY,
+                    scale=factor(0, 4)[:, row, t : t + 1],
+                )
+
+        def scalar_l_plain(first, count):
+            if (0, first // 2) not in l_rows:
+                l_rows[0, first // 2] = work.tile([P, 4, 256], BF16, name="l_rows", align_bytes=64, bufs=L_ROWS_BUFS)
+            if first < 6:
+                scale_plain(l_rows[0, first // 2], first, count, 1)
+            else:
+                for t in range(4):
+                    nc.scalar.activation(
+                        out=l_rows[0, 3][:, t, :].rearrange("p (u a m) -> p a u m", u=2, a=2)[:, first % 2 : first % 2 + count],
+                        in_=plain[:, first - 4 : first - 4 + count, 128 * t : 128 * t + 128].rearrange("p a (u m) -> p a u m", u=2),
+                        func=COPY,
+                        scale=factor(0, 4)[:, 1, t : t + 1],
+                    )
+
+        def scalar_eta_plain(first, count):
+            scale_plain(eta_a[0, first // 2], first, count, 2)
+
+        def gpsimd_eta_pair(sp):
+            for t in range(4):
+                gpsimd_move(
+                    eta_a[0, sp][:, t, :].rearrange("p (j n) -> p j n", j=2),
+                    plain[:, 2 * sp - 4 : 2 * sp - 2, 128 * t : 128 * t + 128],
+                    factor(0, 4)[:, 2, t : t + 1],
+                )
+
+        def vector_eta(h, s):
+            col = 128 * (s % 2)
+            nc.vector.tensor_tensor(
+                out=eta_a[h, s // 2][:, :, col : col + 128],
+                in0=a_bank[h, s][:].rearrange("p (t n) -> p t n", t=4),
+                in1=factor(h, s)[:, 2, :].unsqueeze(2).to_broadcast([P, 4, 128]),
+                op=ALU.mult,
+            )
 
         def scalar_eta(h, s):
             scale_rows(eta_a[h, s // 2], h, s, 2)
@@ -209,23 +348,13 @@ def tile_skewgradientquadraticstep_kernel(tc, x, g, c, d, eta, out_0, out_1, out
             gpsimd_move(
                 eta_plain(t).rearrange("p (s n) -> p s n", s=4),
                 plain[:, :, 128 * t : 128 * t + 128],
-                factor(1, 0)[:, 2, t : t + 1],
+                factor(0, 4)[:, 2, t : t + 1],
             )
 
-        def quantize_rl(in_, h, hp, lo, hi):
-            nc.vector.quantize_mx(out=rl_codes[h, hp][:, lo:hi].bitcast(FP8X4), scales=rl_scales[h, hp][:, lo:hi], in_=in_)
-
-        def quantize_low(h, lo, hi):
-            quantize_rl(rl_tile(h)[:].rearrange("p o n t -> p (o n t)")[:, 4 * lo : 4 * hi], h, 0, lo, hi)
-
-        def quantize_r(h):
-            quantize_rl(r_tile(h)[:].rearrange("p n t -> p (n t)"), h, 1, 0, 512)
-
-        def quantize_l_pair(sp):
-            quantize_rl(l_tile(0, sp).rearrange("p n t -> p (n t)"), 0, 1, 256 * sp, 256 * sp + 256)
-
-        def quantize_l_half():
-            quantize_rl(shared["l", 1][:].rearrange("p n t -> p (n t)"), 1, 1, 512, 1024)
+        def quantize_rl(h, hp, first, last):
+            in_ = rl_part(h, hp, first, last)
+            cols = slice(256 * first, 256 * last)
+            nc.vector.quantize_mx(out=rl_codes[h, hp][:, cols].bitcast(FP8X4), scales=rl_scales[h, hp][:, cols], in_=in_)
 
         q_bank, out_t, out_bank = {}, {}, {}
         out_scales = keep.tile([P, N], U8, name="out_scales", align_bytes=64)
@@ -248,27 +377,57 @@ def tile_skewgradientquadraticstep_kernel(tc, x, g, c, d, eta, out_0, out_1, out
                         stop=(k == 1),
                     )
 
-        def combine(h, sp, lanes=range(4)):
-            if (h, sp) not in out_t:
-                out_t[h, sp] = work.tile([P, 4, 256], F32, name="out_t", align_bytes=64, bufs=OUT_T_BUFS)
-            for t in lanes:
-                first = eta_plain(t)[:, 256 * sp : 256 * sp + 256] if h == 1 and sp < 2 else eta_a[h, sp][:, t, :]
-                nc.vector.scalar_tensor_tensor(
-                    out=out_t[h, sp][:, t, :].rearrange("p (m a) -> p m a", a=2),
-                    in0=q_bank[h, sp, t // 2][:, 256 * (t % 2) : 256 * (t % 2) + 256].rearrange("p (a m) -> p m a", a=2),
-                    scalar=q_factor[:, 4 * h + t : 4 * h + t + 1],
-                    in1=first.rearrange("p (a m) -> p m a", a=2),
-                    op0=ALU.mult,
-                    op1=ALU.add,
-                )
+        def unit_t(h, sp):
+            if (h, sp // 2) not in out_t:
+                out_t[h, sp // 2] = keep.tile([P, 2048], F32, name="out_t", tag="wide_%d" % len(out_t), align_bytes=64)
+            return out_t[h, sp // 2][:, 1024 * (sp % 2) : 1024 * (sp % 2) + 1024].rearrange("p (t n) -> p t n", t=4)
+
+        def combine(h, sp, half):
+            for t in (2 * half, 2 * half + 1):
+                bank = q_bank[h, sp, t // 2][:, 256 * (t % 2) : 256 * (t % 2) + 256]
+                if sp < 3:
+                    combine_lane(h, sp, t, bank, slice(0, 128))
+                else:
+                    for u in range(2):
+                        combine_lane(h, sp, t, bank[:, 128 * u : 128 * u + 128], slice(64 * u, 64 * u + 64))
+
+        def combine_lane(h, sp, t, q, ms):
+            nc.vector.scalar_tensor_tensor(
+                out=unit_t(h, sp)[:, t, :].rearrange("p (m a) -> p m a", a=2)[:, ms, :],
+                in0=q.rearrange("p (a m) -> p m a", a=2),
+                scalar=q_factor[:, 4 * h + t : 4 * h + t + 1],
+                in1=eta_a[h, sp][:, t, :].rearrange("p (a m) -> p m a", a=2)[:, ms, :],
+                op0=ALU.mult,
+                op1=ALU.add,
+            )
+
+        def matmul_q_last(u):
+            q_bank[1, 3, u] = new_bank()
+            rows_ = slice(768 + 128 * u, 896 + 128 * u)
+            for t in range(4):
+                cols = slice(128 * t, 128 * t + 128)
+                for k in range(2):
+                    nc.tensor.matmul_mx(
+                        out=q_bank[1, 3, u][:, cols],
+                        lhsT=rl_codes[k, 1][:, cols].bitcast(FP8X4),
+                        lhsT_scale=rl_scales[k, 1][:, cols],
+                        rhs=rl_codes[k, 1][:, rows_].bitcast(FP8X4),
+                        rhs_scale=rl_scales[k, 1][:, rows_],
+                        start=(k == 0),
+                        stop=(k == 1),
+                    )
+
+        def combine_last(u):
+            for t in range(4):
+                combine_lane(1, 3, t, q_bank[1, 3, u][:, 128 * t : 128 * t + 128], slice(64 * u, 64 * u + 64))
 
         def planes_tile(h, hp):
             return slot_tile(("planes", h, hp), [P, 2048], BF16)
 
-        def interleave_out(h, sp, engine):
+        def interleave_out(h, sp, engine, ms=slice(0, 128)):
             lo = 2 * (sp % 2)
-            out = planes_tile(h, sp // 2)[:].rearrange("p (m a t) -> p m t a", a=4, t=4)[:, :, :, lo : lo + 2]
-            in_ = out_t[h, sp][:].rearrange("p t (m a) -> p m t a", a=2)
+            out = planes_tile(h, sp // 2)[:].rearrange("p (m a t) -> p m t a", a=4, t=4)[:, ms, :, lo : lo + 2]
+            in_ = unit_t(h, sp).rearrange("p t (m a) -> p m t a", a=2)[:, ms]
             if engine is nc.vector:
                 nc.vector.tensor_copy(out=out, in_=in_)
             elif engine is nc.scalar:
@@ -276,11 +435,24 @@ def tile_skewgradientquadraticstep_kernel(tc, x, g, c, d, eta, out_0, out_1, out
             else:
                 gpsimd_move(out.rearrange("p m t a -> p m a t"), in_.rearrange("p m t a -> p m a t"))
 
-        def quantize_out(h, hp):
-            words = keep.tile([P, 512], U32, name="out_codes_%d%d" % (h, hp), align_bytes=64)
-            cols = slice(512 * hp, 512 * hp + 512)
-            nc.vector.quantize_mx(out=words[:].bitcast(FP8X4), scales=out_scales[4 * h : P, cols], in_=planes_tile(h, hp)[:])
-            nc.sync.dma_start(out=out_1[h, :, cols, :].rearrange("p m b -> p (m b)").bitcast(I32), in_=words[:].bitcast(I32))
+        out_words, rows = {}, {}
+
+        def quantize_out(h, lo, hi):
+            hp = lo // 512
+            if (h, hp) not in out_words:
+                out_words[h, hp] = keep.tile([P, 512], U32, name="out_codes_%d%d" % (h, hp), align_bytes=64)
+            nc.vector.quantize_mx(
+                out=out_words[h, hp][:, lo - 512 * hp : hi - 512 * hp].bitcast(FP8X4),
+                scales=out_scales[4 * h : P, lo:hi],
+                in_=planes_tile(h, hp)[:, 4 * (lo - 512 * hp) : 4 * (hi - 512 * hp)],
+            )
+
+        def store_words(h, lo, hi):
+            hp = lo // 512
+            nc.sync.dma_start(
+                out=out_1[h, :, lo:hi, :].rearrange("p m b -> p (m b)").bitcast(I32),
+                in_=out_words[h, hp][:, lo - 512 * hp : hi - 512 * hp].bitcast(I32),
+            )
 
         def store_scales():
             for quad in range(4):
@@ -289,144 +461,244 @@ def tile_skewgradientquadraticstep_kernel(tc, x, g, c, d, eta, out_0, out_1, out
                     in_=out_scales[32 * quad : 32 * quad + 8, :].bitcast(I32),
                 )
 
-        def transpose_out(h, sp):
-            for u in range(2):
-                out_bank[h, sp, u] = new_bank()
-                for t in range(4):
-                    nc.tensor.transpose(
-                        out_bank[h, sp, u][:, 128 * t : 128 * t + 128], out_t[h, sp][:, t, 128 * u : 128 * u + 128], ident[:]
-                    )
-
-        def store_out(h, sp):
-            rows = work.tile([P, 2, 512], F32, name="rows", align_bytes=64, bufs=ROWS_BUFS)
-            lo = 2 * (sp % 2)
-            for u in range(2):
-                nc.scalar.copy(
-                    out=rows[:, u, :].rearrange("m (p t) -> m p t", t=4),
-                    in_=out_bank[h, sp, u][:].rearrange("m (t p) -> m p t", t=4),
+        def transpose_out(h, sp, u):
+            out_bank[h, sp, u] = new_bank()
+            for t in range(4):
+                nc.tensor.transpose(
+                    out_bank[h, sp, u][:, 128 * t : 128 * t + 128], unit_t(h, sp)[:, t, 128 * u : 128 * u + 128], ident[:]
                 )
-                nc.sync.dma_start(out=out_rows[sp // 2, u, :, lo : lo + 2, 512 * h : 512 * h + 512], in_=rows[:, u, :])
 
-        for s in range(8):
-            transpose_in("g", s)
-            quantize_in("g", s)
-            if s > 0:
-                quantize_in("x", s - 1)
-            transpose_in("x", s)
-            negate(s)
+        def copy_rows(h, sp, u, engine):
+            rows[h, sp, u] = keep.tile([P, 512], F32, name="rows", tag="rows_%s%d" % ("gx"[u], 4 * h + sp), align_bytes=64)
+            out = rows[h, sp, u][:].rearrange("m (p t) -> m p t", t=4)
+            in_ = out_bank[h, sp, u][:].rearrange("m (t p) -> m p t", t=4)
+            if engine is nc.vector:
+                nc.vector.tensor_copy(out=out, in_=in_)
+            else:
+                nc.scalar.copy(out=out, in_=in_)
+
+        def store_rows(h, sp, u):
+            lo = 2 * (sp % 2)
+            nc.sync.dma_start(out=out_rows[sp // 2, u, :, lo : lo + 2, 512 * h : 512 * h + 512], in_=rows[h, sp, u][:])
+
+        transpose_in("g", 0)
+        transpose_in("x", 0)
+        transpose_in("g", 1)
+        transpose_in("x", 1)
+        transpose_in("g", 2)
+        transpose_in("x", 2)
+        transpose_in("g", 3)
+        transpose_in("x", 3)
+        transpose_in("g", 4)
+        transpose_in("x", 4)
+        transpose_in("g", 5)
+        transpose_in("x", 5)
+        transpose_in("g", 6)
+        transpose_in("x", 6)
+        transpose_in("g", 7)
+        transpose_in("x", 7)
+        copy_in("g", 0)
+        copy_in("x", 0)
+        copy_in("g", 1)
+        copy_in("x", 1)
+        copy_in("g", 2)
+        copy_in("x", 2)
+        copy_in("g", 3)
+        copy_in("x", 3)
+        copy_in("g", 4)
+        copy_in("x", 4)
+        copy_in("g", 5)
+        copy_in("x", 5)
+        copy_in("g", 6)
+        copy_in("x", 6)
+        copy_in("g", 7)
+        copy_in("x", 7)
+        make_row_factors()
+        quantize_one("g", 0)
+        quantize_one("x", 0)
+        quantize_in(1)
+        negate(0)
+        quantize_in(2)
+        quantize_minus(0)
+        quantize_in(3)
+        negate(1)
+        quantize_in(4)
+        quantize_minus(1)
+        quantize_in(5)
+        negate(2)
+        quantize_in(6)
+        quantize_minus(2)
+        quantize_in(7)
+        negate(3)
+        make_q_factor()
         matmul_a(0, 0)
-        make_factors()
-        quantize_in("x", 7)
-
-        for h, s in ((0, 1), (0, 2), (1, 0), (1, 1), (1, 2), (1, 3), (0, 3)):
-            matmul_a(h, s)
-        scalar_l(0, 0)
-        scalar_eta(0, 0)
-        vector_r(0, 1)
-        vector_r(0, 0)
-        scalar_l(0, 1)
-        gpsimd_l(0, 0)
-        scalar_eta(0, 1)
-        matmul_a(1, 4)
+        matmul_a(0, 1)
+        matmul_a(0, 4)
+        matmul_a(0, 5)
+        matmul_a(0, 6)
+        matmul_a(0, 7)
+        matmul_a(0, 2)
+        vector_rl(0, 0)
+        quantize_minus(3)
+        vector_rl(0, 1)
+        vector_r(0, 4)
+        quantize_rl(0, 0, 0, 1)
+        vector_r(0, 5)
+        quantize_rl(0, 0, 2, 3)
+        vector_r(0, 6)
+        vector_r(0, 7)
+        quantize_rl(0, 1, 0, 2)
         vector_rl(0, 2)
+        scalar_eta(0, 0)
+        scalar_eta(0, 1)
+        copy_plain(4)
+        scalar_l_plain(4, 1)
+        copy_plain(5)
+        copy_plain(6)
+        scalar_l_plain(5, 1)
+        copy_plain(7)
+        scalar_l_plain(6, 2)
         scalar_eta(0, 2)
-        for s in range(2):
-            vector_r(1, s)
-            copy_plain(s)
-            scalar_l(1, s)
-        quantize_low(0, 0, 256)
-        quantize_low(0, 512, 768)
-        quantize_low(1, 0, 256)
-        gpsimd_l(1, 0)
-        for s in range(2, 4):
-            vector_rl(1, s)
-            copy_plain(s)
-        for s in range(4, 8):
-            mirror_a(s)
-        gpsimd_eta(0)
-        gpsimd_eta(1)
-        vector_rl(0, 3)
-        scalar_eta(0, 3)
+        mirror_a(0)
+        matmul_a(0, 3)
+        mirror_a(1)
+        matmul_a(1, 4)
         matmul_a(1, 5)
         matmul_a(1, 6)
-
-        for h, s in ((1, 4), (0, 4), (0, 5)):
-            vector_r(h, s)
-        quantize_low(0, 256, 512)
-        quantize_low(0, 768, 1024)
-        quantize_low(1, 768, 1024)
-        quantize_low(1, 256, 768)
-        gpsimd_eta(2)
-        gpsimd_eta(3)
-        for h in (1, 0):
-            scalar_l(h, 4)
-            scalar_eta(h, 4)
         matmul_a(1, 7)
-        matmul_q(0, 0)
-        scalar_l(0, 5)
+        vector_r(1, 1)
+        vector_r(1, 0)
+        vector_rl(0, 3)
+        vector_rl(1, 3)
+        vector_rl(1, 2)
+        vector_r(1, 5)
+        vector_r(1, 4)
+        quantize_rl(0, 0, 1, 2)
         gpsimd_l(0, 2)
-        scalar_eta(0, 5)
-        for h, s in ((0, 6), (0, 7), (1, 5), (1, 6), (1, 7)):
-            vector_r(h, s)
-        scalar_l(1, 5)
-        scalar_eta(1, 5)
-        matmul_q(0, 1)
-        combine(0, 0, (0, 1))
-        quantize_r(0)
-        quantize_r(1)
-        quantize_l_pair(2)
-        gpsimd_l(1, 2)
-        matmul_q(1, 0)
-        for s in (6, 7):
-            scalar_l(0, s)
-            scalar_eta(0, s)
-        combine(0, 0, (2, 3))
-
-        interleave_out(0, 0, nc.scalar)
-        transpose_out(0, 0)
-        store_out(0, 0)
-        combine(0, 1)
-        matmul_q(1, 1)
-        transpose_out(0, 1)
-        for s in (6, 7):
-            vector_l(1, s)
-            scalar_eta(1, s)
-        quantize_l_half()
+        gpsimd_eta_wide(0, 0)
         gpsimd_l(0, 3)
+        gpsimd_eta_wide(0, 1)
+        scalar_l(1, 1)
+        scalar_l(1, 0)
+        scalar_eta(0, 3)
+        scalar_eta(1, 1)
+        scalar_eta(1, 0)
+        scalar_eta(1, 3)
+        scalar_eta(1, 2)
+        scalar_l(1, 5)
+        scalar_l(1, 4)
+        scalar_eta(1, 4)
+        scalar_eta(1, 5)
+        gpsimd_l(1, 0)
+        gpsimd_eta_wide(0, 2)
+        gpsimd_l(1, 2)
+        quantize_rl(1, 0, 0, 4)
+        quantize_rl(0, 0, 3, 4)
+        vector_r(1, 6)
+        vector_r(1, 7)
+        quantize_rl(0, 1, 2, 4)
+        quantize_rl(1, 1, 0, 2)
+        scalar_l(1, 7)
+        scalar_l(1, 6)
+        scalar_eta(1, 7)
+        scalar_eta(1, 6)
+        matmul_q(0, 0)
+        matmul_q(0, 1)
+        matmul_q(1, 0)
+        combine(0, 0, 1)
+        combine(0, 0, 0)
+        combine(0, 1, 1)
+        combine(0, 1, 0)
+        combine(1, 0, 1)
+        combine(1, 0, 0)
+        gpsimd_l(1, 3)
+        interleave_out(1, 0, nc.gpsimd, slice(0, 112))
+        transpose_out(0, 0, 0)
+        transpose_out(0, 0, 1)
+        matmul_q(1, 1)
+        transpose_out(0, 1, 0)
+        transpose_out(0, 1, 1)
+        transpose_out(1, 0, 0)
+        transpose_out(1, 0, 1)
+        quantize_rl(1, 1, 2, 4)
+        combine(1, 1, 1)
+        combine(1, 1, 0)
+        interleave_out(0, 1, nc.vector)
+        interleave_out(1, 1, nc.gpsimd, slice(0, 112))
+        copy_rows(0, 0, 1, nc.scalar)
+        copy_rows(0, 0, 0, nc.scalar)
+        scalar_eta_wide(0, 3)
+        interleave_out(0, 0, nc.scalar)
+        copy_rows(0, 1, 1, nc.scalar)
+        copy_rows(0, 1, 0, nc.scalar)
+        copy_rows(1, 0, 1, nc.scalar)
+        copy_rows(1, 0, 0, nc.scalar)
+        interleave_out(1, 0, nc.scalar, slice(112, 128))
+        store_rows(0, 0, 1)
+        store_rows(0, 0, 0)
+        store_rows(0, 1, 1)
+        store_rows(0, 1, 0)
+        store_rows(1, 0, 1)
+        store_rows(1, 0, 0)
         matmul_q(0, 2)
-        interleave_out(0, 1, nc.scalar)
-        store_out(0, 1)
-        combine(1, 0)
-        transpose_out(1, 0)
-        matmul_q(1, 2)
-        store_out(1, 0)
-        combine(1, 1)
-        quantize_l_pair(3)
-        quantize_out(0, 0)
-
-        for sp in range(2):
-            interleave_out(1, sp, nc.gpsimd)
-        transpose_out(1, 1)
+        transpose_out(1, 1, 0)
+        transpose_out(1, 1, 1)
         matmul_q(0, 3)
-        store_out(1, 1)
-        combine(0, 2)
-        transpose_out(0, 2)
-        interleave_out(0, 2, nc.scalar)
-        store_out(0, 2)
-        combine(1, 2)
-        transpose_out(1, 2)
-        matmul_q(1, 3)
-        combine(0, 3)
-        store_out(1, 2)
-        transpose_out(0, 3)
-        combine(1, 3)
-        quantize_out(1, 0)
-        transpose_out(1, 3)
-        for h in range(2):
-            store_out(h, 3)
-        interleave_out(0, 3, nc.gpsimd)
-        interleave_out(1, 2, nc.gpsimd)
-        interleave_out(1, 3, nc.gpsimd)
-        quantize_out(0, 1)
-        quantize_out(1, 1)
+        combine(0, 2, 1)
+        combine(0, 2, 0)
+        quantize_out(0, 0, 512)
+        combine(0, 3, 1)
+        combine(0, 3, 0)
+        interleave_out(0, 2, nc.gpsimd, slice(0, 112))
+        interleave_out(0, 3, nc.gpsimd, slice(0, 112))
+        copy_rows(1, 1, 1, nc.scalar)
+        copy_rows(1, 1, 0, nc.scalar)
+        interleave_out(1, 1, nc.scalar, slice(112, 128))
+        store_rows(1, 1, 1)
+        store_rows(1, 1, 0)
+        store_words(0, 0, 512)
+        transpose_out(0, 2, 0)
+        transpose_out(0, 2, 1)
+        matmul_q(1, 2)
+        transpose_out(0, 3, 0)
+        transpose_out(0, 3, 1)
+        matmul_q_last(0)
+        quantize_out(1, 0, 512)
+        combine(1, 2, 1)
+        combine(1, 2, 0)
+        combine_last(0)
+        interleave_out(1, 2, nc.gpsimd, slice(0, 64))
+        interleave_out(1, 3, nc.gpsimd, slice(0, 64))
+        copy_rows(0, 2, 1, nc.scalar)
+        copy_rows(0, 2, 0, nc.scalar)
+        interleave_out(0, 2, nc.scalar, slice(112, 128))
+        copy_rows(0, 3, 1, nc.scalar)
+        copy_rows(0, 3, 0, nc.scalar)
+        interleave_out(0, 3, nc.scalar, slice(112, 128))
+        interleave_out(1, 2, nc.scalar, slice(64, 128))
+        store_rows(0, 2, 1)
+        store_rows(0, 2, 0)
+        store_words(1, 0, 512)
+        store_rows(0, 3, 1)
+        store_rows(0, 3, 0)
+        transpose_out(1, 2, 0)
+        transpose_out(1, 2, 1)
+        matmul_q_last(1)
+        transpose_out(1, 3, 0)
+        quantize_out(0, 512, 1024)
+        combine_last(1)
+        interleave_out(1, 3, nc.vector, slice(64, 128))
+        quantize_out(1, 512, 768)
+        quantize_out(1, 768, 1024)
+        copy_rows(1, 2, 1, nc.scalar)
+        copy_rows(1, 2, 0, nc.scalar)
+        copy_rows(1, 3, 0, nc.scalar)
+        store_words(0, 512, 1024)
+        store_rows(1, 2, 1)
+        store_rows(1, 2, 0)
+        store_rows(1, 3, 0)
+        transpose_out(1, 3, 1)
+        copy_rows(1, 3, 1, nc.scalar)
         store_scales()
+        store_rows(1, 3, 1)
+        store_words(1, 512, 1024)

@@ -19,6 +19,7 @@ FLOPS = 2 * 2 * N * N * N
 RSQRT2 = 1.0 / math.sqrt(2.0)
 PSUM_BANKS = 8
 L_ROWS_BUFS = 4
+SPLIT_LOADS = ()
 Q_SCALE = 0.5 / 32.0
 
 SLOT = {
@@ -29,15 +30,17 @@ SLOT = {
     ("rl", 0, 0): "a",
     ("rl", 1, 0): "b",
     ("r", 0): "c",
-    ("l", 0): "f",
+    ("l", 0): "c",
     ("r", 1): "d",
     ("l", 1): "d",
-    ("eta", 0): "h",
-    ("eta", 1): "i",
+    ("eta", 0): "h0",
+    ("eta", 1): "h1",
+    ("eta", 2): "a",
+    ("eta", 3): "h3",
     ("planes", 0, 0): "m0",
-    ("planes", 1, 0): "g",
-    ("planes", 0, 1): "a",
-    ("planes", 1, 1): "b",
+    ("planes", 1, 0): "d",
+    ("planes", 0, 1): "m0",
+    ("planes", 1, 1): "m0",
 }
 
 
@@ -56,7 +59,7 @@ def tile_skewgradientquadraticstep_kernel(tc, x, g, c, d, eta, out_0, out_1, out
 
         def slot_tile(key, shape, dtype):
             if key not in shared:
-                shared[key] = keep.tile(shape, dtype, name=key[0], tag="slot_" + SLOT[key], align_bytes=64)
+                shared[key] = keep.tile(shape, dtype, name=key[0], tag=SLOT[key], align_bytes=64)
             return shared[key]
 
         src = {"x": x.rearrange("(h m t) k -> h t m k", h=2, t=4), "g": g.rearrange("(h m t) k -> h t m k", h=2, t=4)}
@@ -64,7 +67,8 @@ def tile_skewgradientquadraticstep_kernel(tc, x, g, c, d, eta, out_0, out_1, out
         for s in range(8):
             for op in ("g", "x"):
                 raw[op, s] = keep.tile([P, N], BF16, name="raw", tag="rows_%s%d" % (op, s), align_bytes=64)
-                nc.sync.dma_start(out=raw[op, s][:], in_=src[op][s // 4, s % 4])
+                for lo, hi in ((0, 512), (512, N)) if (op, s) in SPLIT_LOADS else ((0, N),):
+                    nc.sync.dma_start(out=raw[op, s][:, lo:hi], in_=src[op][s // 4, s % 4][:, lo:hi])
         vecs = keep.tile([P, 3, 16], BF16, name="vecs")
         for v, vec in enumerate((c, d, eta)):
             nc.sync.dma_start(
@@ -145,16 +149,12 @@ def tile_skewgradientquadraticstep_kernel(tc, x, g, c, d, eta, out_0, out_1, out
         a_bank, l_rows, eta_a, rl_codes, rl_scales = {}, {}, {}, {}, {}
         for h in range(2):
             for sp in range(4):
-                if sp == 2:
-                    eta_wide[h] = slot_tile(("eta", h), [P, 4, 512], F32)
-                if sp < 2:
+                if h == 1 or sp < 2:
                     eta_a[h, sp] = keep.tile([P, 4, 256], F32, name="eta_a_%d%d" % (h, sp))
-                else:
-                    eta_a[h, sp] = eta_wide[h][:, :, 256 * sp - 512 : 256 * sp - 256]
             for hp in range(2):
                 rl_codes[h, hp] = keep.tile([P, 1024], U32, name="rl_codes_%d%d" % (h, hp), align_bytes=64)
                 rl_scales[h, hp] = keep.tile([P, 1024], U8, name="rl_scales_%d%d" % (h, hp), align_bytes=64)
-        plain_of = [keep.tile([P, 4, 512], F32, name="plain_%d" % h) for h in range(2)]
+        plain_of = [keep.tile([P, 4, 512], F32, name="plain_%d" % h) for h in range(1)]
         plain = plain_of[0]
 
         def matmul_a(h, s, lanes=range(4)):
@@ -187,16 +187,19 @@ def tile_skewgradientquadraticstep_kernel(tc, x, g, c, d, eta, out_0, out_1, out
                 op=ALU.mult,
             )
 
+        def eta_source(t):
+            return slot_tile(("eta", t), [P, 512], F32)
+
         def gpsimd_eta_wide(h, t):
             gpsimd_move(
-                eta_wide[h][:, t, :].rearrange("p (s n) -> p s n", s=4),
+                eta_source(t)[:].rearrange("p (s n) -> p s n", s=4),
                 plain_of[h][:, :, 128 * t : 128 * t + 128],
                 factor(h, 4)[:, 2, t : t + 1],
             )
 
         def scalar_eta_wide(h, t):
             nc.scalar.activation(
-                out=eta_wide[h][:, t, :].rearrange("p (s n) -> p s n", s=4),
+                out=eta_source(t)[:].rearrange("p (s n) -> p s n", s=4),
                 in_=plain_of[h][:, :, 128 * t : 128 * t + 128],
                 func=COPY,
                 scale=factor(h, 4)[:, 2, t : t + 1],
@@ -392,11 +395,12 @@ def tile_skewgradientquadraticstep_kernel(tc, x, g, c, d, eta, out_0, out_1, out
                         combine_lane(h, sp, t, bank[:, 128 * u : 128 * u + 128], slice(64 * u, 64 * u + 64))
 
         def combine_lane(h, sp, t, q, ms):
+            first = eta_source(t)[:, 256 * sp - 512 : 256 * sp - 256] if h == 0 and sp >= 2 else eta_a[h, sp][:, t, :]
             nc.vector.scalar_tensor_tensor(
                 out=unit_t(h, sp)[:, t, :].rearrange("p (m a) -> p m a", a=2)[:, ms, :],
                 in0=q.rearrange("p (a m) -> p m a", a=2),
                 scalar=q_factor[:, 4 * h + t : 4 * h + t + 1],
-                in1=eta_a[h, sp][:, t, :].rearrange("p (a m) -> p m a", a=2)[:, ms, :],
+                in1=first.rearrange("p (a m) -> p m a", a=2)[:, ms, :],
                 op0=ALU.mult,
                 op1=ALU.add,
             )
@@ -559,6 +563,10 @@ def tile_skewgradientquadraticstep_kernel(tc, x, g, c, d, eta, out_0, out_1, out
         copy_plain(7)
         scalar_l_plain(6, 2)
         scalar_eta(0, 2)
+        gpsimd_l(0, 2)
+        gpsimd_eta_wide(0, 0)
+        gpsimd_l(0, 3)
+        gpsimd_eta_wide(0, 1)
         mirror_a(0)
         matmul_a(0, 3)
         mirror_a(1)
@@ -574,10 +582,6 @@ def tile_skewgradientquadraticstep_kernel(tc, x, g, c, d, eta, out_0, out_1, out
         vector_r(1, 5)
         vector_r(1, 4)
         quantize_rl(0, 0, 1, 2)
-        gpsimd_l(0, 2)
-        gpsimd_eta_wide(0, 0)
-        gpsimd_l(0, 3)
-        gpsimd_eta_wide(0, 1)
         scalar_l(1, 1)
         scalar_l(1, 0)
         scalar_eta(0, 3)
@@ -602,6 +606,8 @@ def tile_skewgradientquadraticstep_kernel(tc, x, g, c, d, eta, out_0, out_1, out
         scalar_l(1, 6)
         scalar_eta(1, 7)
         scalar_eta(1, 6)
+        scalar_eta_wide(0, 3)
+        gpsimd_l(1, 3)
         matmul_q(0, 0)
         matmul_q(0, 1)
         matmul_q(1, 0)
@@ -611,8 +617,8 @@ def tile_skewgradientquadraticstep_kernel(tc, x, g, c, d, eta, out_0, out_1, out
         combine(0, 1, 0)
         combine(1, 0, 1)
         combine(1, 0, 0)
-        gpsimd_l(1, 3)
-        interleave_out(1, 0, nc.gpsimd, slice(0, 112))
+        quantize_rl(1, 1, 2, 4)
+        interleave_out(1, 0, nc.gpsimd, slice(0, 72))
         transpose_out(0, 0, 0)
         transpose_out(0, 0, 1)
         matmul_q(1, 1)
@@ -620,85 +626,82 @@ def tile_skewgradientquadraticstep_kernel(tc, x, g, c, d, eta, out_0, out_1, out
         transpose_out(0, 1, 1)
         transpose_out(1, 0, 0)
         transpose_out(1, 0, 1)
-        quantize_rl(1, 1, 2, 4)
+        matmul_q(0, 2)
         combine(1, 1, 1)
         combine(1, 1, 0)
         interleave_out(0, 1, nc.vector)
-        interleave_out(1, 1, nc.gpsimd, slice(0, 112))
+        combine(0, 2, 1)
+        combine(0, 2, 0)
         copy_rows(0, 0, 1, nc.scalar)
         copy_rows(0, 0, 0, nc.scalar)
-        scalar_eta_wide(0, 3)
         interleave_out(0, 0, nc.scalar)
         copy_rows(0, 1, 1, nc.scalar)
         copy_rows(0, 1, 0, nc.scalar)
         copy_rows(1, 0, 1, nc.scalar)
         copy_rows(1, 0, 0, nc.scalar)
-        interleave_out(1, 0, nc.scalar, slice(112, 128))
+        interleave_out(1, 1, nc.gpsimd, slice(0, 128))
+        interleave_out(0, 2, nc.gpsimd, slice(0, 72))
         store_rows(0, 0, 1)
         store_rows(0, 0, 0)
         store_rows(0, 1, 1)
         store_rows(0, 1, 0)
         store_rows(1, 0, 1)
         store_rows(1, 0, 0)
-        matmul_q(0, 2)
         transpose_out(1, 1, 0)
         transpose_out(1, 1, 1)
         matmul_q(0, 3)
-        combine(0, 2, 1)
-        combine(0, 2, 0)
-        quantize_out(0, 0, 512)
-        combine(0, 3, 1)
-        combine(0, 3, 0)
-        interleave_out(0, 2, nc.gpsimd, slice(0, 112))
-        interleave_out(0, 3, nc.gpsimd, slice(0, 112))
-        copy_rows(1, 1, 1, nc.scalar)
-        copy_rows(1, 1, 0, nc.scalar)
-        interleave_out(1, 1, nc.scalar, slice(112, 128))
-        store_rows(1, 1, 1)
-        store_rows(1, 1, 0)
-        store_words(0, 0, 512)
         transpose_out(0, 2, 0)
         transpose_out(0, 2, 1)
         matmul_q(1, 2)
+        quantize_out(0, 0, 512)
+        combine(0, 3, 1)
+        combine(0, 3, 0)
+        copy_rows(1, 1, 1, nc.scalar)
+        copy_rows(1, 1, 0, nc.scalar)
+        interleave_out(1, 0, nc.scalar, slice(72, 128))
+        copy_rows(0, 2, 1, nc.scalar)
+        copy_rows(0, 2, 0, nc.scalar)
+        interleave_out(0, 2, nc.scalar, slice(72, 128))
+        interleave_out(0, 3, nc.gpsimd, slice(0, 96))
+        store_rows(1, 1, 1)
+        store_rows(1, 1, 0)
+        store_words(0, 0, 512)
+        store_rows(0, 2, 1)
+        store_rows(0, 2, 0)
         transpose_out(0, 3, 0)
         transpose_out(0, 3, 1)
         matmul_q_last(0)
         quantize_out(1, 0, 512)
         combine(1, 2, 1)
         combine(1, 2, 0)
-        combine_last(0)
-        interleave_out(1, 2, nc.gpsimd, slice(0, 64))
-        interleave_out(1, 3, nc.gpsimd, slice(0, 64))
-        copy_rows(0, 2, 1, nc.scalar)
-        copy_rows(0, 2, 0, nc.scalar)
-        interleave_out(0, 2, nc.scalar, slice(112, 128))
+        interleave_out(0, 3, nc.scalar, slice(96, 128))
         copy_rows(0, 3, 1, nc.scalar)
         copy_rows(0, 3, 0, nc.scalar)
-        interleave_out(0, 3, nc.scalar, slice(112, 128))
-        interleave_out(1, 2, nc.scalar, slice(64, 128))
-        store_rows(0, 2, 1)
-        store_rows(0, 2, 0)
+        interleave_out(1, 2, nc.gpsimd, slice(0, 64))
         store_words(1, 0, 512)
         store_rows(0, 3, 1)
         store_rows(0, 3, 0)
         transpose_out(1, 2, 0)
         transpose_out(1, 2, 1)
         matmul_q_last(1)
-        transpose_out(1, 3, 0)
         quantize_out(0, 512, 1024)
+        combine_last(0)
         combine_last(1)
-        interleave_out(1, 3, nc.vector, slice(64, 128))
-        quantize_out(1, 512, 768)
-        quantize_out(1, 768, 1024)
+        interleave_out(1, 2, nc.scalar, slice(64, 128))
         copy_rows(1, 2, 1, nc.scalar)
         copy_rows(1, 2, 0, nc.scalar)
-        copy_rows(1, 3, 0, nc.scalar)
+        interleave_out(1, 3, nc.gpsimd, slice(0, 64))
         store_words(0, 512, 1024)
         store_rows(1, 2, 1)
         store_rows(1, 2, 0)
-        store_rows(1, 3, 0)
+        transpose_out(1, 3, 0)
         transpose_out(1, 3, 1)
+        interleave_out(1, 3, nc.vector, slice(64, 128))
+        quantize_out(1, 512, 768)
+        quantize_out(1, 768, 1024)
+        copy_rows(1, 3, 0, nc.scalar)
         copy_rows(1, 3, 1, nc.scalar)
         store_scales()
+        store_rows(1, 3, 0)
         store_rows(1, 3, 1)
         store_words(1, 512, 1024)

@@ -19,28 +19,21 @@ FLOPS = 2 * 2 * N * N * N
 RSQRT2 = 1.0 / math.sqrt(2.0)
 PSUM_BANKS = 8
 L_ROWS_BUFS = 4
-SPLIT_LOADS = ()
 Q_SCALE = 0.5 / 32.0
+SHARE_FIRST = 72
+SHARE_SECOND = 96
+HALF = 64
 
 SLOT = {
-    ("minus", 0): "m0",
-    ("minus", 1): "m1",
-    ("minus", 2): "m0",
-    ("minus", 3): "m1",
-    ("rl", 0, 0): "a",
-    ("rl", 1, 0): "b",
-    ("r", 0): "c",
-    ("l", 0): "c",
-    ("r", 1): "d",
-    ("l", 1): "d",
-    ("eta", 0): "h0",
-    ("eta", 1): "h1",
-    ("eta", 2): "a",
-    ("eta", 3): "h3",
-    ("planes", 0, 0): "m0",
-    ("planes", 1, 0): "d",
-    ("planes", 0, 1): "m0",
-    ("planes", 1, 1): "m0",
+    ("minus", 0): "a", ("minus", 2): "a", ("planes", 0, 0): "a", ("planes", 0, 1): "a", ("planes", 1, 1): "a",
+    ("minus", 1): "b", ("minus", 3): "b",
+    ("rl", 0): "c",
+    ("rl", 1): "d", ("eta", 2): "d",
+    ("r", 0): "e", ("l", 0): "e",
+    ("r", 1): "f", ("l", 1): "f", ("planes", 1, 0): "f",
+    ("eta", 0): "g",
+    ("eta", 1): "h",
+    ("eta", 3): "i",
 }
 
 
@@ -59,16 +52,15 @@ def tile_skewgradientquadraticstep_kernel(tc, x, g, c, d, eta, out_0, out_1, out
 
         def slot_tile(key, shape, dtype):
             if key not in shared:
-                shared[key] = keep.tile(shape, dtype, name=key[0], tag=SLOT[key], align_bytes=64)
+                shared[key] = keep.tile(shape, dtype, name=key[0], tag="slot_" + SLOT[key], align_bytes=64)
             return shared[key]
 
         src = {"x": x.rearrange("(h m t) k -> h t m k", h=2, t=4), "g": g.rearrange("(h m t) k -> h t m k", h=2, t=4)}
         raw = {}
         for s in range(8):
             for op in ("g", "x"):
-                raw[op, s] = keep.tile([P, N], BF16, name="raw", tag="rows_%s%d" % (op, s), align_bytes=64)
-                for lo, hi in ((0, 512), (512, N)) if (op, s) in SPLIT_LOADS else ((0, N),):
-                    nc.sync.dma_start(out=raw[op, s][:, lo:hi], in_=src[op][s // 4, s % 4][:, lo:hi])
+                raw[op, s] = keep.tile([P, N], BF16, name="raw_%s%d" % (op, s), align_bytes=64)
+                nc.sync.dma_start(out=raw[op, s][:], in_=src[op][s // 4, s % 4])
         vecs = keep.tile([P, 3, 16], BF16, name="vecs")
         for v, vec in enumerate((c, d, eta)):
             nc.sync.dma_start(
@@ -92,7 +84,7 @@ def tile_skewgradientquadraticstep_kernel(tc, x, g, c, d, eta, out_0, out_1, out
         def factor(h, s):
             return row_factor[:, 3:6, 4:8] if h == 1 and s < 4 else row_factor[:, 0:3, 4 * h : 4 * h + 4]
 
-        codes, scales, turned, minus, in_bank = {}, {}, {}, {}, {}
+        codes, scales, turned = {}, {}, {}
 
         def transpose_in(op, s):
             words = raw[op, s][:].bitcast(F32)
@@ -101,10 +93,6 @@ def tile_skewgradientquadraticstep_kernel(tc, x, g, c, d, eta, out_0, out_1, out
                 for u in range(2):
                     lo = 128 * (2 * h + u)
                     nc.tensor.transpose(bank[:, lo : lo + 128], words[:, 256 * h + u : 256 * h + 256 : 2], ident[:])
-            in_bank[op, s] = bank
-
-        def copy_in(op, s):
-            bank = in_bank[op, s]
             if s // 2 not in turned:
                 turned[s // 2] = keep.tile([P, 4 * N], BF16, name="turned", tag="wide_%d" % (s // 2), align_bytes=64)
             lo = N * (2 * (s % 2) + (op == "x"))
@@ -124,18 +112,13 @@ def tile_skewgradientquadraticstep_kernel(tc, x, g, c, d, eta, out_0, out_1, out
                     codes[name, s, h] = words[:, lo : lo + 128].bitcast(FP8X4)
                     scales[name, s, h] = plane[:, lo : lo + 128]
 
-        def quantize_in(s):
-            lo = 2 * N * (s % 2)
-            quantize_operands(turned[s // 2][:, lo : lo + 2 * N], (("g", s), ("x", s)))
-
-        def quantize_one(op, s):
-            lo = N * (2 * (s % 2) + (op == "x"))
-            quantize_operands(turned[s // 2][:, lo : lo + N], ((op, s),))
+        def quantize_in(s, ops=("g", "x")):
+            lo = N * (2 * (s % 2) + (ops[0] == "x"))
+            quantize_operands(turned[s // 2][:, lo : lo + N * len(ops)], [(op, s) for op in ops])
 
         def negate(sp):
-            minus[sp] = slot_tile(("minus", sp), [P, 2 * N], BF16)
             nc.vector.tensor_scalar(
-                out=minus[sp][:].rearrange("p (j k) -> p j k", j=2),
+                out=slot_tile(("minus", sp), [P, 2 * N], BF16)[:].rearrange("p (j k) -> p j k", j=2),
                 in0=turned[sp][:].rearrange("p (j o k) -> p j o k", j=2, o=2)[:, :, 1, :],
                 scalar1=-1.0,
                 scalar2=None,
@@ -143,9 +126,8 @@ def tile_skewgradientquadraticstep_kernel(tc, x, g, c, d, eta, out_0, out_1, out
             )
 
         def quantize_minus(sp):
-            quantize_operands(minus[sp][:], (("minus_x", 2 * sp), ("minus_x", 2 * sp + 1)))
+            quantize_operands(shared["minus", sp][:], (("minus_x", 2 * sp), ("minus_x", 2 * sp + 1)))
 
-        eta_wide = {}
         a_bank, l_rows, eta_a, rl_codes, rl_scales = {}, {}, {}, {}, {}
         for h in range(2):
             for sp in range(4):
@@ -154,14 +136,12 @@ def tile_skewgradientquadraticstep_kernel(tc, x, g, c, d, eta, out_0, out_1, out
             for hp in range(2):
                 rl_codes[h, hp] = keep.tile([P, 1024], U32, name="rl_codes_%d%d" % (h, hp), align_bytes=64)
                 rl_scales[h, hp] = keep.tile([P, 1024], U8, name="rl_scales_%d%d" % (h, hp), align_bytes=64)
-        plain_of = [keep.tile([P, 4, 512], F32, name="plain_%d" % h) for h in range(1)]
-        plain = plain_of[0]
+        plain = keep.tile([P, 4, 512], F32, name="plain")
 
-        def matmul_a(h, s, lanes=range(4)):
-            if (h, s) not in a_bank:
-                a_bank[h, s] = new_bank()
+        def matmul_a(h, s):
+            a_bank[h, s] = new_bank()
             passes = [(left, right, k) for left, right in (("g", "x"), ("minus_x", "g")) for k in range(2)]
-            for t in lanes:
+            for t in range(4):
                 for step, (left, right, k) in enumerate(passes):
                     nc.tensor.matmul_mx(
                         out=a_bank[h, s][:, 128 * t : 128 * t + 128],
@@ -176,35 +156,6 @@ def tile_skewgradientquadraticstep_kernel(tc, x, g, c, d, eta, out_0, out_1, out
         def copy_plain(s):
             nc.scalar.copy(out=plain[:, s - 4, :], in_=a_bank[0, s][:])
 
-        def copy_plain1(s):
-            nc.scalar.copy(out=plain_of[1][:, s - 4, :], in_=a_bank[1, s][:])
-
-        def gpsimd_l_plain(h, sp):
-            nc.gpsimd.tensor_tensor(
-                out=l_flat(h, sp).rearrange("p (j n t) -> p j n t", j=2, t=4),
-                in0=plain_of[h][:, 2 * sp - 4 : 2 * sp - 2, :].rearrange("p j (t n) -> p j n t", t=4),
-                in1=factor(h, 4)[:, 1:2, :].unsqueeze(1).to_broadcast([P, 2, 128, 4]),
-                op=ALU.mult,
-            )
-
-        def eta_source(t):
-            return slot_tile(("eta", t), [P, 512], F32)
-
-        def gpsimd_eta_wide(h, t):
-            gpsimd_move(
-                eta_source(t)[:].rearrange("p (s n) -> p s n", s=4),
-                plain_of[h][:, :, 128 * t : 128 * t + 128],
-                factor(h, 4)[:, 2, t : t + 1],
-            )
-
-        def scalar_eta_wide(h, t):
-            nc.scalar.activation(
-                out=eta_source(t)[:].rearrange("p (s n) -> p s n", s=4),
-                in_=plain_of[h][:, :, 128 * t : 128 * t + 128],
-                func=COPY,
-                scale=factor(h, 4)[:, 2, t : t + 1],
-            )
-
         def mirror_a(sp):
             for s in (2 * sp, 2 * sp + 1):
                 a_bank[1, s] = new_bank()
@@ -214,188 +165,114 @@ def tile_skewgradientquadraticstep_kernel(tc, x, g, c, d, eta, out_0, out_1, out
                         a_bank[1, s][:, 128 * t : 128 * t + 128], plain[:, t, 128 * s : 128 * s + 128], ident[:]
                     )
 
-        def rl_tile(h, hp):
-            return slot_tile(("rl", h, hp), [P, 4096], BF16)
-
         def rl_part(h, hp, first, last):
             if hp == 0:
-                return rl_tile(h, hp)[:, 1024 * first : 1024 * last]
+                return slot_tile(("rl", h), [P, 4096], BF16)[:, 1024 * first : 1024 * last]
             if first < 2:
                 return slot_tile(("r", h), [P, 2048], BF16)[:, 1024 * first : 1024 * last]
-            if ("l", h) in SLOT:
-                return slot_tile(("l", h), [P, 2048], BF16)[:, 1024 * (first - 2) : 1024 * (last - 2)]
-            return slot_tile(("l", h, first), [P, 1024], BF16)[:]
+            return slot_tile(("l", h), [P, 2048], BF16)[:, 1024 * (first - 2) : 1024 * (last - 2)]
 
-        def r_part(h, s):
-            lo = 512 * (s % 2)
-            return rl_part(h, s // 4, s % 4 // 2, s % 4 // 2 + 1)[:, lo : lo + 512].rearrange("p (n t) -> p n t", t=4)
-
-        def l_flat(h, sp):
-            return rl_part(h, sp // 2, 2 + sp % 2, 3 + sp % 2)
-
-        def l_tile(h, sp):
-            return l_flat(h, sp).rearrange("p (n t) -> p n t", t=4)
-
-        def scale_interleaved(out, h, s, row):
+        def vector_r(h, s):
+            lo = 512 * (s % 4)
             nc.vector.tensor_tensor(
-                out=out,
+                out=rl_part(h, s // 4, 0, 2)[:, lo : lo + 512].rearrange("p (n t) -> p n t", t=4),
                 in0=a_bank[h, s][:].rearrange("p (t n) -> p n t", t=4),
-                in1=factor(h, s)[:, row : row + 1, :].to_broadcast([P, 128, 4]),
+                in1=factor(h, s)[:, 0:1, :].to_broadcast([P, 128, 4]),
                 op=ALU.mult,
             )
 
-        def vector_r(h, s):
-            scale_interleaved(r_part(h, s), h, s, 0)
-
-        def vector_l(h, s):
-            if s < 6:
-                scale_interleaved(l_tile(h, s // 2)[:, 128 * (s % 2) : 128 * (s % 2) + 128, :], h, s, 1)
-            else:
-                nc.vector.tensor_tensor(
-                    out=l_flat(h, 3).rearrange("p (u a m t) -> p a u m t", u=2, a=2, t=4)[:, s % 2],
-                    in0=a_bank[h, s][:].rearrange("p (t u m) -> p u m t", t=4, u=2),
-                    in1=factor(h, s)[:, 1:2, :].unsqueeze(1).to_broadcast([P, 2, 64, 4]),
-                    op=ALU.mult,
-                )
-
         def vector_rl(h, s):
-            lo = 512 * (s % 4)
             nc.vector.tensor_tensor(
-                out=rl_tile(h, s // 4)[:].rearrange("p (o n t) -> p o n t", o=2, t=4)[:, :, lo // 4 : lo // 4 + 128, :],
+                out=rl_part(h, 0, 0, 4).rearrange("p (o n t) -> p o n t", o=2, t=4)[:, :, 128 * s : 128 * s + 128, :],
                 in0=a_bank[h, s][:].rearrange("p (t n) -> p n t", t=4).unsqueeze(1).to_broadcast([P, 2, 128, 4]),
                 in1=factor(h, s)[:, 0:2, :].unsqueeze(2).to_broadcast([P, 2, 128, 4]),
                 op=ALU.mult,
             )
 
-        def scale_rows(tile, h, s, row):
-            col = 128 * (s % 2)
+        def scale_rows(out, in_, h, s, row):
             for t in range(4):
-                nc.scalar.activation(
-                    out=tile[:, t, col : col + 128],
-                    in_=a_bank[h, s][:, 128 * t : 128 * t + 128],
-                    func=COPY,
-                    scale=factor(h, s)[:, row, t : t + 1],
-                )
+                nc.scalar.activation(out=out(t), in_=in_(t), func=COPY, scale=factor(h, s)[:, row, t : t + 1])
+
+        def l_columns(h, first, count):
+            if (h, first // 2) not in l_rows:
+                l_rows[h, first // 2] = work.tile([P, 4, 256], BF16, name="l_rows", align_bytes=64, bufs=L_ROWS_BUFS)
+            order = "p t (u a m) -> p t a u m" if first >= 6 else "p t (a u m) -> p t a u m"
+            return l_rows[h, first // 2][:].rearrange(order, u=2, a=2)[:, :, first % 2 : first % 2 + count]
 
         def scalar_l(h, s):
-            if (h, s // 2) not in l_rows:
-                l_rows[h, s // 2] = work.tile([P, 4, 256], BF16, name="l_rows", align_bytes=64, bufs=L_ROWS_BUFS)
-            if s < 6:
-                scale_rows(l_rows[h, s // 2], h, s, 1)
-            else:
-                for t in range(4):
-                    nc.scalar.activation(
-                        out=l_rows[h, 3][:, t, :].rearrange("p (u a m) -> p a u m", u=2, a=2)[:, s % 2],
-                        in_=a_bank[h, s][:, 128 * t : 128 * t + 128].rearrange("p (u m) -> p u m", u=2),
-                        func=COPY,
-                        scale=factor(h, s)[:, 1, t : t + 1],
-                    )
-
-        def scale_plain(tile, first, count, row):
-            lo = 128 * (first % 2)
-            for t in range(4):
-                nc.scalar.activation(
-                    out=tile[:, t, lo : lo + 128 * count].rearrange("p (j n) -> p j n", j=count),
-                    in_=plain[:, first - 4 : first - 4 + count, 128 * t : 128 * t + 128],
-                    func=COPY,
-                    scale=factor(0, 4)[:, row, t : t + 1],
-                )
+            bank = a_bank[h, s][:].rearrange("p (t a u m) -> p t a u m", t=4, a=1, u=2)
+            scale_rows(lambda t: l_columns(h, s, 1)[:, t], lambda t: bank[:, t], h, s, 1)
 
         def scalar_l_plain(first, count):
-            if (0, first // 2) not in l_rows:
-                l_rows[0, first // 2] = work.tile([P, 4, 256], BF16, name="l_rows", align_bytes=64, bufs=L_ROWS_BUFS)
-            if first < 6:
-                scale_plain(l_rows[0, first // 2], first, count, 1)
-            else:
-                for t in range(4):
-                    nc.scalar.activation(
-                        out=l_rows[0, 3][:, t, :].rearrange("p (u a m) -> p a u m", u=2, a=2)[:, first % 2 : first % 2 + count],
-                        in_=plain[:, first - 4 : first - 4 + count, 128 * t : 128 * t + 128].rearrange("p a (u m) -> p a u m", u=2),
-                        func=COPY,
-                        scale=factor(0, 4)[:, 1, t : t + 1],
-                    )
-
-        def scalar_eta_plain(first, count):
-            scale_plain(eta_a[0, first // 2], first, count, 2)
-
-        def gpsimd_eta_pair(sp):
-            for t in range(4):
-                gpsimd_move(
-                    eta_a[0, sp][:, t, :].rearrange("p (j n) -> p j n", j=2),
-                    plain[:, 2 * sp - 4 : 2 * sp - 2, 128 * t : 128 * t + 128],
-                    factor(0, 4)[:, 2, t : t + 1],
-                )
-
-        def vector_eta(h, s):
-            col = 128 * (s % 2)
-            nc.vector.tensor_tensor(
-                out=eta_a[h, s // 2][:, :, col : col + 128],
-                in0=a_bank[h, s][:].rearrange("p (t n) -> p t n", t=4),
-                in1=factor(h, s)[:, 2, :].unsqueeze(2).to_broadcast([P, 4, 128]),
-                op=ALU.mult,
-            )
+            banks = plain[:, first - 4 : first - 4 + count, :].rearrange("p a (t u m) -> p t a u m", t=4, u=2)
+            scale_rows(lambda t: l_columns(0, first, count)[:, t], lambda t: banks[:, t], 0, first, 1)
 
         def scalar_eta(h, s):
-            scale_rows(eta_a[h, s // 2], h, s, 2)
+            col = 128 * (s % 2)
+            scale_rows(
+                lambda t: eta_a[h, s // 2][:, t, col : col + 128], lambda t: a_bank[h, s][:, 128 * t : 128 * t + 128], h, s, 2
+            )
 
         def gpsimd_move(out, in_, scale=1.0):
             nc.gpsimd.tensor_scalar(out=out, in0=in_, scalar1=scale, scalar2=0.0, op0=ALU.mult, op1=ALU.add)
 
         def gpsimd_l(h, sp):
-            gpsimd_move(l_tile(h, sp), l_rows[h, sp][:].rearrange("p t n -> p n t"))
+            out = rl_part(h, sp // 2, 2 + sp % 2, 3 + sp % 2).rearrange("p (n t) -> p n t", t=4)
+            gpsimd_move(out, l_rows[h, sp][:].rearrange("p t n -> p n t"))
 
-        def eta_plain(t):
-            return slot_tile(("eta_a", t // 2), [P, 2, 512], F32)[:, t % 2, :]
-
-        def gpsimd_eta(t):
-            gpsimd_move(
-                eta_plain(t).rearrange("p (s n) -> p s n", s=4),
-                plain[:, :, 128 * t : 128 * t + 128],
-                factor(0, 4)[:, 2, t : t + 1],
-            )
+        def eta_source(t, engine):
+            out = slot_tile(("eta", t), [P, 512], F32)[:].rearrange("p (s n) -> p s n", s=4)
+            in_, scale = plain[:, :, 128 * t : 128 * t + 128], factor(0, 4)[:, 2, t : t + 1]
+            if engine is nc.scalar:
+                nc.scalar.activation(out=out, in_=in_, func=COPY, scale=scale)
+            else:
+                gpsimd_move(out, in_, scale)
 
         def quantize_rl(h, hp, first, last):
-            in_ = rl_part(h, hp, first, last)
             cols = slice(256 * first, 256 * last)
-            nc.vector.quantize_mx(out=rl_codes[h, hp][:, cols].bitcast(FP8X4), scales=rl_scales[h, hp][:, cols], in_=in_)
+            nc.vector.quantize_mx(
+                out=rl_codes[h, hp][:, cols].bitcast(FP8X4), scales=rl_scales[h, hp][:, cols], in_=rl_part(h, hp, first, last)
+            )
 
-        q_bank, out_t, out_bank = {}, {}, {}
+        q_bank, out_t, out_bank, out_words = {}, {}, {}, {}
         out_scales = keep.tile([P, N], U8, name="out_scales", align_bytes=64)
         out_rows = out_0.rearrange("(hp u m a) j -> hp u m a j", hp=2, u=2, a=4)
 
-        def matmul_q(h, sp):
+        def q_pass(out, h, sp, t, k, rows, start, stop):
+            cols = slice(128 * t, 128 * t + 128)
+            nc.tensor.matmul_mx(
+                out=out,
+                lhsT=rl_codes[k, h][:, cols].bitcast(FP8X4),
+                lhsT_scale=rl_scales[k, h][:, cols],
+                rhs=rl_codes[k, sp // 2][:, rows].bitcast(FP8X4),
+                rhs_scale=rl_scales[k, sp // 2][:, rows],
+                start=start,
+                stop=stop,
+            )
+
+        def matmul_q(h, sp, k_halves=(0, 1)):
             rows = slice(512 + 256 * (sp % 2), 768 + 256 * (sp % 2))
+            for k in k_halves:
+                for t in range(4):
+                    if k == 0 and t % 2 == 0:
+                        q_bank[h, sp, t // 2] = new_bank()
+                    out = q_bank[h, sp, t // 2][:, 256 * (t % 2) : 256 * (t % 2) + 256]
+                    q_pass(out, h, sp, t, k, rows, k == 0 and t % 2 == 0, k == 1 and t % 2 == 1)
+
+        def matmul_q_last(u):
+            q_bank[1, 3, u] = new_bank()
+            rows = slice(768 + 128 * u, 896 + 128 * u)
             for t in range(4):
-                if t % 2 == 0:
-                    q_bank[h, sp, t // 2] = new_bank()
-                cols = slice(128 * t, 128 * t + 128)
                 for k in range(2):
-                    nc.tensor.matmul_mx(
-                        out=q_bank[h, sp, t // 2][:, 256 * (t % 2) : 256 * (t % 2) + 256],
-                        lhsT=rl_codes[k, h][:, cols].bitcast(FP8X4),
-                        lhsT_scale=rl_scales[k, h][:, cols],
-                        rhs=rl_codes[k, sp // 2][:, rows].bitcast(FP8X4),
-                        rhs_scale=rl_scales[k, sp // 2][:, rows],
-                        start=(k == 0),
-                        stop=(k == 1),
-                    )
+                    q_pass(q_bank[1, 3, u][:, 128 * t : 128 * t + 128], 1, 3, t, k, rows, k == 0, k == 1)
 
         def unit_t(h, sp):
             if (h, sp // 2) not in out_t:
                 out_t[h, sp // 2] = keep.tile([P, 2048], F32, name="out_t", tag="wide_%d" % len(out_t), align_bytes=64)
             return out_t[h, sp // 2][:, 1024 * (sp % 2) : 1024 * (sp % 2) + 1024].rearrange("p (t n) -> p t n", t=4)
 
-        def combine(h, sp, half):
-            for t in (2 * half, 2 * half + 1):
-                bank = q_bank[h, sp, t // 2][:, 256 * (t % 2) : 256 * (t % 2) + 256]
-                if sp < 3:
-                    combine_lane(h, sp, t, bank, slice(0, 128))
-                else:
-                    for u in range(2):
-                        combine_lane(h, sp, t, bank[:, 128 * u : 128 * u + 128], slice(64 * u, 64 * u + 64))
-
         def combine_lane(h, sp, t, q, ms):
-            first = eta_source(t)[:, 256 * sp - 512 : 256 * sp - 256] if h == 0 and sp >= 2 else eta_a[h, sp][:, t, :]
+            first = shared["eta", t][:, 256 * sp - 512 : 256 * sp - 256] if h == 0 and sp >= 2 else eta_a[h, sp][:, t, :]
             nc.vector.scalar_tensor_tensor(
                 out=unit_t(h, sp)[:, t, :].rearrange("p (m a) -> p m a", a=2)[:, ms, :],
                 in0=q.rearrange("p (a m) -> p m a", a=2),
@@ -405,33 +282,26 @@ def tile_skewgradientquadraticstep_kernel(tc, x, g, c, d, eta, out_0, out_1, out
                 op1=ALU.add,
             )
 
-        def matmul_q_last(u):
-            q_bank[1, 3, u] = new_bank()
-            rows_ = slice(768 + 128 * u, 896 + 128 * u)
-            for t in range(4):
-                cols = slice(128 * t, 128 * t + 128)
-                for k in range(2):
-                    nc.tensor.matmul_mx(
-                        out=q_bank[1, 3, u][:, cols],
-                        lhsT=rl_codes[k, 1][:, cols].bitcast(FP8X4),
-                        lhsT_scale=rl_scales[k, 1][:, cols],
-                        rhs=rl_codes[k, 1][:, rows_].bitcast(FP8X4),
-                        rhs_scale=rl_scales[k, 1][:, rows_],
-                        start=(k == 0),
-                        stop=(k == 1),
-                    )
+        def combine(h, sp):
+            for t in (2, 3, 0, 1):
+                q = q_bank[h, sp, t // 2][:, 256 * (t % 2) : 256 * (t % 2) + 256]
+                if sp < 3:
+                    combine_lane(h, sp, t, q, slice(0, P))
+                else:
+                    for u in range(2):
+                        combine_lane(h, sp, t, q[:, 128 * u : 128 * u + 128], slice(HALF * u, HALF * u + HALF))
 
         def combine_last(u):
             for t in range(4):
-                combine_lane(1, 3, t, q_bank[1, 3, u][:, 128 * t : 128 * t + 128], slice(64 * u, 64 * u + 64))
+                combine_lane(1, 3, t, q_bank[1, 3, u][:, 128 * t : 128 * t + 128], slice(HALF * u, HALF * u + HALF))
 
         def planes_tile(h, hp):
             return slot_tile(("planes", h, hp), [P, 2048], BF16)
 
-        def interleave_out(h, sp, engine, ms=slice(0, 128)):
+        def interleave_out(h, sp, engine, first=0, last=P):
             lo = 2 * (sp % 2)
-            out = planes_tile(h, sp // 2)[:].rearrange("p (m a t) -> p m t a", a=4, t=4)[:, ms, :, lo : lo + 2]
-            in_ = unit_t(h, sp).rearrange("p t (m a) -> p m t a", a=2)[:, ms]
+            out = planes_tile(h, sp // 2)[:].rearrange("p (m a t) -> p m t a", a=4, t=4)[:, first:last, :, lo : lo + 2]
+            in_ = unit_t(h, sp).rearrange("p t (m a) -> p m t a", a=2)[:, first:last]
             if engine is nc.vector:
                 nc.vector.tensor_copy(out=out, in_=in_)
             elif engine is nc.scalar:
@@ -439,23 +309,19 @@ def tile_skewgradientquadraticstep_kernel(tc, x, g, c, d, eta, out_0, out_1, out
             else:
                 gpsimd_move(out.rearrange("p m t a -> p m a t"), in_.rearrange("p m t a -> p m a t"))
 
-        out_words, rows = {}, {}
-
-        def quantize_out(h, lo, hi):
-            hp = lo // 512
+        def quantize_out(h, hp, first=0, last=512):
             if (h, hp) not in out_words:
                 out_words[h, hp] = keep.tile([P, 512], U32, name="out_codes_%d%d" % (h, hp), align_bytes=64)
             nc.vector.quantize_mx(
-                out=out_words[h, hp][:, lo - 512 * hp : hi - 512 * hp].bitcast(FP8X4),
-                scales=out_scales[4 * h : P, lo:hi],
-                in_=planes_tile(h, hp)[:, 4 * (lo - 512 * hp) : 4 * (hi - 512 * hp)],
+                out=out_words[h, hp][:, first:last].bitcast(FP8X4),
+                scales=out_scales[4 * h : P, 512 * hp + first : 512 * hp + last],
+                in_=planes_tile(h, hp)[:, 4 * first : 4 * last],
             )
 
-        def store_words(h, lo, hi):
-            hp = lo // 512
+        def store_words(h, hp):
+            cols = slice(512 * hp, 512 * hp + 512)
             nc.sync.dma_start(
-                out=out_1[h, :, lo:hi, :].rearrange("p m b -> p (m b)").bitcast(I32),
-                in_=out_words[h, hp][:, lo - 512 * hp : hi - 512 * hp].bitcast(I32),
+                out=out_1[h, :, cols, :].rearrange("p m b -> p (m b)").bitcast(I32), in_=out_words[h, hp][:].bitcast(I32)
             )
 
         def store_scales():
@@ -465,243 +331,165 @@ def tile_skewgradientquadraticstep_kernel(tc, x, g, c, d, eta, out_0, out_1, out
                     in_=out_scales[32 * quad : 32 * quad + 8, :].bitcast(I32),
                 )
 
-        def transpose_out(h, sp, u):
-            out_bank[h, sp, u] = new_bank()
-            for t in range(4):
-                nc.tensor.transpose(
-                    out_bank[h, sp, u][:, 128 * t : 128 * t + 128], unit_t(h, sp)[:, t, 128 * u : 128 * u + 128], ident[:]
-                )
+        def transpose_out(h, sp, halves=(0, 1)):
+            for u in halves:
+                out_bank[h, sp, u] = new_bank()
+                for t in range(4):
+                    nc.tensor.transpose(
+                        out_bank[h, sp, u][:, 128 * t : 128 * t + 128], unit_t(h, sp)[:, t, 128 * u : 128 * u + 128], ident[:]
+                    )
 
-        def copy_rows(h, sp, u, engine):
-            rows[h, sp, u] = keep.tile([P, 512], F32, name="rows", tag="rows_%s%d" % ("gx"[u], 4 * h + sp), align_bytes=64)
-            out = rows[h, sp, u][:].rearrange("m (p t) -> m p t", t=4)
-            in_ = out_bank[h, sp, u][:].rearrange("m (t p) -> m p t", t=4)
-            if engine is nc.vector:
-                nc.vector.tensor_copy(out=out, in_=in_)
-            else:
-                nc.scalar.copy(out=out, in_=in_)
-
-        def store_rows(h, sp, u):
+        def store_rows(h, sp, halves=(1, 0)):
             lo = 2 * (sp % 2)
-            nc.sync.dma_start(out=out_rows[sp // 2, u, :, lo : lo + 2, 512 * h : 512 * h + 512], in_=rows[h, sp, u][:])
+            for u in halves:
+                rows = keep.tile([P, 512], F32, name="rows_%d%d%d" % (h, sp, u), align_bytes=64)
+                nc.scalar.copy(
+                    out=rows[:].rearrange("m (p t) -> m p t", t=4),
+                    in_=out_bank[h, sp, u][:].rearrange("m (t p) -> m p t", t=4),
+                )
+                nc.sync.dma_start(out=out_rows[sp // 2, u, :, lo : lo + 2, 512 * h : 512 * h + 512], in_=rows[:])
 
-        transpose_in("g", 0)
-        transpose_in("x", 0)
-        transpose_in("g", 1)
-        transpose_in("x", 1)
-        transpose_in("g", 2)
-        transpose_in("x", 2)
-        transpose_in("g", 3)
-        transpose_in("x", 3)
-        transpose_in("g", 4)
-        transpose_in("x", 4)
-        transpose_in("g", 5)
-        transpose_in("x", 5)
-        transpose_in("g", 6)
-        transpose_in("x", 6)
-        transpose_in("g", 7)
-        transpose_in("x", 7)
-        copy_in("g", 0)
-        copy_in("x", 0)
-        copy_in("g", 1)
-        copy_in("x", 1)
-        copy_in("g", 2)
-        copy_in("x", 2)
-        copy_in("g", 3)
-        copy_in("x", 3)
-        copy_in("g", 4)
-        copy_in("x", 4)
-        copy_in("g", 5)
-        copy_in("x", 5)
-        copy_in("g", 6)
-        copy_in("x", 6)
-        copy_in("g", 7)
-        copy_in("x", 7)
+        for s in range(8):
+            transpose_in("g", s)
+            if s == 0:
+                quantize_in(s, ("g",))
+            transpose_in("x", s)
+            quantize_in(s, ("x",) if s == 0 else ("g", "x"))
+            if s % 2 == 1:
+                negate(s // 2)
+            elif s > 0:
+                quantize_minus(s // 2 - 1)
         make_row_factors()
-        quantize_one("g", 0)
-        quantize_one("x", 0)
-        quantize_in(1)
-        negate(0)
-        quantize_in(2)
-        quantize_minus(0)
-        quantize_in(3)
-        negate(1)
-        quantize_in(4)
-        quantize_minus(1)
-        quantize_in(5)
-        negate(2)
-        quantize_in(6)
-        quantize_minus(2)
-        quantize_in(7)
-        negate(3)
         make_q_factor()
-        matmul_a(0, 0)
-        matmul_a(0, 1)
-        matmul_a(0, 4)
-        matmul_a(0, 5)
-        matmul_a(0, 6)
-        matmul_a(0, 7)
-        matmul_a(0, 2)
+
+        for s in (0, 1, 4, 5, 6, 7, 2):
+            matmul_a(0, s)
         vector_rl(0, 0)
         quantize_minus(3)
         vector_rl(0, 1)
-        vector_r(0, 4)
-        quantize_rl(0, 0, 0, 1)
-        vector_r(0, 5)
-        quantize_rl(0, 0, 2, 3)
-        vector_r(0, 6)
-        vector_r(0, 7)
-        quantize_rl(0, 1, 0, 2)
-        vector_rl(0, 2)
         scalar_eta(0, 0)
         scalar_eta(0, 1)
+        vector_r(0, 4)
+        quantize_rl(0, 0, 0, 1)
         copy_plain(4)
         scalar_l_plain(4, 1)
+        vector_r(0, 5)
+        quantize_rl(0, 0, 2, 3)
         copy_plain(5)
+        vector_r(0, 6)
         copy_plain(6)
         scalar_l_plain(5, 1)
+        vector_r(0, 7)
         copy_plain(7)
-        scalar_l_plain(6, 2)
-        scalar_eta(0, 2)
-        gpsimd_l(0, 2)
-        gpsimd_eta_wide(0, 0)
-        gpsimd_l(0, 3)
-        gpsimd_eta_wide(0, 1)
+        quantize_rl(0, 1, 0, 2)
+
         mirror_a(0)
         matmul_a(0, 3)
         mirror_a(1)
         matmul_a(1, 4)
-        matmul_a(1, 5)
-        matmul_a(1, 6)
-        matmul_a(1, 7)
+        scalar_l_plain(6, 2)
+        gpsimd_l(0, 2)
+        eta_source(0, nc.gpsimd)
+        gpsimd_l(0, 3)
+        eta_source(1, nc.gpsimd)
+        vector_rl(0, 2)
+        scalar_eta(0, 2)
         vector_r(1, 1)
         vector_r(1, 0)
-        vector_rl(0, 3)
-        vector_rl(1, 3)
-        vector_rl(1, 2)
-        vector_r(1, 5)
-        vector_r(1, 4)
-        quantize_rl(0, 0, 1, 2)
-        scalar_l(1, 1)
         scalar_l(1, 0)
+        scalar_l(1, 1)
+        gpsimd_l(1, 0)
+        vector_rl(0, 3)
         scalar_eta(0, 3)
+        matmul_a(1, 5)
         scalar_eta(1, 1)
         scalar_eta(1, 0)
-        scalar_eta(1, 3)
+        matmul_a(1, 6)
+        matmul_a(1, 7)
+        vector_rl(1, 3)
+        vector_rl(1, 2)
         scalar_eta(1, 2)
-        scalar_l(1, 5)
+        scalar_eta(1, 3)
+        vector_r(1, 5)
+        vector_r(1, 4)
+
+        quantize_rl(0, 0, 1, 2)
+        quantize_rl(0, 0, 3, 4)
+        quantize_rl(1, 0, 0, 4)
+        for k in range(2):
+            for sp in range(2):
+                matmul_q(0, sp, (k,))
+        eta_source(2, nc.gpsimd)
         scalar_l(1, 4)
+        scalar_l(1, 5)
         scalar_eta(1, 4)
         scalar_eta(1, 5)
-        gpsimd_l(1, 0)
-        gpsimd_eta_wide(0, 2)
-        gpsimd_l(1, 2)
-        quantize_rl(1, 0, 0, 4)
-        quantize_rl(0, 0, 3, 4)
         vector_r(1, 6)
         vector_r(1, 7)
         quantize_rl(0, 1, 2, 4)
         quantize_rl(1, 1, 0, 2)
+        matmul_q(1, 0)
+        gpsimd_l(1, 2)
         scalar_l(1, 7)
         scalar_l(1, 6)
+        gpsimd_l(1, 3)
         scalar_eta(1, 7)
         scalar_eta(1, 6)
-        scalar_eta_wide(0, 3)
-        gpsimd_l(1, 3)
-        matmul_q(0, 0)
-        matmul_q(0, 1)
-        matmul_q(1, 0)
-        combine(0, 0, 1)
-        combine(0, 0, 0)
-        combine(0, 1, 1)
-        combine(0, 1, 0)
-        combine(1, 0, 1)
-        combine(1, 0, 0)
-        quantize_rl(1, 1, 2, 4)
-        interleave_out(1, 0, nc.gpsimd, slice(0, 72))
-        transpose_out(0, 0, 0)
-        transpose_out(0, 0, 1)
+        eta_source(3, nc.scalar)
+
+        combine(0, 0)
+        transpose_out(0, 0)
         matmul_q(1, 1)
-        transpose_out(0, 1, 0)
-        transpose_out(0, 1, 1)
-        transpose_out(1, 0, 0)
-        transpose_out(1, 0, 1)
-        matmul_q(0, 2)
-        combine(1, 1, 1)
-        combine(1, 1, 0)
-        interleave_out(0, 1, nc.vector)
-        combine(0, 2, 1)
-        combine(0, 2, 0)
-        copy_rows(0, 0, 1, nc.scalar)
-        copy_rows(0, 0, 0, nc.scalar)
+        store_rows(0, 0)
         interleave_out(0, 0, nc.scalar)
-        copy_rows(0, 1, 1, nc.scalar)
-        copy_rows(0, 1, 0, nc.scalar)
-        copy_rows(1, 0, 1, nc.scalar)
-        copy_rows(1, 0, 0, nc.scalar)
-        interleave_out(1, 1, nc.gpsimd, slice(0, 128))
-        interleave_out(0, 2, nc.gpsimd, slice(0, 72))
-        store_rows(0, 0, 1)
-        store_rows(0, 0, 0)
-        store_rows(0, 1, 1)
-        store_rows(0, 1, 0)
-        store_rows(1, 0, 1)
-        store_rows(1, 0, 0)
-        transpose_out(1, 1, 0)
-        transpose_out(1, 1, 1)
+        combine(0, 1)
+        transpose_out(0, 1)
+        matmul_q(0, 2, (0,))
+        store_rows(0, 1)
+        combine(1, 0)
+        transpose_out(1, 0)
+        quantize_rl(1, 1, 2, 4)
+        matmul_q(0, 2, (1,))
+        interleave_out(1, 0, nc.gpsimd, 0, SHARE_FIRST)
+        store_rows(1, 0)
+        combine(1, 1)
+        transpose_out(1, 1)
         matmul_q(0, 3)
-        transpose_out(0, 2, 0)
-        transpose_out(0, 2, 1)
+        interleave_out(0, 1, nc.vector)
+        interleave_out(1, 1, nc.gpsimd)
+        store_rows(1, 1)
+        interleave_out(1, 0, nc.scalar, SHARE_FIRST, P)
+        combine(0, 2)
+        transpose_out(0, 2)
         matmul_q(1, 2)
-        quantize_out(0, 0, 512)
-        combine(0, 3, 1)
-        combine(0, 3, 0)
-        copy_rows(1, 1, 1, nc.scalar)
-        copy_rows(1, 1, 0, nc.scalar)
-        interleave_out(1, 0, nc.scalar, slice(72, 128))
-        copy_rows(0, 2, 1, nc.scalar)
-        copy_rows(0, 2, 0, nc.scalar)
-        interleave_out(0, 2, nc.scalar, slice(72, 128))
-        interleave_out(0, 3, nc.gpsimd, slice(0, 96))
-        store_rows(1, 1, 1)
-        store_rows(1, 1, 0)
-        store_words(0, 0, 512)
-        store_rows(0, 2, 1)
-        store_rows(0, 2, 0)
-        transpose_out(0, 3, 0)
-        transpose_out(0, 3, 1)
+        quantize_out(0, 0)
+        store_words(0, 0)
+        interleave_out(0, 2, nc.gpsimd, 0, SHARE_FIRST)
+        store_rows(0, 2)
+        interleave_out(0, 2, nc.scalar, SHARE_FIRST, P)
+        combine(0, 3)
+        transpose_out(0, 3)
         matmul_q_last(0)
-        quantize_out(1, 0, 512)
-        combine(1, 2, 1)
-        combine(1, 2, 0)
-        interleave_out(0, 3, nc.scalar, slice(96, 128))
-        copy_rows(0, 3, 1, nc.scalar)
-        copy_rows(0, 3, 0, nc.scalar)
-        interleave_out(1, 2, nc.gpsimd, slice(0, 64))
-        store_words(1, 0, 512)
-        store_rows(0, 3, 1)
-        store_rows(0, 3, 0)
-        transpose_out(1, 2, 0)
-        transpose_out(1, 2, 1)
+        quantize_out(1, 0)
+        store_words(1, 0)
+        interleave_out(0, 3, nc.gpsimd, 0, SHARE_SECOND)
+        interleave_out(0, 3, nc.scalar, SHARE_SECOND, P)
+        store_rows(0, 3)
+        combine(1, 2)
+        transpose_out(1, 2)
         matmul_q_last(1)
-        quantize_out(0, 512, 1024)
-        combine_last(0)
-        combine_last(1)
-        interleave_out(1, 2, nc.scalar, slice(64, 128))
-        copy_rows(1, 2, 1, nc.scalar)
-        copy_rows(1, 2, 0, nc.scalar)
-        interleave_out(1, 3, nc.gpsimd, slice(0, 64))
-        store_words(0, 512, 1024)
-        store_rows(1, 2, 1)
-        store_rows(1, 2, 0)
-        transpose_out(1, 3, 0)
-        transpose_out(1, 3, 1)
-        interleave_out(1, 3, nc.vector, slice(64, 128))
-        quantize_out(1, 512, 768)
-        quantize_out(1, 768, 1024)
-        copy_rows(1, 3, 0, nc.scalar)
-        copy_rows(1, 3, 1, nc.scalar)
+        quantize_out(0, 1)
+        store_words(0, 1)
+
+        interleave_out(1, 2, nc.gpsimd, 0, HALF)
+        interleave_out(1, 2, nc.scalar, HALF, P)
+        store_rows(1, 2)
+        for u in range(2):
+            combine_last(u)
+            transpose_out(1, 3, (u,))
+            store_rows(1, 3, (u,))
+            interleave_out(1, 3, (nc.gpsimd, nc.vector)[u], HALF * u, HALF * u + HALF)
+        for u in range(2):
+            quantize_out(1, 1, 256 * u, 256 * u + 256)
+        store_words(1, 1)
         store_scales()
-        store_rows(1, 3, 0)
-        store_rows(1, 3, 1)
-        store_words(1, 512, 1024)

@@ -18,6 +18,7 @@ P = 128
 FLOPS = 2 * 2 * N * N * N
 RSQRT2 = 1.0 / math.sqrt(2.0)
 PSUM_BANKS = 8
+EARLY_SLICES = 4
 L_ROWS_BUFS = 4
 Q_SCALE = 0.5 / 32.0
 SHARE_FIRST = 72
@@ -60,7 +61,8 @@ def tile_skewgradientquadraticstep_kernel(tc, x, g, c, d, eta, out_0, out_1, out
         for s in range(8):
             for op in ("g", "x"):
                 raw[op, s] = keep.tile([P, N], BF16, name="raw_%s%d" % (op, s), align_bytes=64)
-                nc.sync.dma_start(out=raw[op, s][:], in_=src[op][s // 4, s % 4])
+                queue = nc.scalar if op == "x" and s < EARLY_SLICES else nc.sync
+                queue.dma_start(out=raw[op, s][:], in_=src[op][s // 4, s % 4])
         vecs = keep.tile([P, 3, 16], BF16, name="vecs")
         for v, vec in enumerate((c, d, eta)):
             nc.sync.dma_start(

@@ -12,6 +12,7 @@ U8 = mybir.dt.uint8
 FP8X4 = mybir.dt.float8_e4m3fn_x4
 ALU = mybir.AluOpType
 COPY = mybir.ActivationFunctionType.Copy
+SQUARE = mybir.ActivationFunctionType.Square
 
 N = 1024
 P = 128
@@ -24,17 +25,17 @@ Q_SCALE = 0.5 / 32.0
 SHARE_FIRST = 72
 SHARE_SECOND = 96
 HALF = 64
+LAST_PAIR = 1
+LAST_HALF = 0
+FIRST_PLANE = (1, 1)
 
+WHOLE = ((0, 1), (1, 0))
 SLOT = {
-    ("minus", 0): "a", ("minus", 2): "a", ("planes", 0, 0): "a", ("planes", 0, 1): "a", ("planes", 1, 1): "a",
-    ("minus", 1): "b", ("minus", 3): "b",
-    ("rl", 0): "c",
-    ("rl", 1): "d", ("eta", 2): "d",
-    ("r", 0): "e", ("l", 0): "e",
-    ("r", 1): "f", ("l", 1): "f", ("planes", 1, 0): "f",
-    ("eta", 0): "g",
-    ("eta", 1): "h",
-    ("eta", 3): "i",
+    ("minus", 0): "a", ("minus", 2): "a", ("r", 1, 1): "a", ("planes", 1, 1, 0): "a",
+    ("minus", 1): "b", ("minus", 3): "b", ("r", 0, 0): "b", ("planes", 0, 0): "b",
+    ("rl", 0, 1): "c", ("planes", 1, 0): "c",
+    ("rl", 1, 0): "d", ("planes", 0, 1): "d",
+    ("l", 1, 1, 2): "e", ("l", 1, 1, 3): "e", ("l", 0, 0, 2): "e", ("l", 0, 0, 3): "e", ("planes", 1, 1, 1): "e",
 }
 
 
@@ -43,11 +44,11 @@ def tile_skewgradientquadraticstep_kernel(tc, x, g, c, d, eta, out_0, out_1, out
     with ExitStack() as ctx:
         keep = ctx.enter_context(tc.tile_pool(name="keep", bufs=1))
         work = ctx.enter_context(tc.tile_pool(name="work", bufs=2))
-        psum = ctx.enter_context(tc.psum_pool(name="psum", bufs=PSUM_BANKS))
+        psum = ctx.enter_context(tc.psum_pool(name="psum", bufs=1))
         ctx.enter_context(tc.manual_schedule())
 
-        def new_bank():
-            return psum.tile([P, 512], F32, name="bank")
+        def new_bank(index):
+            return psum.tile([P, 512], F32, name="bank", tag="bank_%d" % index)
 
         shared = {}
 
@@ -79,9 +80,7 @@ def tile_skewgradientquadraticstep_kernel(tc, x, g, c, d, eta, out_0, out_1, out
                 nc.scalar.activation(out=row_factor[:, rows, :], in_=vecs[:, first:last, 0:8], func=COPY, scale=sign * RSQRT2)
 
         def make_q_factor():
-            nc.vector.scalar_tensor_tensor(
-                out=q_factor[:], in0=vecs[:, 2, 0:8], scalar=Q_SCALE, in1=vecs[:, 2, 0:8], op0=ALU.mult, op1=ALU.mult
-            )
+            nc.scalar.activation(out=q_factor[:], in_=vecs[:, 2, 0:8], func=SQUARE, scale=math.sqrt(Q_SCALE))
 
         def factor(h, s):
             return row_factor[:, 3:6, 4:8] if h == 1 and s < 4 else row_factor[:, 0:3, 4 * h : 4 * h + 4]
@@ -90,7 +89,7 @@ def tile_skewgradientquadraticstep_kernel(tc, x, g, c, d, eta, out_0, out_1, out
 
         def transpose_in(op, s):
             words = raw[op, s][:].bitcast(F32)
-            bank = new_bank()
+            bank = new_bank((2 * s + (op == "x")) % PSUM_BANKS)
             for h in range(2):
                 for u in range(2):
                     lo = 128 * (2 * h + u)
@@ -133,15 +132,15 @@ def tile_skewgradientquadraticstep_kernel(tc, x, g, c, d, eta, out_0, out_1, out
         a_bank, l_rows, eta_a, rl_codes, rl_scales = {}, {}, {}, {}, {}
         for h in range(2):
             for sp in range(4):
-                if h == 1 or sp < 2:
+                if True:
                     eta_a[h, sp] = keep.tile([P, 4, 256], F32, name="eta_a_%d%d" % (h, sp))
             for hp in range(2):
                 rl_codes[h, hp] = keep.tile([P, 1024], U32, name="rl_codes_%d%d" % (h, hp), align_bytes=64)
                 rl_scales[h, hp] = keep.tile([P, 1024], U8, name="rl_scales_%d%d" % (h, hp), align_bytes=64)
         plain = keep.tile([P, 4, 512], F32, name="plain")
 
-        def matmul_a(h, s):
-            a_bank[h, s] = new_bank()
+        def matmul_a(h, s, index):
+            a_bank[h, s] = new_bank(index)
             passes = [(left, right, k) for left, right in (("g", "x"), ("minus_x", "g")) for k in range(2)]
             for t in range(4):
                 for step, (left, right, k) in enumerate(passes):
@@ -158,21 +157,17 @@ def tile_skewgradientquadraticstep_kernel(tc, x, g, c, d, eta, out_0, out_1, out
         def copy_plain(s):
             nc.scalar.copy(out=plain[:, s - 4, :], in_=a_bank[0, s][:])
 
-        def mirror_a(sp):
-            for s in (2 * sp, 2 * sp + 1):
-                a_bank[1, s] = new_bank()
+        def mirror_a(s, index):
+            a_bank[1, s] = new_bank(index)
             for t in range(4):
-                for s in (2 * sp, 2 * sp + 1):
-                    nc.tensor.transpose(
-                        a_bank[1, s][:, 128 * t : 128 * t + 128], plain[:, t, 128 * s : 128 * s + 128], ident[:]
-                    )
+                nc.tensor.transpose(a_bank[1, s][:, 128 * t : 128 * t + 128], plain[:, t, 128 * s : 128 * s + 128], ident[:])
 
         def rl_part(h, hp, first, last):
-            if hp == 0:
-                return slot_tile(("rl", h), [P, 4096], BF16)[:, 1024 * first : 1024 * last]
+            if (h, hp) in WHOLE:
+                return slot_tile(("rl", h, hp), [P, 4096], BF16)[:, 1024 * first : 1024 * last]
             if first < 2:
-                return slot_tile(("r", h), [P, 2048], BF16)[:, 1024 * first : 1024 * last]
-            return slot_tile(("l", h), [P, 2048], BF16)[:, 1024 * (first - 2) : 1024 * (last - 2)]
+                return slot_tile(("r", h, hp), [P, 2048], BF16)[:, 1024 * first : 1024 * last]
+            return slot_tile(("l", h, hp, first), [P, 1024], BF16)[:]
 
         def vector_r(h, s):
             lo = 512 * (s % 4)
@@ -184,10 +179,29 @@ def tile_skewgradientquadraticstep_kernel(tc, x, g, c, d, eta, out_0, out_1, out
             )
 
         def vector_rl(h, s):
+            col = 128 * (s % 4)
             nc.vector.tensor_tensor(
-                out=rl_part(h, 0, 0, 4).rearrange("p (o n t) -> p o n t", o=2, t=4)[:, :, 128 * s : 128 * s + 128, :],
+                out=rl_part(h, s // 4, 0, 4).rearrange("p (o n t) -> p o n t", o=2, t=4)[:, :, col : col + 128, :],
                 in0=a_bank[h, s][:].rearrange("p (t n) -> p n t", t=4).unsqueeze(1).to_broadcast([P, 2, 128, 4]),
                 in1=factor(h, s)[:, 0:2, :].unsqueeze(2).to_broadcast([P, 2, 128, 4]),
+                op=ALU.mult,
+            )
+
+        def vector_l_halves(h, s):
+            quarter = 2 + LAST_PAIR % 2
+            nc.vector.tensor_tensor(
+                out=rl_part(h, s // 4, quarter, quarter + 1).rearrange("p (u a m t) -> p a u m t", u=2, a=2, t=4)[:, s % 2],
+                in0=a_bank[h, s][:].rearrange("p (t u m) -> p u m t", t=4, u=2),
+                in1=factor(h, s)[:, 1:2, :].unsqueeze(1).to_broadcast([P, 2, HALF, 4]),
+                op=ALU.mult,
+            )
+
+        def gpsimd_l_plain(first, count):
+            lo = 512 * (first - 4)
+            nc.gpsimd.tensor_tensor(
+                out=rl_part(0, 1, 2, 4)[:, lo : lo + 512 * count].rearrange("p (a n t) -> p a n t", a=count, t=4),
+                in0=plain[:, first - 4 : first - 4 + count, :].rearrange("p a (t n) -> p a n t", t=4),
+                in1=factor(0, 4)[:, 1:2, :].unsqueeze(1).to_broadcast([P, count, 128, 4]),
                 op=ALU.mult,
             )
 
@@ -198,7 +212,7 @@ def tile_skewgradientquadraticstep_kernel(tc, x, g, c, d, eta, out_0, out_1, out
         def l_columns(h, first, count):
             if (h, first // 2) not in l_rows:
                 l_rows[h, first // 2] = work.tile([P, 4, 256], BF16, name="l_rows", align_bytes=64, bufs=L_ROWS_BUFS)
-            order = "p t (u a m) -> p t a u m" if first >= 6 else "p t (a u m) -> p t a u m"
+            order = "p t (u a m) -> p t a u m" if first // 2 == LAST_PAIR else "p t (a u m) -> p t a u m"
             return l_rows[h, first // 2][:].rearrange(order, u=2, a=2)[:, :, first % 2 : first % 2 + count]
 
         def scalar_l(h, s):
@@ -221,6 +235,20 @@ def tile_skewgradientquadraticstep_kernel(tc, x, g, c, d, eta, out_0, out_1, out
         def gpsimd_l(h, sp):
             out = rl_part(h, sp // 2, 2 + sp % 2, 3 + sp % 2).rearrange("p (n t) -> p n t", t=4)
             gpsimd_move(out, l_rows[h, sp][:].rearrange("p t n -> p n t"))
+
+        def scalar_eta_plain(s):
+            col = 128 * (s % 2)
+            scale_rows(
+                lambda t: eta_a[0, s // 2][:, t, col : col + 128], lambda t: plain[:, s - 4, 128 * t : 128 * t + 128], 0, s, 2
+            )
+
+        def gpsimd_eta_plain(sp):
+            for t in range(4):
+                gpsimd_move(
+                    eta_a[0, sp][:, t, :].rearrange("p (a n) -> p a n", a=2),
+                    plain[:, 2 * sp - 4 : 2 * sp - 2, 128 * t : 128 * t + 128],
+                    factor(0, 4)[:, 2, t : t + 1],
+                )
 
         def eta_source(t, engine):
             out = slot_tile(("eta", t), [P, 512], F32)[:].rearrange("p (s n) -> p s n", s=4)
@@ -252,21 +280,21 @@ def tile_skewgradientquadraticstep_kernel(tc, x, g, c, d, eta, out_0, out_1, out
                 stop=stop,
             )
 
-        def matmul_q(h, sp, k_halves=(0, 1)):
+        def matmul_q(h, sp, banks, k_halves=(0, 1), first_k=0):
             rows = slice(512 + 256 * (sp % 2), 768 + 256 * (sp % 2))
             for k in k_halves:
                 for t in range(4):
-                    if k == 0 and t % 2 == 0:
-                        q_bank[h, sp, t // 2] = new_bank()
+                    if k == first_k and t % 2 == 0:
+                        q_bank[h, sp, t // 2] = new_bank(banks[t // 2])
                     out = q_bank[h, sp, t // 2][:, 256 * (t % 2) : 256 * (t % 2) + 256]
-                    q_pass(out, h, sp, t, k, rows, k == 0 and t % 2 == 0, k == 1 and t % 2 == 1)
+                    q_pass(out, h, sp, t, k, rows, k == first_k and t % 2 == 0, k != first_k and t % 2 == 1)
 
-        def matmul_q_last(u):
-            q_bank[1, 3, u] = new_bank()
+        def matmul_q_last(u, index):
+            q_bank["last", u] = new_bank(index)
             rows = slice(768 + 128 * u, 896 + 128 * u)
             for t in range(4):
                 for k in range(2):
-                    q_pass(q_bank[1, 3, u][:, 128 * t : 128 * t + 128], 1, 3, t, k, rows, k == 0, k == 1)
+                    q_pass(q_bank["last", u][:, 128 * t : 128 * t + 128], LAST_HALF, LAST_PAIR, t, k, rows, k == 0, k == 1)
 
         def unit_t(h, sp):
             if (h, sp // 2) not in out_t:
@@ -274,7 +302,7 @@ def tile_skewgradientquadraticstep_kernel(tc, x, g, c, d, eta, out_0, out_1, out
             return out_t[h, sp // 2][:, 1024 * (sp % 2) : 1024 * (sp % 2) + 1024].rearrange("p (t n) -> p t n", t=4)
 
         def combine_lane(h, sp, t, q, ms):
-            first = shared["eta", t][:, 256 * sp - 512 : 256 * sp - 256] if h == 0 and sp >= 2 else eta_a[h, sp][:, t, :]
+            first = eta_a[h, sp][:, t, :]
             nc.vector.scalar_tensor_tensor(
                 out=unit_t(h, sp)[:, t, :].rearrange("p (m a) -> p m a", a=2)[:, ms, :],
                 in0=q.rearrange("p (a m) -> p m a", a=2),
@@ -284,10 +312,10 @@ def tile_skewgradientquadraticstep_kernel(tc, x, g, c, d, eta, out_0, out_1, out
                 op1=ALU.add,
             )
 
-        def combine(h, sp):
-            for t in (2, 3, 0, 1):
+        def combine(h, sp, lanes=(2, 3, 0, 1)):
+            for t in lanes:
                 q = q_bank[h, sp, t // 2][:, 256 * (t % 2) : 256 * (t % 2) + 256]
-                if sp < 3:
+                if sp != LAST_PAIR:
                     combine_lane(h, sp, t, q, slice(0, P))
                 else:
                     for u in range(2):
@@ -295,14 +323,22 @@ def tile_skewgradientquadraticstep_kernel(tc, x, g, c, d, eta, out_0, out_1, out
 
         def combine_last(u):
             for t in range(4):
-                combine_lane(1, 3, t, q_bank[1, 3, u][:, 128 * t : 128 * t + 128], slice(HALF * u, HALF * u + HALF))
+                combine_lane(LAST_HALF, LAST_PAIR, t, q_bank["last", u][:, 128 * t : 128 * t + 128], slice(HALF * u, HALF * u + HALF))
 
-        def planes_tile(h, hp):
-            return slot_tile(("planes", h, hp), [P, 2048], BF16)
+        def planes_tile(h, hp, u):
+            if (h, hp) == FIRST_PLANE:
+                return slot_tile(("planes", h, hp, u), [P, 1024], BF16)[:]
+            return slot_tile(("planes", h, hp), [P, 2048], BF16)[:, 1024 * u : 1024 * u + 1024]
+
+        def planes_part(h, hp, first, last):
+            if (h, hp) == FIRST_PLANE:
+                u = first // HALF
+                return planes_tile(h, hp, u)[:, 16 * (first - HALF * u) : 16 * (last - HALF * u)]
+            return slot_tile(("planes", h, hp), [P, 2048], BF16)[:, 16 * first : 16 * last]
 
         def interleave_out(h, sp, engine, first=0, last=P):
             lo = 2 * (sp % 2)
-            out = planes_tile(h, sp // 2)[:].rearrange("p (m a t) -> p m t a", a=4, t=4)[:, first:last, :, lo : lo + 2]
+            out = planes_part(h, sp // 2, first, last).rearrange("p (m a t) -> p m t a", a=4, t=4)[:, :, :, lo : lo + 2]
             in_ = unit_t(h, sp).rearrange("p t (m a) -> p m t a", a=2)[:, first:last]
             if engine is nc.vector:
                 nc.vector.tensor_copy(out=out, in_=in_)
@@ -317,7 +353,7 @@ def tile_skewgradientquadraticstep_kernel(tc, x, g, c, d, eta, out_0, out_1, out
             nc.vector.quantize_mx(
                 out=out_words[h, hp][:, first:last].bitcast(FP8X4),
                 scales=out_scales[4 * h : P, 512 * hp + first : 512 * hp + last],
-                in_=planes_tile(h, hp)[:, 4 * first : 4 * last],
+                in_=planes_part(h, hp, first // 4, last // 4),
             )
 
         def store_words(h, hp):
@@ -333,19 +369,19 @@ def tile_skewgradientquadraticstep_kernel(tc, x, g, c, d, eta, out_0, out_1, out
                     in_=out_scales[32 * quad : 32 * quad + 8, :].bitcast(I32),
                 )
 
-        def transpose_out(h, sp, halves=(0, 1)):
-            for u in halves:
-                out_bank[h, sp, u] = new_bank()
+        def transpose_out(h, sp, banks, halves=(0, 1)):
+            for u, index in zip(halves, banks):
+                out_bank[h, sp, u] = new_bank(index)
                 for t in range(4):
                     nc.tensor.transpose(
                         out_bank[h, sp, u][:, 128 * t : 128 * t + 128], unit_t(h, sp)[:, t, 128 * u : 128 * u + 128], ident[:]
                     )
 
-        def store_rows(h, sp, halves=(1, 0)):
+        def store_rows(h, sp, halves=(1, 0), engine=nc.scalar):
             lo = 2 * (sp % 2)
             for u in halves:
                 rows = keep.tile([P, 512], F32, name="rows_%d%d%d" % (h, sp, u), align_bytes=64)
-                nc.scalar.copy(
+                (nc.scalar.copy if engine is nc.scalar else nc.vector.tensor_copy)(
                     out=rows[:].rearrange("m (p t) -> m p t", t=4),
                     in_=out_bank[h, sp, u][:].rearrange("m (t p) -> m p t", t=4),
                 )
@@ -364,134 +400,145 @@ def tile_skewgradientquadraticstep_kernel(tc, x, g, c, d, eta, out_0, out_1, out
         make_row_factors()
         make_q_factor()
 
-        for s in (0, 1, 4, 5, 6, 7, 2):
-            matmul_a(0, s)
-        vector_rl(0, 0)
+        for s in range(4, 8):
+            matmul_a(0, s, s - 4)
         quantize_minus(3)
-        vector_rl(0, 1)
-        scalar_eta(0, 0)
-        scalar_eta(0, 1)
-        vector_r(0, 4)
-        quantize_rl(0, 0, 0, 1)
+        matmul_a(1, 4, 4)
         copy_plain(4)
-        scalar_l_plain(4, 1)
-        vector_r(0, 5)
-        quantize_rl(0, 0, 2, 3)
+        vector_rl(0, 4)
         copy_plain(5)
-        vector_r(0, 6)
+        vector_rl(0, 5)
+        scalar_eta_plain(4)
         copy_plain(6)
-        scalar_l_plain(5, 1)
-        vector_r(0, 7)
+        vector_r(0, 6)
+        scalar_eta_plain(5)
+        quantize_rl(0, 1, 0, 1)
+        quantize_rl(0, 1, 2, 3)
         copy_plain(7)
-        quantize_rl(0, 1, 0, 2)
-
-        mirror_a(0)
-        matmul_a(0, 3)
-        mirror_a(1)
-        matmul_a(1, 4)
-        scalar_l_plain(6, 2)
-        gpsimd_l(0, 2)
-        eta_source(0, nc.gpsimd)
-        gpsimd_l(0, 3)
-        eta_source(1, nc.gpsimd)
-        vector_rl(0, 2)
-        scalar_eta(0, 2)
-        vector_r(1, 1)
-        vector_r(1, 0)
-        scalar_l(1, 0)
-        scalar_l(1, 1)
-        gpsimd_l(1, 0)
-        vector_rl(0, 3)
-        scalar_eta(0, 3)
-        matmul_a(1, 5)
-        scalar_eta(1, 1)
-        scalar_eta(1, 0)
-        matmul_a(1, 6)
-        matmul_a(1, 7)
-        vector_rl(1, 3)
-        vector_rl(1, 2)
-        scalar_eta(1, 2)
-        scalar_eta(1, 3)
-        vector_r(1, 5)
+        vector_r(0, 7)
+        gpsimd_l_plain(6, 2)
+        for s, index in zip(range(4), (5, 6, 7, 0)):
+            mirror_a(s, index)
+        matmul_a(1, 5, 1)
+        matmul_a(1, 6, 2)
+        matmul_a(1, 7, 3)
+        scalar_eta_plain(6)
+        scalar_eta_plain(7)
         vector_r(1, 4)
-
-        quantize_rl(0, 0, 1, 2)
-        quantize_rl(0, 0, 3, 4)
-        quantize_rl(1, 0, 0, 4)
-        for k in range(2):
-            for sp in range(2):
-                matmul_q(0, sp, (k,))
-        eta_source(2, nc.gpsimd)
         scalar_l(1, 4)
-        scalar_l(1, 5)
         scalar_eta(1, 4)
+        vector_rl(1, 0)
+        scalar_eta(1, 0)
+        vector_rl(1, 1)
+        vector_r(1, 5)
+        scalar_eta(1, 1)
+        scalar_l(1, 5)
+        quantize_rl(0, 1, 1, 2)
+        quantize_rl(0, 1, 3, 4)
+        gpsimd_l(1, 2)
         scalar_eta(1, 5)
         vector_r(1, 6)
+        vector_r(1, 2)
         vector_r(1, 7)
-        quantize_rl(0, 1, 2, 4)
-        quantize_rl(1, 1, 0, 2)
-        matmul_q(1, 0)
-        gpsimd_l(1, 2)
-        scalar_l(1, 7)
         scalar_l(1, 6)
+        scalar_l(1, 7)
+        matmul_a(0, 0, 4)
+        matmul_a(0, 1, 5)
+        vector_l_halves(1, 2)
+        quantize_rl(1, 1, 0, 2)
+        quantize_rl(1, 1, 2, 3)
         gpsimd_l(1, 3)
-        scalar_eta(1, 7)
         scalar_eta(1, 6)
-        eta_source(3, nc.scalar)
-
-        combine(0, 0)
-        transpose_out(0, 0)
-        matmul_q(1, 1)
-        store_rows(0, 0)
-        interleave_out(0, 0, nc.scalar)
-        combine(0, 1)
-        transpose_out(0, 1)
-        matmul_q(0, 2, (0,))
-        store_rows(0, 1)
-        combine(1, 0)
-        transpose_out(1, 0)
-        quantize_rl(1, 1, 2, 4)
-        matmul_q(0, 2, (1,))
-        interleave_out(1, 0, nc.gpsimd, 0, SHARE_FIRST)
-        store_rows(1, 0)
-        combine(1, 1)
-        transpose_out(1, 1)
-        matmul_q(0, 3)
-        interleave_out(0, 1, nc.vector)
-        interleave_out(1, 1, nc.gpsimd)
-        store_rows(1, 1)
-        interleave_out(1, 0, nc.scalar, SHARE_FIRST, P)
+        scalar_eta(1, 7)
+        matmul_q(1, 2, (6, 1))
+        matmul_a(0, 2, 2)
+        vector_r(1, 3)
+        vector_l_halves(1, 3)
+        scalar_eta(1, 2)
+        scalar_eta(1, 3)
+        combine(1, 2, (2, 3))
+        quantize_rl(1, 1, 3, 4)
+        matmul_q(1, 3, (3, 7))
+        combine(1, 2, (0, 1))
+        scalar_l(0, 0)
+        scalar_l(0, 1)
+        quantize_rl(1, 0, 0, 4)
+        gpsimd_l(0, 0)
+        scalar_eta(0, 0)
+        scalar_eta(0, 1)
+        transpose_out(1, 2, (0, 6))
+        matmul_a(0, 3, 1)
+        combine(1, 3)
+        interleave_out(1, 2, nc.gpsimd, 0, HALF)
+        scalar_l(0, 2)
+        scalar_l(0, 3)
+        store_rows(1, 2)
+        vector_r(0, 0)
+        vector_r(0, 1)
+        matmul_q(1, 0, (3, 7), (1,), 1)
+        transpose_out(1, 3, (4, 5))
+        quantize_rl(0, 0, 2, 3)
+        gpsimd_l(0, 1)
+        matmul_q(1, 0, (3, 7), (0,), 1)
+        matmul_q(0, 2, (0, 6), (1,), 1)
+        vector_r(0, 2)
+        vector_r(0, 3)
+        store_rows(1, 3)
+        combine(1, 0, (2, 3))
+        quantize_rl(0, 0, 0, 2)
+        quantize_rl(0, 0, 3, 4)
+        interleave_out(1, 3, nc.gpsimd, HALF, P)
+        matmul_q(0, 3, (4, 5), (1,), 1)
+        matmul_q(0, 2, (0, 6), (0,), 1)
+        matmul_q(0, 3, (4, 5), (0,), 1)
+        scalar_eta(0, 2)
+        scalar_eta(0, 3)
+        interleave_out(1, 3, nc.scalar, 0, HALF)
+        interleave_out(1, 2, nc.scalar, HALF, P)
+        combine(1, 0, (0, 1))
+        interleave_out(1, 0, nc.gpsimd, 0, 112)
+        transpose_out(1, 0, (2, 1))
         combine(0, 2)
-        transpose_out(0, 2)
-        matmul_q(1, 2)
-        quantize_out(0, 0)
-        store_words(0, 0)
-        interleave_out(0, 2, nc.gpsimd, 0, SHARE_FIRST)
+        matmul_q(1, 1, (3, 7))
+        store_rows(1, 0)
+        interleave_out(0, 2, nc.scalar, 0, 80)
+        transpose_out(0, 2, (0, 6))
+        combine(0, 3, (2, 3, 0))
+        quantize_out(1, 1, 0, 256)
+        combine(0, 3, (1,))
+        quantize_out(1, 1, 256, 512)
+        store_words(1, 1)
+        transpose_out(0, 3, (4, 5))
+        interleave_out(0, 3, nc.gpsimd)
+        interleave_out(0, 2, nc.gpsimd, 80, P)
+        matmul_q(0, 0, (2, 1))
         store_rows(0, 2)
-        interleave_out(0, 2, nc.scalar, SHARE_FIRST, P)
-        combine(0, 3)
-        transpose_out(0, 3)
-        matmul_q_last(0)
+        combine(1, 1)
+        store_rows(0, 3)
+        transpose_out(1, 1, (3, 7))
+        matmul_q_last(0, 0)
+        matmul_q_last(1, 6)
+        interleave_out(1, 0, nc.scalar, 112, P)
+        interleave_out(1, 1, nc.scalar, 0, 48)
+        combine(0, 0)
+        quantize_out(0, 1)
+        interleave_out(0, 0, nc.gpsimd, 0, HALF)
+        store_rows(1, 1)
+        store_words(0, 1)
+        interleave_out(1, 1, nc.scalar, 48, P)
+        transpose_out(0, 0, (2, 1))
+        combine_last(0)
+        interleave_out(0, 1, nc.gpsimd, 0, HALF)
+        transpose_out(0, 1, (4,), (0,))
+        combine_last(1)
+        transpose_out(0, 1, (5,), (1,))
+        store_rows(0, 0)
+        store_rows(0, 1, (0,), nc.vector)
+        interleave_out(0, 0, nc.vector, HALF, P)
+        interleave_out(0, 1, nc.vector, HALF, P)
         quantize_out(1, 0)
         store_words(1, 0)
-        interleave_out(0, 3, nc.gpsimd, 0, SHARE_SECOND)
-        interleave_out(0, 3, nc.scalar, SHARE_SECOND, P)
-        store_rows(0, 3)
-        combine(1, 2)
-        transpose_out(1, 2)
-        matmul_q_last(1)
-        quantize_out(0, 1)
-        store_words(0, 1)
-
-        interleave_out(1, 2, nc.gpsimd, 0, HALF)
-        interleave_out(1, 2, nc.scalar, HALF, P)
-        store_rows(1, 2)
-        for u in range(2):
-            combine_last(u)
-            transpose_out(1, 3, (u,))
-            store_rows(1, 3, (u,))
-            interleave_out(1, 3, (nc.gpsimd, nc.vector)[u], HALF * u, HALF * u + HALF)
-        for u in range(2):
-            quantize_out(1, 1, 256 * u, 256 * u + 256)
-        store_words(1, 1)
+        store_rows(0, 1, (1,))
+        quantize_out(0, 0)
+        store_words(0, 0)
         store_scales()

@@ -364,7 +364,7 @@ def tile_skewgradientquadraticstep_kernel(tc, x, g, c, d, eta, out_0, out_1, out
 
         def store_scales():
             for quad in range(4):
-                nc.scalar.dma_start(
+                (nc.scalar if quad % 2 else nc.sync).dma_start(
                     out=out_2[:, 4 * quad : 4 * quad + 4, :].bitcast(I32),
                     in_=out_scales[32 * quad : 32 * quad + 8, :].bitcast(I32),
                 )

@@ -510,35 +510,35 @@ def tile_skewgradientquadraticstep_kernel(tc, x, g, c, d, eta, out_0, out_1, out
         store_words(1, 1)
         transpose_out(0, 3, (4, 5))
         interleave_out(0, 3, nc.gpsimd)
-        interleave_out(0, 2, nc.gpsimd, 80, P)
         matmul_q(0, 0, (2, 1))
         store_rows(0, 2)
         combine(1, 1)
-        store_rows(0, 3)
+        interleave_out(1, 1, nc.gpsimd)
+        store_rows(0, 3, (1,))
+        store_rows(0, 3, (0,), nc.vector)
         transpose_out(1, 1, (3, 7))
         matmul_q_last(0, 0)
         matmul_q_last(1, 6)
         interleave_out(1, 0, nc.scalar, 112, P)
-        interleave_out(1, 1, nc.scalar, 0, 48)
+        interleave_out(0, 2, nc.scalar, 80, P)
         combine(0, 0)
         quantize_out(0, 1)
-        interleave_out(0, 0, nc.gpsimd, 0, HALF)
+        quantize_out(1, 0)
         store_rows(1, 1)
         store_words(0, 1)
-        interleave_out(1, 1, nc.scalar, 48, P)
+        store_words(1, 0)
+        interleave_out(0, 0, nc.scalar)
         transpose_out(0, 0, (2, 1))
         combine_last(0)
-        interleave_out(0, 1, nc.gpsimd, 0, HALF)
         transpose_out(0, 1, (4,), (0,))
         combine_last(1)
         transpose_out(0, 1, (5,), (1,))
         store_rows(0, 0)
-        store_rows(0, 1, (0,), nc.vector)
-        interleave_out(0, 0, nc.vector, HALF, P)
+        interleave_out(0, 1, nc.vector, 0, HALF)
         interleave_out(0, 1, nc.vector, HALF, P)
-        quantize_out(1, 0)
-        store_words(1, 0)
+        store_rows(0, 1, (0,))
+        quantize_out(0, 0, 0, 256)
+        quantize_out(0, 0, 256, 512)
         store_rows(0, 1, (1,))
-        quantize_out(0, 0)
         store_words(0, 0)
         store_scales()

from contextlib import ExitStack
import math

import concourse.mybir as mybir
from concourse.masks import make_identity

F32 = mybir.dt.float32
BF16 = mybir.dt.bfloat16
I32 = mybir.dt.int32
U32 = mybir.dt.uint32
U8 = mybir.dt.uint8
FP8X4 = mybir.dt.float8_e4m3fn_x4
ALU = mybir.AluOpType
COPY = mybir.ActivationFunctionType.Copy
SQUARE = mybir.ActivationFunctionType.Square

N = 1024
P = 128
FLOPS = 2 * 2 * N * N * N
RSQRT2 = 1.0 / math.sqrt(2.0)
PSUM_BANKS = 8
EARLY_SLICES = 4
L_ROWS_BUFS = 4
Q_SCALE = 0.5 / 32.0
SHARE_FIRST = 72
SHARE_SECOND = 96
HALF = 64
LAST_PAIR = 1
LAST_HALF = 0
FIRST_PLANE = (1, 1)

WHOLE = ((0, 1), (1, 0))
SLOT = {
    ("minus", 0): "a", ("minus", 2): "a", ("r", 1, 1): "a", ("planes", 1, 1, 0): "a",
    ("minus", 1): "b", ("minus", 3): "b", ("r", 0, 0): "b", ("planes", 0, 0): "b",
    ("rl", 0, 1): "c", ("planes", 1, 0): "c",
    ("rl", 1, 0): "d", ("planes", 0, 1): "d",
    ("l", 1, 1, 2): "e", ("l", 1, 1, 3): "e", ("l", 0, 0, 2): "e", ("l", 0, 0, 3): "e", ("planes", 1, 1, 1): "e",
}


def tile_skewgradientquadraticstep_kernel(tc, x, g, c, d, eta, out_0, out_1, out_2):
    nc = tc.nc
    with ExitStack() as ctx:
        keep = ctx.enter_context(tc.tile_pool(name="keep", bufs=1))
        work = ctx.enter_context(tc.tile_pool(name="work", bufs=2))
        psum = ctx.enter_context(tc.psum_pool(name="psum", bufs=1))
        ctx.enter_context(tc.manual_schedule())

        def new_bank(index):
            return psum.tile([P, 512], F32, name="bank", tag="bank_%d" % index)

        shared = {}

        def slot_tile(key, shape, dtype):
            if key not in shared:
                shared[key] = keep.tile(shape, dtype, name=key[0], tag="slot_" + SLOT[key], align_bytes=64)
            return shared[key]

        src = {"x": x.rearrange("(h m t) k -> h t m k", h=2, t=4), "g": g.rearrange("(h m t) k -> h t m k", h=2, t=4)}
        raw = {}
        for s in range(8):
            for op in ("g", "x"):
                raw[op, s] = keep.tile([P, N], BF16, name="raw_%s%d" % (op, s), align_bytes=64)
                queue = nc.scalar if op == "x" and s < EARLY_SLICES else nc.sync
                queue.dma_start(out=raw[op, s][:], in_=src[op][s // 4, s % 4])
        vecs = keep.tile([P, 3, 16], BF16, name="vecs")
        for v, vec in enumerate((c, d, eta)):
            nc.sync.dma_start(
                out=vecs[:, v, 0:8].rearrange("p (h t) -> p h t", h=2), in_=vec.rearrange("(h p t) -> p h t", h=2, t=4)
            )
        ident = keep.tile([P, P], F32, name="ident")
        make_identity(nc, ident[:])

        row_factor = keep.tile([P, 6, 8], F32, name="row_factor")
        q_factor = keep.tile([P, 8], F32, name="q_factor")

        def make_row_factors():
            for rows, first, last, sign in ((slice(1, 6, 2), 0, 3, -1.0), (slice(0, 3, 2), 1, 3, 1.0), (slice(4, 5), 0, 1, 1.0)):
                nc.scalar.activation(out=row_factor[:, rows, :], in_=vecs[:, first:last, 0:8], func=COPY, scale=sign * RSQRT2)

        def make_q_factor():
            nc.scalar.activation(out=q_factor[:], in_=vecs[:, 2, 0:8], func=SQUARE, scale=math.sqrt(Q_SCALE))

        def factor(h, s):
            return row_factor[:, 3:6, 4:8] if h == 1 and s < 4 else row_factor[:, 0:3, 4 * h : 4 * h + 4]

        codes, scales, turned = {}, {}, {}

        def transpose_in(op, s):
            words = raw[op, s][:].bitcast(F32)
            bank = new_bank((2 * s + (op == "x")) % PSUM_BANKS)
            for h in range(2):
                for u in range(2):
                    lo = 128 * (2 * h + u)
                    nc.tensor.transpose(bank[:, lo : lo + 128], words[:, 256 * h + u : 256 * h + 256 : 2], ident[:])
            if s // 2 not in turned:
                turned[s // 2] = keep.tile([P, 4 * N], BF16, name="turned", tag="wide_%d" % (s // 2), align_bytes=64)
            lo = N * (2 * (s % 2) + (op == "x"))
            nc.scalar.copy(
                out=turned[s // 2][:, lo : lo + N].bitcast(F32).rearrange("p (h m u) -> p h m u", h=2, u=2),
                in_=bank[:].rearrange("p (h u m) -> p h m u", h=2, u=2),
            )

        def quantize_operands(in_, names):
            label = "%s%d" % names[0]
            words = keep.tile([P, 256 * len(names)], U32, name="codes_" + label, align_bytes=64)
            plane = keep.tile([P, 256 * len(names)], U8, name="scales_" + label, align_bytes=64)
            nc.vector.quantize_mx(out=words[:].bitcast(FP8X4), scales=plane[:], in_=in_)
            for pos, (name, s) in enumerate(names):
                for h in range(2):
                    lo = 256 * pos + 128 * h
                    codes[name, s, h] = words[:, lo : lo + 128].bitcast(FP8X4)
                    scales[name, s, h] = plane[:, lo : lo + 128]

        def quantize_in(s, ops=("g", "x")):
            lo = N * (2 * (s % 2) + (ops[0] == "x"))
            quantize_operands(turned[s // 2][:, lo : lo + N * len(ops)], [(op, s) for op in ops])

        def negate(sp):
            nc.vector.tensor_scalar(
                out=slot_tile(("minus", sp), [P, 2 * N], BF16)[:].rearrange("p (j k) -> p j k", j=2),
                in0=turned[sp][:].rearrange("p (j o k) -> p j o k", j=2, o=2)[:, :, 1, :],
                scalar1=-1.0,
                scalar2=None,
                op0=ALU.mult,
            )

        def quantize_minus(sp):
            quantize_operands(shared["minus", sp][:], (("minus_x", 2 * sp), ("minus_x", 2 * sp + 1)))

        a_bank, l_rows, eta_a, rl_codes, rl_scales = {}, {}, {}, {}, {}
        for h in range(2):
            for sp in range(4):
                if True:
                    eta_a[h, sp] = keep.tile([P, 4, 256], F32, name="eta_a_%d%d" % (h, sp))
            for hp in range(2):
                rl_codes[h, hp] = keep.tile([P, 1024], U32, name="rl_codes_%d%d" % (h, hp), align_bytes=64)
                rl_scales[h, hp] = keep.tile([P, 1024], U8, name="rl_scales_%d%d" % (h, hp), align_bytes=64)
        plain = keep.tile([P, 4, 512], F32, name="plain")

        def matmul_a(h, s, index):
            a_bank[h, s] = new_bank(index)
            passes = [(left, right, k) for left, right in (("g", "x"), ("minus_x", "g")) for k in range(2)]
            for t in range(4):
                for step, (left, right, k) in enumerate(passes):
                    nc.tensor.matmul_mx(
                        out=a_bank[h, s][:, 128 * t : 128 * t + 128],
                        lhsT=codes[left, 4 * h + t, k],
                        lhsT_scale=scales[left, 4 * h + t, k],
                        rhs=codes[right, s, k],
                        rhs_scale=scales[right, s, k],
                        start=(step == 0),
                        stop=(step == 3),
                    )

        def copy_plain(s):
            nc.scalar.copy(out=plain[:, s - 4, :], in_=a_bank[0, s][:])

        def mirror_a(s, index):
            a_bank[1, s] = new_bank(index)
            for t in range(4):
                nc.tensor.transpose(a_bank[1, s][:, 128 * t : 128 * t + 128], plain[:, t, 128 * s : 128 * s + 128], ident[:])

        def rl_part(h, hp, first, last):
            if (h, hp) in WHOLE:
                return slot_tile(("rl", h, hp), [P, 4096], BF16)[:, 1024 * first : 1024 * last]
            if first < 2:
                return slot_tile(("r", h, hp), [P, 2048], BF16)[:, 1024 * first : 1024 * last]
            return slot_tile(("l", h, hp, first), [P, 1024], BF16)[:]

        def vector_r(h, s):
            lo = 512 * (s % 4)
            nc.vector.tensor_tensor(
                out=rl_part(h, s // 4, 0, 2)[:, lo : lo + 512].rearrange("p (n t) -> p n t", t=4),
                in0=a_bank[h, s][:].rearrange("p (t n) -> p n t", t=4),
                in1=factor(h, s)[:, 0:1, :].to_broadcast([P, 128, 4]),
                op=ALU.mult,
            )

        def vector_rl(h, s):
            col = 128 * (s % 4)
            nc.vector.tensor_tensor(
                out=rl_part(h, s // 4, 0, 4).rearrange("p (o n t) -> p o n t", o=2, t=4)[:, :, col : col + 128, :],
                in0=a_bank[h, s][:].rearrange("p (t n) -> p n t", t=4).unsqueeze(1).to_broadcast([P, 2, 128, 4]),
                in1=factor(h, s)[:, 0:2, :].unsqueeze(2).to_broadcast([P, 2, 128, 4]),
                op=ALU.mult,
            )

        def vector_l_halves(h, s):
            quarter = 2 + LAST_PAIR % 2
            nc.vector.tensor_tensor(
                out=rl_part(h, s // 4, quarter, quarter + 1).rearrange("p (u a m t) -> p a u m t", u=2, a=2, t=4)[:, s % 2],
                in0=a_bank[h, s][:].rearrange("p (t u m) -> p u m t", t=4, u=2),
                in1=factor(h, s)[:, 1:2, :].unsqueeze(1).to_broadcast([P, 2, HALF, 4]),
                op=ALU.mult,
            )

        def gpsimd_l_plain(first, count):
            lo = 512 * (first - 4)
            nc.gpsimd.tensor_tensor(
                out=rl_part(0, 1, 2, 4)[:, lo : lo + 512 * count].rearrange("p (a n t) -> p a n t", a=count, t=4),
                in0=plain[:, first - 4 : first - 4 + count, :].rearrange("p a (t n) -> p a n t", t=4),
                in1=factor(0, 4)[:, 1:2, :].unsqueeze(1).to_broadcast([P, count, 128, 4]),
                op=ALU.mult,
            )

        def scale_rows(out, in_, h, s, row):
            for t in range(4):
                nc.scalar.activation(out=out(t), in_=in_(t), func=COPY, scale=factor(h, s)[:, row, t : t + 1])

        def l_columns(h, first, count):
            if (h, first // 2) not in l_rows:
                l_rows[h, first // 2] = work.tile([P, 4, 256], BF16, name="l_rows", align_bytes=64, bufs=L_ROWS_BUFS)
            order = "p t (u a m) -> p t a u m" if first // 2 == LAST_PAIR else "p t (a u m) -> p t a u m"
            return l_rows[h, first // 2][:].rearrange(order, u=2, a=2)[:, :, first % 2 : first % 2 + count]

        def scalar_l(h, s):
            bank = a_bank[h, s][:].rearrange("p (t a u m) -> p t a u m", t=4, a=1, u=2)
            scale_rows(lambda t: l_columns(h, s, 1)[:, t], lambda t: bank[:, t], h, s, 1)

        def scalar_l_plain(first, count):
            banks = plain[:, first - 4 : first - 4 + count, :].rearrange("p a (t u m) -> p t a u m", t=4, u=2)
            scale_rows(lambda t: l_columns(0, first, count)[:, t], lambda t: banks[:, t], 0, first, 1)

        def scalar_eta(h, s):
            col = 128 * (s % 2)
            scale_rows(
                lambda t: eta_a[h, s // 2][:, t, col : col + 128], lambda t: a_bank[h, s][:, 128 * t : 128 * t + 128], h, s, 2
            )

        def gpsimd_move(out, in_, scale=1.0):
            nc.gpsimd.tensor_scalar(out=out, in0=in_, scalar1=scale, scalar2=0.0, op0=ALU.mult, op1=ALU.add)

        def gpsimd_l(h, sp):
            out = rl_part(h, sp // 2, 2 + sp % 2, 3 + sp % 2).rearrange("p (n t) -> p n t", t=4)
            gpsimd_move(out, l_rows[h, sp][:].rearrange("p t n -> p n t"))

        def scalar_eta_plain(s):
            col = 128 * (s % 2)
            scale_rows(
                lambda t: eta_a[0, s // 2][:, t, col : col + 128], lambda t: plain[:, s - 4, 128 * t : 128 * t + 128], 0, s, 2
            )

        def gpsimd_eta_plain(sp):
            for t in range(4):
                gpsimd_move(
                    eta_a[0, sp][:, t, :].rearrange("p (a n) -> p a n", a=2),
                    plain[:, 2 * sp - 4 : 2 * sp - 2, 128 * t : 128 * t + 128],
                    factor(0, 4)[:, 2, t : t + 1],
                )

        def eta_source(t, engine):
            out = slot_tile(("eta", t), [P, 512], F32)[:].rearrange("p (s n) -> p s n", s=4)
            in_, scale = plain[:, :, 128 * t : 128 * t + 128], factor(0, 4)[:, 2, t : t + 1]
            if engine is nc.scalar:
                nc.scalar.activation(out=out, in_=in_, func=COPY, scale=scale)
            else:
                gpsimd_move(out, in_, scale)

        def quantize_rl(h, hp, first, last):
            cols = slice(256 * first, 256 * last)
            nc.vector.quantize_mx(
                out=rl_codes[h, hp][:, cols].bitcast(FP8X4), scales=rl_scales[h, hp][:, cols], in_=rl_part(h, hp, first, last)
            )

        q_bank, out_t, out_bank, out_words = {}, {}, {}, {}
        out_scales = keep.tile([P, N], U8, name="out_scales", align_bytes=64)
        out_rows = out_0.rearrange("(hp u m a) j -> hp u m a j", hp=2, u=2, a=4)

        def q_pass(out, h, sp, t, k, rows, start, stop):
            cols = slice(128 * t, 128 * t + 128)
            nc.tensor.matmul_mx(
                out=out,
                lhsT=rl_codes[k, h][:, cols].bitcast(FP8X4),
                lhsT_scale=rl_scales[k, h][:, cols],
                rhs=rl_codes[k, sp // 2][:, rows].bitcast(FP8X4),
                rhs_scale=rl_scales[k, sp // 2][:, rows],
                start=start,
                stop=stop,
            )

        def matmul_q(h, sp, banks, k_halves=(0, 1), first_k=0):
            rows = slice(512 + 256 * (sp % 2), 768 + 256 * (sp % 2))
            for k in k_halves:
                for t in range(4):
                    if k == first_k and t % 2 == 0:
                        q_bank[h, sp, t // 2] = new_bank(banks[t // 2])
                    out = q_bank[h, sp, t // 2][:, 256 * (t % 2) : 256 * (t % 2) + 256]
                    q_pass(out, h, sp, t, k, rows, k == first_k and t % 2 == 0, k != first_k and t % 2 == 1)

        def matmul_q_last(u, index):
            q_bank["last", u] = new_bank(index)
            rows = slice(768 + 128 * u, 896 + 128 * u)
            for t in range(4):
                for k in range(2):
                    q_pass(q_bank["last", u][:, 128 * t : 128 * t + 128], LAST_HALF, LAST_PAIR, t, k, rows, k == 0, k == 1)

        def unit_t(h, sp):
            if (h, sp // 2) not in out_t:
                out_t[h, sp // 2] = keep.tile([P, 2048], F32, name="out_t", tag="wide_%d" % len(out_t), align_bytes=64)
            return out_t[h, sp // 2][:, 1024 * (sp % 2) : 1024 * (sp % 2) + 1024].rearrange("p (t n) -> p t n", t=4)

        def combine_lane(h, sp, t, q, ms):
            first = eta_a[h, sp][:, t, :]
            nc.vector.scalar_tensor_tensor(
                out=unit_t(h, sp)[:, t, :].rearrange("p (m a) -> p m a", a=2)[:, ms, :],
                in0=q.rearrange("p (a m) -> p m a", a=2),
                scalar=q_factor[:, 4 * h + t : 4 * h + t + 1],
                in1=first.rearrange("p (a m) -> p m a", a=2)[:, ms, :],
                op0=ALU.mult,
                op1=ALU.add,
            )

        def combine(h, sp, lanes=(2, 3, 0, 1)):
            for t in lanes:
                q = q_bank[h, sp, t // 2][:, 256 * (t % 2) : 256 * (t % 2) + 256]
                if sp != LAST_PAIR:
                    combine_lane(h, sp, t, q, slice(0, P))
                else:
                    for u in range(2):
                        combine_lane(h, sp, t, q[:, 128 * u : 128 * u + 128], slice(HALF * u, HALF * u + HALF))

        def combine_last(u):
            for t in range(4):
                combine_lane(LAST_HALF, LAST_PAIR, t, q_bank["last", u][:, 128 * t : 128 * t + 128], slice(HALF * u, HALF * u + HALF))

        def planes_tile(h, hp, u):
            if (h, hp) == FIRST_PLANE:
                return slot_tile(("planes", h, hp, u), [P, 1024], BF16)[:]
            return slot_tile(("planes", h, hp), [P, 2048], BF16)[:, 1024 * u : 1024 * u + 1024]

        def planes_part(h, hp, first, last):
            if (h, hp) == FIRST_PLANE:
                u = first // HALF
                return planes_tile(h, hp, u)[:, 16 * (first - HALF * u) : 16 * (last - HALF * u)]
            return slot_tile(("planes", h, hp), [P, 2048], BF16)[:, 16 * first : 16 * last]

        def interleave_out(h, sp, engine, first=0, last=P):
            lo = 2 * (sp % 2)
            out = planes_part(h, sp // 2, first, last).rearrange("p (m a t) -> p m t a", a=4, t=4)[:, :, :, lo : lo + 2]
            in_ = unit_t(h, sp).rearrange("p t (m a) -> p m t a", a=2)[:, first:last]
            if engine is nc.vector:
                nc.vector.tensor_copy(out=out, in_=in_)
            elif engine is nc.scalar:
                nc.scalar.copy(out=out, in_=in_)
            else:
                gpsimd_move(out.rearrange("p m t a -> p m a t"), in_.rearrange("p m t a -> p m a t"))

        def quantize_out(h, hp, first=0, last=512):
            if (h, hp) not in out_words:
                out_words[h, hp] = keep.tile([P, 512], U32, name="out_codes_%d%d" % (h, hp), align_bytes=64)
            nc.vector.quantize_mx(
                out=out_words[h, hp][:, first:last].bitcast(FP8X4),
                scales=out_scales[4 * h : P, 512 * hp + first : 512 * hp + last],
                in_=planes_part(h, hp, first // 4, last // 4),
            )

        def store_words(h, hp):
            cols = slice(512 * hp, 512 * hp + 512)
            nc.sync.dma_start(
                out=out_1[h, :, cols, :].rearrange("p m b -> p (m b)").bitcast(I32), in_=out_words[h, hp][:].bitcast(I32)
            )

        def store_scales():
            for quad in range(4):
                (nc.scalar if quad % 2 else nc.sync).dma_start(
                    out=out_2[:, 4 * quad : 4 * quad + 4, :].bitcast(I32),
                    in_=out_scales[32 * quad : 32 * quad + 8, :].bitcast(I32),
                )

        def transpose_out(h, sp, banks, halves=(0, 1)):
            for u, index in zip(halves, banks):
                out_bank[h, sp, u] = new_bank(index)
                for t in range(4):
                    nc.tensor.transpose(
                        out_bank[h, sp, u][:, 128 * t : 128 * t + 128], unit_t(h, sp)[:, t, 128 * u : 128 * u + 128], ident[:]
                    )

        def store_rows(h, sp, halves=(1, 0), engine=nc.scalar):
            lo = 2 * (sp % 2)
            for u in halves:
                rows = keep.tile([P, 512], F32, name="rows_%d%d%d" % (h, sp, u), align_bytes=64)
                (nc.scalar.copy if engine is nc.scalar else nc.vector.tensor_copy)(
                    out=rows[:].rearrange("m (p t) -> m p t", t=4),
                    in_=out_bank[h, sp, u][:].rearrange("m (t p) -> m p t", t=4),
                )
                nc.sync.dma_start(out=out_rows[sp // 2, u, :, lo : lo + 2, 512 * h : 512 * h + 512], in_=rows[:])

        for s in range(8):
            transpose_in("g", s)
            if s == 0:
                quantize_in(s, ("g",))
            transpose_in("x", s)
            quantize_in(s, ("x",) if s == 0 else ("g", "x"))
            if s % 2 == 1:
                negate(s // 2)
            elif s > 0:
                quantize_minus(s // 2 - 1)
        make_row_factors()
        make_q_factor()

        for s in range(4, 8):
            matmul_a(0, s, s - 4)
        quantize_minus(3)
        matmul_a(1, 4, 4)
        copy_plain(4)
        vector_rl(0, 4)
        copy_plain(5)
        vector_rl(0, 5)
        scalar_eta_plain(4)
        copy_plain(6)
        vector_r(0, 6)
        scalar_eta_plain(5)
        quantize_rl(0, 1, 0, 1)
        quantize_rl(0, 1, 2, 3)
        copy_plain(7)
        vector_r(0, 7)
        gpsimd_l_plain(6, 2)
        for s, index in zip(range(4), (5, 6, 7, 0)):
            mirror_a(s, index)
        matmul_a(1, 5, 1)
        matmul_a(1, 6, 2)
        matmul_a(1, 7, 3)
        scalar_eta_plain(6)
        scalar_eta_plain(7)
        vector_r(1, 4)
        scalar_l(1, 4)
        scalar_eta(1, 4)
        vector_rl(1, 0)
        scalar_eta(1, 0)
        vector_rl(1, 1)
        vector_r(1, 5)
        scalar_eta(1, 1)
        scalar_l(1, 5)
        quantize_rl(0, 1, 1, 2)
        quantize_rl(0, 1, 3, 4)
        gpsimd_l(1, 2)
        scalar_eta(1, 5)
        vector_r(1, 6)
        vector_r(1, 2)
        vector_r(1, 7)
        scalar_l(1, 6)
        scalar_l(1, 7)
        matmul_a(0, 0, 4)
        matmul_a(0, 1, 5)
        vector_l_halves(1, 2)
        quantize_rl(1, 1, 0, 2)
        quantize_rl(1, 1, 2, 3)
        gpsimd_l(1, 3)
        scalar_eta(1, 6)
        scalar_eta(1, 7)
        matmul_q(1, 2, (6, 1))
        matmul_a(0, 2, 2)
        vector_r(1, 3)
        vector_l_halves(1, 3)
        scalar_eta(1, 2)
        scalar_eta(1, 3)
        combine(1, 2, (2, 3))
        quantize_rl(1, 1, 3, 4)
        matmul_q(1, 3, (3, 7))
        combine(1, 2, (0, 1))
        scalar_l(0, 0)
        scalar_l(0, 1)
        quantize_rl(1, 0, 0, 4)
        gpsimd_l(0, 0)
        scalar_eta(0, 0)
        scalar_eta(0, 1)
        transpose_out(1, 2, (0, 6))
        matmul_a(0, 3, 1)
        combine(1, 3)
        interleave_out(1, 2, nc.gpsimd, 0, HALF)
        scalar_l(0, 2)
        scalar_l(0, 3)
        store_rows(1, 2)
        vector_r(0, 0)
        vector_r(0, 1)
        matmul_q(1, 0, (3, 7), (1,), 1)
        transpose_out(1, 3, (4, 5))
        quantize_rl(0, 0, 2, 3)
        gpsimd_l(0, 1)
        matmul_q(1, 0, (3, 7), (0,), 1)
        matmul_q(0, 2, (0, 6), (1,), 1)
        vector_r(0, 2)
        vector_r(0, 3)
        store_rows(1, 3)
        combine(1, 0, (2, 3))
        quantize_rl(0, 0, 0, 2)
        quantize_rl(0, 0, 3, 4)
        interleave_out(1, 3, nc.gpsimd, HALF, P)
        matmul_q(0, 3, (4, 5), (1,), 1)
        matmul_q(0, 2, (0, 6), (0,), 1)
        matmul_q(0, 3, (4, 5), (0,), 1)
        scalar_eta(0, 2)
        scalar_eta(0, 3)
        interleave_out(1, 3, nc.scalar, 0, HALF)
        interleave_out(1, 2, nc.scalar, HALF, P)
        combine(1, 0, (0, 1))
        interleave_out(1, 0, nc.gpsimd, 0, 112)
        transpose_out(1, 0, (2, 1))
        combine(0, 2)
        matmul_q(1, 1, (3, 7))
        store_rows(1, 0)
        interleave_out(0, 2, nc.scalar, 0, 80)
        transpose_out(0, 2, (0, 6))
        combine(0, 3, (2, 3, 0))
        quantize_out(1, 1, 0, 256)
        combine(0, 3, (1,))
        quantize_out(1, 1, 256, 512)
        store_words(1, 1)
        transpose_out(0, 3, (4, 5))
        interleave_out(0, 3, nc.gpsimd)
        matmul_q(0, 0, (2, 1))
        store_rows(0, 2)
        combine(1, 1)
        interleave_out(1, 1, nc.gpsimd)
        store_rows(0, 3, (1,))
        store_rows(0, 3, (0,), nc.vector)
        transpose_out(1, 1, (3, 7))
        matmul_q_last(0, 0)
        matmul_q_last(1, 6)
        interleave_out(1, 0, nc.scalar, 112, P)
        interleave_out(0, 2, nc.scalar, 80, P)
        combine(0, 0)
        quantize_out(0, 1)
        quantize_out(1, 0)
        store_rows(1, 1)
        store_words(0, 1)
        store_words(1, 0)
        interleave_out(0, 0, nc.scalar)
        transpose_out(0, 0, (2, 1))
        combine_last(0)
        transpose_out(0, 1, (4,), (0,))
        combine_last(1)
        transpose_out(0, 1, (5,), (1,))
        store_rows(0, 0)
        interleave_out(0, 1, nc.vector, 0, HALF)
        interleave_out(0, 1, nc.vector, HALF, P)
        store_rows(0, 1, (0,))
        quantize_out(0, 0, 0, 256)
        quantize_out(0, 0, 256, 512)
        store_rows(0, 1, (1,))
        store_words(0, 0)
        store_scales()
